import numpy as np, ml_dtypes
CORES = [23,119,17,113]
N = 4
import mx_ref
BF = ml_dtypes.bfloat16
def gcols(t, e):
    v = np.concatenate([t.reshape(8, 16, -1, 4), np.zeros((8, 16, 1, 4), BF)], axis=2)
    return np.ascontiguousarray(np.stack([v[g][:, e[g]] for g in range(8)])).reshape(128, -1)
def tile(rs):
    return np.stack(rs, axis=2).reshape(128, -1).astype(BF)
def cut(t, i, w=512):
    return t[:, w * i:w * i + w]
def pick(q, e):
    c = np.concatenate([q[0].reshape(128, -1, 4), np.zeros((128, 1, 4), np.uint8)], axis=1); s = np.concatenate([q[1], np.ones((16, 1), np.uint8)], axis=1)
    return (np.ascontiguousarray(c[:, e].reshape(128, -1)), np.ascontiguousarray(s[:, e]))
def join(*qs):
    return (np.concatenate([q[0] for q in qs], axis=1), np.concatenate([q[1] for q in qs], axis=1))
def put(q, e, v):
    c, s = q[0].reshape(128, -1, 4).copy(), q[1].copy(); c[:, e] = v[0].reshape(128, -1, 4); s[:, e] = v[1]
    return (c.reshape(128, -1), s)
def pk(c, s):
    return (np.ascontiguousarray(c), mx_ref.live(s))
def emit(q):
    return q[0], q[1]
def packed(v, rng):
    q = [mx_ref.quantize(np.ascontiguousarray(v[r])) for r in range(N)]
    return np.stack([a for a, b in q]), np.stack([mx_ref.plane(b, rng) for a, b in q])
def values_of_codes():
    e, c = np.zeros((128, 128, 4), np.float32), np.zeros((128, 2, 4), np.uint8)
    e[np.arange(128), np.arange(128), 0] = 1
    c[:127, :, 0] = np.arange(256).reshape(2, 128).T[:127]
    return mx_ref.matmul(mx_ref.quantize(e.reshape(128, 512).astype(BF)), (c.reshape(128, 8), np.full((16, 2), 127, np.uint8))).T.reshape(-1).astype(np.float64)
CODE_VALUE, SCALE_VALUE = values_of_codes(), 2.0 ** (np.arange(256) - 127.0)
def decode(q):
    return (CODE_VALUE[q[0]].reshape(16, 8, -1, 4) * SCALE_VALUE[q[1]][:, None, :, None] + 0.0).reshape(128, -1).astype(np.float32)
def f(rng, *shape):
    return mx_ref.flush((rng.standard_normal(shape, dtype=np.float32) * np.exp2(rng.integers(-2, 3, shape[:-1] + (1,)))).astype(BF))
def wide(rng, *shape, cols=0):
    v = rng.standard_normal(shape, dtype=np.float32) * np.exp2(rng.integers(-12, 13, shape)).astype(np.float32)
    if cols: v *= np.repeat(np.exp2(rng.integers(-cols, cols + 1, shape[:-2] + (1, shape[-1] // 4))) * (rng.random(shape[:-2] + (1, shape[-1] // 4)) > 0.0625), 4, axis=-1).astype(np.float32)
    return mx_ref.flush(v.astype(BF))
C, L, R = 320, 96, 3
def order(p, s):
    return np.lexsort((-(s + np.float32(0.0)), -p))
def pairs(p):
    a, b = np.zeros((8, C // 2), np.int64), np.zeros((8, C // 2), np.int64)
    for g in range(8):
        end = [int(np.sum(p[g] >= k)) // 2 * 2 for k in range(3 + R, -1, -1)]
        for i, k in zip(end, end[1:]):
            m = (k - i) // 2
            a[g, i // 2:k // 2] = np.arange(i, i + m)
            b[g, i // 2:k // 2] = np.arange(i + m, k)
    return a, b
def gput(t, e, h):
    a, b = t.reshape(8, 16, -1, 4).copy(), h.reshape(8, 16, -1, 4)
    for g in range(8): a[g][:, e[g]] = b[g]
    return a.reshape(128, -1)
def big(v):
    v = v.astype(np.float32)
    v[np.abs(v) < np.float32(2.0 ** -16)] = 0
    return v.astype(BF)
def numbers_of(rng):
    return {"x": big(f(rng, N, 128, 4 * C)), "u": np.array(f(rng, N, 128, 512)), "v": np.array(f(rng, N, 128, 512))}
def layers(rng):
    return big(f(rng, N, 128, 2048)).reshape(N, 8, 16, 4, 8, 16, 4)
def weights(rng, w):
    c, p = packed(np.ascontiguousarray(w).reshape(N, 128, 2048), rng)
    return {"wc": c, "ws": p}
def signs(rng):
    return np.stack([rng.permutation(8) % 2 * 2.0 - 1.0 for r in range(N)])
def setup_inputs(rng):
    return {**numbers_of(rng), **weights(rng, layers(rng))}
def setup_inputs_ties(rng):
    d = numbers_of(rng)
    e = rng.permutation(N)
    x = d["x"].reshape(N, 8, 16, C, 4)
    for r in range(N):
        k = np.zeros(C, int) if r == e[0] else rng.permutation(C) % 3
        a = x[r][:, :8, :3].copy()
        a[:, :, 2] = 0
        x[r][:, :8] = a[:, :, k]
    x[e[1]] = 0
    u = d["u"].reshape(N, 8, 16, 8, 16, 4)
    u[:, :, 8:, :, :4] = 0
    w = layers(rng)
    w[:, :, 8:, :, :, :8] = 0
    return {"x": x.reshape(N, 128, 4 * C), "u": u.reshape(N, 128, 512), "v": d["v"], **weights(rng, w)}
def setup_inputs_near(rng):
    d = numbers_of(rng)
    x = np.zeros((N, 8, 16, C, 4), np.float32)
    u = d["u"].reshape(N, 128, 128, 4)
    for m in range(4): u[:, :, m::16] = 0
    o, c = rng.permutation(N) % 4, signs(rng)
    upper = np.arange(C) // (C // 2)
    for r in range(N):
        i = (np.arange(C) + rng.integers(0, C, (8, 1))) % C
        if o[r] == 3: i = i % (C // 2) * 2 + upper
        s = (i + 1) // 2
        size = 1.0 if o[r] < 2 else 2.0 ** -4
        g = ((s[:, :, None] >> np.arange(8)) & 1) * np.exp2(np.arange(8) - 23.0) * size
        if o[r] < 2: x[r, :, 0, :, 0] = c[r][:, None]
        if o[r] == 3:
            x[r, :, 0, :, 0] = (8 + upper) * 2.0 ** -33
            x[r, :, 1, :, 0] = (9 - upper) * 2.0 ** -33
        x[r, :, 8] = g[:, :, :4]
        x[r, :, 9] = g[:, :, 4:]
        x[r, :, 10:] = rng.integers(4, 8, (8, 6, C, 4)) * 2.0 ** -20 * size
        x[r, :, 11, :, 0] = rng.integers(-1, 2, (8, C)) * 2.0 ** -18 * size
        x[r, :, 12, :, 0] = 0
        same = (rng.permutation(8) % 2 == 0)[:, None, None]
        x[r, :, 13:, :, 0] = np.where(same, rng.integers(-1, 2, (8, 3, 1)), rng.integers(-1, 2, (8, 3, C))) * 2.0 ** -18 * size
        k = 1.0 if o[r] == 0 else 2.0 ** -30
        for h in range(0, 128, 16):
            u[r, h, h, 0] = 1.125 * k if o[r] == 3 else k
            u[r, h + 1, h, 0] = k
            u[r, h + 8:h + 10, h] = k
            u[r, h + 12, h, 0] = k
            for m in range(3): u[r, h + 13 + m, h + 1 + m, 0] = k
    w = layers(rng)
    w[:, :, :10] = 0
    w[:, :, :, :, :, :2] = 0
    w[:, :, :, :, :, 8:] = 0
    for g in range(8): w[:, g, 11, 0, g, 12, 0] = 0.25
    return {"x": x.reshape(N, 128, 4 * C).astype(BF), "u": u.reshape(N, 128, 512), "v": d["v"], **weights(rng, w)}
def setup_inputs_brackets(rng):
    d = numbers_of(rng)
    x = d["x"].reshape(N, 8, 16, C, 4)
    x[:, :, :8] = 0
    x[:, :, 12] = 0
    q = rng.integers(-1, 2, (N, 8, C))
    for g, m in enumerate(rng.permutation(8)):
        if m < 3: q[:, g] = m - 1
    x[:, :, 13, :, 0] = q.astype(np.float32).astype(BF)
    small = rng.permutation(N) < N // 2
    for r in range(N):
        i, j, k = 2 * rng.integers(0, C // 8, 3) + 1
        n = rng.permutation(np.array([[0, 0, 0, C], [C, 0, 0, 0], [1, 0, 0, C - 1], [C - 1, 0, 0, 1], [1, 1, 1, C - 3], [C - 2 * L, 0, 0, 2 * L], [0, 3, 0, C - 3], [i, j, k, C - i - j - k]]))
        unit = 2.0 ** -30 if small[r] else 0.125
        for g in range(8):
            p = rng.permutation(np.repeat([3, 2, 1, 0], n[g]))
            on = np.argsort(rng.random((3, C)), axis=0) < p
            a = np.where(on, 1.0, -1.0 * rng.integers(0, 2, (3, C)))
            x[r, g, :3, :, 0] = ((8 + np.maximum(a, 0)) * unit).astype(np.float32).astype(BF)
            x[r, g, 3:6, :, 0] = ((8 + np.maximum(-a, 0)) * unit).astype(np.float32).astype(BF)
    u = d["u"].reshape(N, 8, 16, 8, 16, 4)
    b = u.copy()
    s = np.where(small, 2.0 ** -30, 1.0).astype(np.float32)
    u[:, :, :, :, :4] = 0
    w = layers(rng)
    w[:, :, :, :, :, 8:] = 0
    for g in range(8):
        u[:, g, 8:11, g, 0] = b[:, g, 8:11, g, 0]
        u[:, g, 12, g, 0, 0] = 1
        for m in range(3):
            u[:, g, m, g, 1 + m, 0] = s.astype(BF)
            u[:, g, 3 + m, g, 1 + m, 0] = (-s).astype(BF)
        w[:, g, 13, 0, g, 12, 0] = 1
    return {"x": x.reshape(N, 128, 4 * C), "u": u.reshape(N, 128, 512), "v": d["v"], **weights(rng, w)}
def setup_inputs_huge(rng):
    d = numbers_of(rng)
    c = np.stack([rng.permutation(C) % 2 * 2.0 - 1.0 for r in range(N)])
    c[rng.permutation(N) < N // 2] = -1
    x = 2.0 ** 30 * (0.55 + 0.2 * rng.random((N, 128, C, 4))) * c[:, None, :, None]
    u = d["u"].reshape(N, 128, 8, 16, 4)
    k = rng.choice([-1.0, 1.0], (N, 8, 4))
    k[:, :, 0] = signs(rng)
    a = 2.0 ** 30 * (1 - 0.1 * rng.random((N, 128, 8, 4, 4))) * k[:, None, :, :, None]
    u[:, :, :, :4] = a.astype(np.float32).astype(BF)
    w = np.zeros((N, 128, 4, 128, 4), np.float32)
    i = np.arange(128)
    for b in range(4): w[:, i, b, i, b] = -1
    return {"x": x.astype(np.float32).reshape(N, 128, 4 * C).astype(BF), "u": u.reshape(N, 128, 512), "v": d["v"], **weights(rng, w.astype(BF))}
def setup_inputs_spread(rng):
    d = setup_inputs(rng)
    d["x"] = big(wide(rng, N, 128, 4 * C, cols=6))
    return d
def check_inputs(d):
    b = []
    for k in ("x", "u", "v"):
        a = np.abs(d[k].astype(np.float32))
        if not (np.isfinite(a).all() and ((a == 0) | (a >= 2.0 ** -30) & (a <= 2.0 ** 30)).all()): b.append("a value of " + k)
    none, least, most = [emit(mx_ref.quantize(np.full((128, 16), k, np.float32).astype(BF)))[1][0, 0] for k in (0.0, 2.0 ** -30, 2.0 ** 30)]
    for r in range(N):
        if ((d["wc"][r] == 0x7F) | (d["wc"][r] == 0xFF)).any(): b.append("wc: a code that is no number")
        s = mx_ref.live(d["ws"][r])
        if ((s != none) & ((s < least) | (s > most))).any(): b.append("ws: a scale out of range")
    return b
def reference(x, u, v, wc, ws):
    qu = [mx_ref.quantize(u[r]) for r in range(N)]
    lay = [pk(wc[r], ws[r]) for r in range(N)]
    now = [x[r] for r in range(N)]
    points = []
    for t in range(R):
        sent, gone, moved = [], [], []
        for r in range(N):
            s = mx_ref.matmul(qu[r], mx_ref.quantize(now[r]))
            if t == 0: points.append(np.sum(s.reshape(8, 16, C)[:, 1:4] > 0, axis=1))
            o = order(points[r], s[::16])
            i, k = pairs(points[r])
            a, b = np.take_along_axis(o, i, 1), np.take_along_axis(o, k, 1)
            first, second = gcols(now[r], a).astype(np.float32), gcols(now[r], b).astype(np.float32)
            q = mx_ref.quantize(((first + second) * np.float32(0.5)).astype(BF))
            h = tile([mx_ref.matmul(pick(lay[r], np.arange(128 * m, 128 * m + 128)), q) * np.float32(0.03125) for m in range(4)])
            won = mx_ref.matmul(qu[r], mx_ref.quantize(h))[::16] > 0
            h = h.astype(np.float32)
            now[r] = gput(gput(now[r], a, (first + h).astype(BF)), b, (second - h).astype(BF))
            gain = np.zeros((8, C), np.int64)
            np.put_along_axis(gain, a, won.astype(np.int64), 1)
            np.put_along_axis(gain, b, (~won).astype(np.int64), 1)
            points[r] = points[r] + gain
            back = np.take_along_axis(points[r], o, 1)[:, ::-1]
            e = np.take_along_axis(o, C - 1 - np.argsort(back, axis=1, kind="stable")[:, :L], 1)
            gone.append(e)
            moved.append(np.take_along_axis(points[r], e, 1))
            sent.append(mx_ref.quantize(gcols(now[r], e)))
        came = decode(join(*sent)).astype(BF)
        for r in range(N):
            p = (r - 1) % N
            now[r] = gput(now[r], gone[r], cut(came, p, 4 * L))
            np.put_along_axis(points[r], gone[r], moved[p], 1)
    y, pts = np.zeros((N, 128, C), np.float32), np.zeros((N, 8, C), np.float32)
    oc, osc = np.zeros((N, 128, 4 * C), np.uint8), np.zeros((N, 16, C), np.uint8)
    for r in range(N):
        q = mx_ref.quantize(now[r])
        y[r] = mx_ref.matmul(mx_ref.quantize(v[r]), q)
        pts[r] = points[r]
        oc[r], osc[r] = emit(q)
    return {"y": y, "pts": pts, "oc": oc, "osc": osc}

@@ -1,0 +1,578 @@
+import numpy as np
+from concourse.mybir import dt, AluOpType, ActivationFunctionType
+
+C, L, R = 320, 96, 3
+F32, BF, I32, U16, Q4, U8 = "float32", "bfloat16", "int32", "uint16", "float8_e4m3fn_x4", "uint8"
+NV1, NV2 = (4, 6, 6), 8
+PAT1 = "rsrsrssrTsrTrTsTT"
+ZCUT = (0, 8, 24, 40)
+XH = 800
+
+
+def _sb(n, d):
+    return ("sbuf", [128, n], d)
+
+
+SCRATCH = {
+    "x0": _sb(4 * C, BF), "X": _sb(4 * C, BF), "Xh": _sb(4 * C, BF), "Y": _sb(4 * (C + L), BF),
+    "ut": _sb(512, BF), "vt": _sb(512, BF),
+    "qu": _sb(128, Q4), "su": _sb(128, U8), "qur": _sb(384, Q4), "sur": _sb(384, U8), "qv": _sb(128, Q4), "sv": _sb(128, U8),
+    "qw": _sb(512, Q4), "sw": _sb(512, U8), "qx": _sb(C, Q4), "sx": _sb(C, U8),
+    "qz": _sb(160, Q4), "sz": _sb(160, U8), "qh": _sb(160, Q4), "sh": _sb(160, U8),
+    "ones": _sb(512, BF), "zero": _sb(512, BF), "et": _sb(2048, BF), "qe": _sb(512, Q4), "se": _sb(512, U8),
+    "a1i": _sb(512, BF), "a0i": _sb(512, BF), "at": _sb(1024, BF), "qa": _sb(256, Q4), "sa": _sb(256, U8),
+    "q0": _sb(128, Q4), "s0": _sb(128, U8),
+    "bits": _sb(5 * 4 * C, BF), "qb": _sb(5 * C, Q4), "sb": _sb(5 * C, U8), "pb": _sb(4 * C, BF), "qp": _sb(C, Q4), "sp": _sb(C, U8),
+    "tr": _sb(C, F32), "ah": _sb(640, BF), "Z": _sb(640, BF), "H": _sb(640, BF), "cmp": _sb(512, BF),
+    "ic": _sb(C, F32), "icb": _sb(C + L, BF), "ic2": _sb(2 * C, BF), "i16": _sb(C, BF), "i4": _sb(C, BF), "fr0": _sb(C, F32),
+    "m16": _sb(C, BF), "m4": _sb(C, BF), "r16": _sb(C, BF), "r4": _sb(C, BF), "r8": _sb(160, BF),
+    "pi": _sb(8, I32), "pf": _sb(20, F32), "ui": _sb(24, I32), "uo": _sb(24, U16),
+    "kst": _sb(C, F32), "K": _sb(C, F32), "km": _sb(C, F32), "kw": _sb(C, F32),
+    "kb": _sb(C, BF), "kc": _sb(C, BF), "kd": _sb(C, BF), "ke": _sb(C, BF),
+    "cb": _sb(3 * C, BF), "co": _sb(20 * 160, BF), "junk": _sb(2 * C, BF),
+    "O": _sb(C, BF), "Gp": _sb(2 * C, BF), "p3": _sb(2 * C, BF), "pc": _sb(C, BF), "t320": _sb(16, BF), "old": _sb(L, BF),
+    "lp": _sb(C, BF), "lpl": _sb(C, BF), "pn": _sb(C, BF), "tb": _sb(C, BF), "tc": _sb(C, BF),
+    "win": _sb(480, BF), "wi": _sb(80, I32), "ei": _sb(16, I32), "sm": _sb(320, F32),
+    "seg": _sb(160, F32), "sgo": _sb(160, F32), "seh": _sb(C, F32), "sho": _sb(C, F32),
+    "oplace": _sb(20, U16), "opt": _sb(20, U16), "oab": _sb(80, U16), "oidx": _sb(20, U16), "olam": _sb(20, U16), "onp": _sb(40, U16),
+    "osg": _sb(6, U16), "ol4": _sb(24, U16), "ol16": _sb(6, U16), "os4": _sb(80, U16), "os16": _sb(20, U16),
+    "yo": _sb(C, F32), "po": _sb(C, F32), "po2": _sb(C, F32),
+}
+for _r in range(R):
+    SCRATCH["qc%d" % _r] = _sb(128, Q4)
+    SCRATCH["sc%d" % _r] = _sb(128, U8)
+    SCRATCH["lq%d" % _r] = _sb(128, Q4)
+    SCRATCH["ls%d" % _r] = _sb(128, U8)
+    SCRATCH["pa%d" % _r] = _sb(L, BF)
+    SCRATCH["ps%d" % _r] = _sb(L, BF)
+for _b in "ABCDEFG":
+    SCRATCH["p" + _b] = ("psum", [128, 512], F32)
+SMALL = {}
+_at = 0
+for _n, _w in (("mpar", 32), ("em", 32), ("ef", 32), ("acc", 32), ("es", 1), ("e16", 16), ("bk", 8), ("wk", 8), ("su2", 8), ("df", 8),
+               ("dg", 8), ("jw", 10), ("sig", 20), ("s2", 20), ("s1", 20), ("lw", 6), ("lx", 6)):
+    SMALL[_n] = (_at, _w)
+    _at += _w
+
+NDMA = 20
+SEMAPHORES = ["cV", "cS", "cT", "cG", "sent"] + ["d%d" % i for i in range(NDMA)] + \
+    ["a%s%d" % (k, r) for k in "qsp" for r in range(R)]
+
+A = AluOpType
+ACT = ActivationFunctionType
+
+
+def vw(name, a=0, b=None, s=1):
+    if name in SMALL:
+        o, w = SMALL[name]
+        return ("sm", o + a, o + (w if b is None else b), s)
+    return (name, a, SCRATCH[name][1][1] if b is None else b, s)
+
+
+def col(name, j):
+    return vw(name, j, j + 1)
+
+
+def ind(win, off):
+    return ("*", win, off)
+
+
+def rank_program(g, core, T, topo):
+    rank = T.rank_of(core)
+    if rank is None:
+        return
+    cores = list(T.cores)
+    nxt, prv = cores[(rank + 1) % len(cores)], cores[(rank - 1) % len(cores)]
+    Q = {"V": g.vector, "S": g.scalar, "T": g.tensor, "G": g, "Y": g.sync}
+    ops = []
+    ndma = [0]
+
+    def ap(v, cast=None):
+        if v[0] == "*":
+            return ap(v[1], cast).indirect(ap(v[2]))
+        a = T[v[0]][:, v[1]:v[2]:v[3]] if v[3] != 1 else T[v[0]][:, v[1]:v[2]]
+        return a.bitcast(cast) if cast is not None else a
+
+    def sc(v):
+        return ap(v) if isinstance(v, tuple) else v
+
+    def parts(vs):
+        out = []
+        for v in vs:
+            if isinstance(v, tuple):
+                out += [v[1], v[2]] if v[0] == "*" else [v]
+        return out
+
+    def add(eng, fn, reads, writes, sem=None, val=0, acc=False):
+        ops.append({"eng": eng, "fn": fn, "r": parts(reads), "w": parts(writes), "sem": sem, "val": val, "acc": acc})
+
+    def scat(out, off, in_):
+        add("V", lambda q: q.tensor_copy(ap(ind(out, off)), ap(in_)), [off, in_], [out])
+
+    def cp(e, out, in_, scale=None):
+        if e == "V" and scale is None:
+            add(e, lambda q: q.tensor_copy(ap(out), ap(in_)), [in_], [out])
+        elif e == "V":
+            ts(out, in_, scale, A.mult)
+        elif scale is None:
+            add(e, lambda q: q.activation(ap(out), ap(in_), ACT.Copy), [in_], [out])
+        else:
+            add(e, lambda q: q.activation(ap(out), ap(in_), ACT.Copy, scale=scale), [in_], [out])
+
+    def plus(out, in_, bias):
+        add("S", lambda q: q.activation(ap(out), ap(in_), ACT.Identity, bias=ap(bias)), [in_, bias], [out])
+
+    def ts(out, in0, s1, o0, s2=None, o1=None):
+        if o1 is None:
+            add("V", lambda q: q.tensor_scalar(ap(out), ap(in0), sc(s1), None, o0), [in0, s1], [out])
+        else:
+            add("V", lambda q: q.tensor_scalar(ap(out), ap(in0), sc(s1), sc(s2), o0, o1), [in0, s1, s2], [out])
+
+    def tt(out, in0, in1, o):
+        add("V", lambda q: q.tensor_tensor(ap(out), ap(in0), ap(in1), o), [in0, in1], [out])
+
+    def scan(out, d0, d1, init, o0):
+        add("V", lambda q: q.tensor_tensor_scan(ap(out), ap(d0), ap(d1), init, o0, A.add), [d0, d1], [out])
+
+    def sign(out, in_, bias, scale, accum=None):
+        if accum is None:
+            add("S", lambda q: q.activation(ap(out), ap(in_), ACT.Sign, bias=sc(bias), scale=scale), [in_, bias], [out])
+        else:
+            add("S", lambda q: q.activation(ap(out), ap(in_), ACT.Sign, bias=sc(bias), scale=scale, accum_out=ap(accum)),
+                [in_, bias], [out, accum])
+
+    def fill(out, c):
+        add("V", lambda q: q.memset(ap(out), c), [], [out])
+
+    def trans(out, in_):
+        add("V", lambda q: q.transpose(ap(out), ap(in_)), [in_], [out])
+
+    def quant(qn, sn, a, b, in_):
+        add("V", lambda q: q.quantize_mx(ap(vw(qn, a, b)), ap(vw(sn, a, b)), ap(in_)), [in_], [vw(qn, a, b), vw(sn, a, b)])
+
+    def mm(bank, w, x, start=True, stop=True):
+        lq, ls, rq, rs = vw(w[0], w[2], w[2] + 128), vw(w[1], w[2], w[2] + 128), vw(x[0], x[2], x[3]), vw(x[1], x[2], x[3])
+        out = vw(bank, 0, x[3] - x[2])
+        add("T", lambda q: q.matmul_mx(ap(out), ap(lq), ap(ls), ap(rq), ap(rs), start, stop), [lq, ls, rq, rs], [out], acc=not start)
+
+    def iota(out, pat, base, cm):
+        if SCRATCH[out[0]][2] == I32:
+            add("G", lambda q: q.iota(ap(out), pat, base, cm), [], [out])
+        else:
+            add("G", lambda q: q.iota(ap(out), pat, base, cm, allow_small_or_imprecise_dtypes=True), [], [out])
+
+    def where(out, pat, op, base, cm):
+        ones = vw("ones", 0, out[2] - out[1])
+        add("G", lambda q: q.affine_select(ap(out), ap(ones), pat, op, 0.0, base, cm), [ones], [out])
+
+    def dma(e, fo, fi, reads, writes):
+        s = "d%d" % ndma[0]
+        ndma[0] += 1
+        add(e, lambda q: q.dma_start(fo(), fi()), reads, writes, sem=s, val=16)
+
+    rid, pid, _ = topo.addr(nxt)
+    nout, nin = len(topo.engines(core, nxt)), len(topo.engines(prv, core))
+    nsent = [0]
+
+    def send(dst, src, sem, cast=None):
+        nsent[0] += nout
+        add("G", lambda q: q.remote_dma(ap(dst, cast), ap(src, cast), T.sem[sem], T.sem.sent, pid, rid, topo.mask(core, nxt)),
+            [src], [], sem="-")
+
+    def arrive(dst, sem):
+        add(None, None, [], [dst], sem=sem, val=nin)
+
+    def wrap(out, masked, b, seg, a=0):
+        scan(vw(out, a, b), vw("r%d" % seg, a, b), vw(masked, a, b), 0.0, A.mult)
+
+    def pick(a, b):
+        o, s, off = vw("qur", 16 * a, 16 * b), vw("sur", 16 * a, 16 * b), vw("uo", a, b)
+        add("V", lambda q: q.tensor_copy(ap(o, dt.uint32), ap(ind(vw("qu"), off), dt.uint32)), [vw("qu"), off], [o])
+        cp("S", s, ind(vw("su"), off))
+
+    dma("S", lambda: T.ut[:], lambda: T.u[:], [], [vw("ut")])
+    dma("Y", lambda: T.x0[:], lambda: T.x[:], [], [vw("x0")])
+    dma("Y", lambda: ap(vw("qw"), dt.uint8), lambda: T.wc[:], [], [vw("qw")])
+    dma("Y", lambda: T.sw[:], lambda: T.ws[:], [], [vw("sw")])
+    dma("Y", lambda: T.vt[:], lambda: T.v[:], [], [vw("vt")])
+    iota(col("pi", 0), [[0, 1]], 0, 1)
+    iota(vw("ui", 0, 8), [[16, 8]], 0, 0)
+    iota(vw("ui", 8, 24), [[16, 2], [32, 4], [0, 2]], 0, 0)
+    iota(vw("a0i"), [[1, 8], [0, 16], [50, 4]], 0, 0)
+    iota(vw("ic"), [[1, C]], 0, 0)
+    iota(vw("a1i"), [[1, 8], [0, 32], [-1, 2]], 0, 0)
+    iota(vw("seg"), [[0, 160]], 0, 0)
+    iota(vw("seh"), [[0, C]], 0, 0)
+    iota(vw("i16"), [[0, 20], [1, 16]], 0, 0)
+    iota(vw("ones"), [[0, 512]], 1, 0)
+    for n, w, k in (("r8", 160, 8), ("r16", C, 16), ("r4", C, 4)):
+        where(vw(n), [[0, w // k], [1, k]], A.not_equal, 0, 0)
+    iota(vw("icb"), [[1, C + L]], -240, 0)
+    iota(vw("Gp", 0, C), [[0, C]], 0, 0)
+    iota(vw("O"), [[0, C]], 0, 0)
+    iota(vw("ic2"), [[0, 2], [1, C]], -160, 0)
+    iota(vw("i4"), [[0, 80], [1, 4]], 0, 0)
+    iota(vw("t320"), [[320, 16]], 320, 0)
+    iota(vw("zero"), [[0, 512]], 0, 0)
+    iota(vw("cmp", 4 * L, 512), [[0, 512 - 4 * L]], 0, 0)
+    for b in range(4):
+        where(vw("et", 512 * b, 512 * b + 512), [[1, 512]], A.is_equal, -b, -4)
+    fill(vw("pb"), 0.0)
+    for j, m in ((1, 15), (2, 3), (3, 7)):
+        ts(col("pi", j), col("pi", 0), m, A.bitwise_and)
+    ts(col("pi", 4), col("pi", 0), 4, A.arith_shift_right)
+    ts(col("pi", 5), col("pi", 0), 5, A.arith_shift_right)
+    ts(col("pi", 6), col("pi", 0), 15, A.bitwise_and, 2, A.arith_shift_right)
+    ts(col("pi", 7), col("pi", 0), 4, A.arith_shift_right, 1, A.bitwise_and)
+    cp("V", vw("uo"), vw("ui"))
+    cp("V", vw("pf", 0, 8), vw("pi"))
+    fill(col("pf", 16), 160.0)
+    ts(col("pf", 11), col("pf", 1), 2.0, A.subtract)
+    ts(col("pf", 9), col("pf", 2), 640.0, A.add)
+    tt(col("pf", 12), col("pf", 11), col("pf", 11), A.mult)
+    ts(col("pf", 8), col("pf", 5), 2.0, A.mult)
+    ts(col("pf", 13), col("pf", 12), 1.5, A.is_gt, 20.0, A.mult)
+    ts(col("pf", 10), col("pf", 3), -320.0, A.mult, -160.0, A.add)
+    tt(col("pf", 14), col("pf", 13), col("pf", 4), A.add)
+    ts(col("pf", 17), col("pf", 2), 960.0, A.add)
+    quant("qu", "su", 0, 128, vw("ut"))
+    quant("qx", "sx", 0, C, vw("x0"))
+    pick(0, 8)
+    pick(16, 24)
+    pick(8, 16)
+
+    def consts_0():
+        ts(vw("at", 512, 1024), vw("a0i"), col("pf", 14), A.is_equal, 320.0, A.mult)
+        quant("qa", "sa", 128, 256, vw("at", 512, 1024))
+
+    def consts_a():
+        ts(vw("at", 0, 512), vw("a1i"), col("pf", 8), A.is_equal, -0.25, A.mult)
+        quant("qa", "sa", 0, 128, vw("at", 0, 512))
+
+    def consts_b():
+        ts(vw("em"), vw("ic", 0, 32), 15.5, A.is_gt)
+        ts(vw("sig"), vw("ic", 0, 20), 16.0, A.mult, col("pf", 1), A.add)
+        ts(vw("m16"), vw("i16"), col("pf", 1), A.is_equal)
+        ts(vw("mpar"), vw("em"), col("pf", 7), A.is_equal)
+        cp("V", vw("jw"), vw("sig", 0, 10))
+        cp("V", vw("seg", 7, 80, 8), vw("sig", 0, 10))
+        cp("V", vw("seg", 87, 160, 8), vw("sig", 0, 10))
+        ts(vw("s2"), vw("sig"), -2.0, A.mult, 640.0, A.add)
+        ts(vw("s1"), vw("sig"), -1.0, A.mult, 320.0, A.add)
+        ts(vw("seh", 15, C, 16), vw("sig"), -2.0, A.mult, 2.0 * 639, A.add)
+
+    def consts_e():
+        ts(vw("m4"), vw("i4"), col("pf", 6), A.is_equal)
+
+    def consts_f():
+        ts(vw("lw"), vw("sig", 0, 6), -160.0, A.add)
+        ts(vw("lx"), vw("sig", 0, 6), -159.5, A.add)
+
+    def consts_c():
+        quant("q0", "s0", 0, 128, vw("zero"))
+        for r in range(R):
+            dma("Y", lambda r=r: ap(vw("lq%d" % r, L, 128), dt.uint8), lambda: ap(vw("q0", 0, 128 - L), dt.uint8),
+                [vw("q0")], [vw("lq%d" % r, L, 128)])
+            dma("Y", lambda r=r: ap(vw("ls%d" % r, L, 128)), lambda: ap(vw("s0", 0, 128 - L)), [vw("s0")], [vw("ls%d" % r, L, 128)])
+
+    def statics(r):
+        top = 3 + r
+        st = []
+        st.append(lambda: ts(vw("em"), vw("mpar"), col("es", 0), A.mult))
+        st.append(lambda: trans(vw("ef"), vw("em")))
+        st.append(lambda: tt(vw("e16"), vw("ef", 0, 16), vw("ef", 16, 32), A.add))
+
+        def s1():
+            ts(vw("ei", 0, 8), vw("e16", 0, 8), 320.0, A.add)
+            tt(vw("su2", 0, 7), vw("e16", 0, 7), vw("e16", 1, 8), A.add)
+            tt(vw("df", 0, 7), vw("e16", 0, 7), vw("e16", 1, 8), A.subtract)
+            ts(vw("ei", 8, 16), vw("ei", 0, 8), 2, A.arith_shift_right)
+
+        def s2():
+            ts(vw("dg", 0, 7), vw("df", 0, 7), 2048.0 - 640.0, A.add)
+            cp("V", vw("bk"), vw("ei", 8, 16))
+            for k in range(top):
+                ts(vw("seh", 8 + k, C, 16), vw("s1"), col("e16", k + 1), A.is_le, 16384.0 + 640.0, A.mult)
+            tt(vw("wk", 0, 7), vw("bk", 0, 7), vw("bk", 1, 8), A.subtract)
+            for k in range(top + 1):
+                ts(vw("seh", k, C, 16), vw("s2"), col("su2", k), A.is_le, col("dg", k), A.mult)
+
+        def s3():
+            for k in range(top + 1):
+                if k:
+                    ts(vw("seg", k, 80, 8), vw("jw"), col("bk", k), A.is_ge, col("wk", k), A.mult)
+                ts(vw("seg", 80 + k, 160, 8), vw("jw"), col("bk", k + 1), A.is_ge, col("wk", k), A.mult)
+
+        def s4():
+            wrap("sgo", "seg", 160, 8)
+            wrap("sho", "seh", C, 16)
+
+        def s5():
+            cp("V", vw("opt"), vw("sgo", 7, 160, 8))
+            cp("V", vw("wi", 0, 20), vw("sho", 15, C, 16))
+
+        def s6():
+            ts(vw("wi", 20, 40), vw("wi", 0, 20), 2047, A.bitwise_and)
+            ts(vw("wi", 40, 60), vw("wi", 0, 20), 11, A.arith_shift_right, 7, A.bitwise_and)
+            ts(vw("wi", 60, 80), vw("wi", 0, 20), 14, A.arith_shift_right)
+
+        def s7():
+            ts(vw("oidx"), vw("wi", 20, 40), 0.5, A.mult)
+            cp("V", vw("onp"), vw("wi", 40, 80))
+        return st + [s1, s2, s3, s4, s5, s6, s7]
+
+    def s_rows(keys, a, b, own):
+        for m in range(a, b):
+            sign(vw("junk", C * (m % 2), C * (m % 2) + C), keys, own(m), -1.0, col("acc", m))
+
+    def v_row(keys, m, own, op):
+        ts(vw("cb", C * (m % 3), C * (m % 3) + C), keys, own(m), op)
+
+    def v_sum(m):
+        k = C * (m % 3)
+        scan(vw("co", 160 * m, 160 * m + 160), vw("cb", k, k + 160), vw("cb", k + 160, k + C), -160.0, A.add)
+
+    def counts(out, nv, rows, s_mul, s_add):
+        ts(vw(out, 0, nv), vw("co", 159, 160 * nv, 160), 160.0, A.add)
+        ts(vw(out, nv, rows), vw("acc", nv, rows), s_mul, A.mult, s_add, A.add)
+
+    def new_points(r):
+        tt(vw("win", C, C + L), vw("pa%d" % r), vw("old"), A.subtract)
+        tt(vw("kst"), ind(vw("win", 0, C + L), vw("os16")), vw("kst"), A.add)
+
+    U16R, U32A, U32B = ("qur", "sur", 0), ("qur", "sur", 128), ("qur", "sur", 256)
+    QX = ("qx", "sx", 0, C)
+    for r in range(R):
+        xs = "x0" if r == 0 else "X"
+        if r == 0:
+            mm("pF", ("qu", "su", 0), QX)
+        else:
+            quant("qx", "sx", 0, C, vw(xs))
+        mm("pA", U16R, QX)
+        mm("pD", U32B, QX)
+        mm("pB", U32A, QX)
+        mm("pC", U32A, QX)
+        side = statics(r)
+        if r == 0:
+            ts(vw("pb", 0, 4 * C, 4), vw("pF", 0, C), 0.0, A.is_gt)
+            trans(vw("tr"), vw("pA", 0, C))
+            quant("qp", "sp", 0, C, vw("pb"))
+            consts_0()
+            mm("pG", ("qa", "sa", 128), ("qp", "sp", 0, C))
+            ts(vw("fr0"), vw("ic"), -1.0 / 2048, A.mult, 320 + 511.0 / 2048, A.add)
+            consts_a()
+            tt(vw("kst"), vw("pG", 0, C), vw("fr0"), A.add)
+            consts_b()
+        else:
+            cp("S", vw("Xh", 0, XH), vw(xs, 0, XH), 0.5)
+            trans(vw("tr"), vw("pA", 0, C))
+        rows_v = [(b // 2, 2 * (b % 2)) for b in range(NV1[r])]
+        order = [4, 3, 2, 1, 0]
+        rows_s = [(tl, t) for tl in order for t in (1, 3, 0, 2) if (tl, t) not in rows_v]
+        rows_v = [(tl, t) for tl in order for t in range(4) if (tl, t) in rows_v]
+        for i, (tl, t) in enumerate(rows_s):
+            if r == 0 and i == 5:
+                sign(vw("junk", 0, C), vw("kst"), col("pf", 10), 1.0, col("es", 0))
+            sign(vw("bits", 4 * C * tl + t, 4 * C * (tl + 1), 4), vw("pD" if t % 2 else "pC", 0, C),
+                 col("tr", 32 * (2 * tl + t // 2) + 16 * (t % 2)), -1.0)
+
+        def row(tl, t):
+            ts(vw("bits", 4 * C * tl + t, 4 * C * (tl + 1), 4), vw("pB", 0, C), col("tr", 32 * (2 * tl + t // 2)), A.is_lt, 2.0, A.mult)
+
+        def tile(k):
+            quant("qb", "sb", C * k, C * k + C, vw("bits", 4 * C * k, 4 * C * k + 4 * C))
+            mm("pE", ("qa", "sa", 0), ("qb", "sb", C * k, C * k + C), k == order[0], k == order[-1])
+        rv = [lambda x=x: row(*x) for x in rows_v]
+        tl_ = [lambda k=k: tile(k) for k in order]
+        for ch in PAT1:
+            lst = {"r": rv, "s": side, "T": tl_}[ch]
+            if lst:
+                lst.pop(0)()
+        xa = 0 if r == 0 else XH
+        cp("S", vw("Xh", xa, min(xa + 640, 4 * C)), vw(xs, xa, min(xa + 640, 4 * C)), 0.5)
+        side.pop(0)()
+        h = 16 * NV2
+        tt(vw("K"), vw("pE", 0, C), vw("kst"), A.add)
+        side.pop(0)()
+        tt(vw("km", h, C), vw("K", h, C), vw("m16", h, C), A.mult)
+        wrap("kw", "km", C, 16, h)
+        tt(vw("km", 0, h), vw("K", 0, h), vw("m16", 0, h), A.mult)
+        wrap("kw", "km", h, 16)
+        own = lambda m: col("kw", 16 * m + 15)
+        s_rows(vw("K"), NV2, 20, own)
+        scat(vw("Gp", 0, C), vw("opt"), vw("icb", 0, C))
+        for m in range(NV2 + 1):
+            if m < NV2:
+                v_row(vw("K"), m, own, A.is_gt)
+            if m:
+                v_sum(m - 1)
+            if side:
+                side.pop(0)()
+        if r == 0:
+            consts_e()
+        counts("oplace", NV2, 20, -0.5, 159.5)
+        scat(vw("O"), vw("oplace"), vw("ic2", 0, C))
+        if r == 0:
+            cp("S", vw("Xh", 640, 4 * C), vw(xs, 640, 4 * C), 0.5)
+        plus(vw("Gp", C, 2 * C), vw("Gp", 0, C), col("pf", 16))
+        cp("S", vw("p3", 0, C), vw("Gp", 0, C))
+        cp("S", vw("p3", C, 2 * C), vw("Gp", 0, C))
+        if r:
+            cp("S", vw("lp"), ind(vw("p3"), vw("oidx")))
+        for k in range(2):
+            tt(vw("kb", 160 * k, 160 * k + 160), ind(vw("O"), vw("opt", 10 * k, 10 * k + 10)), vw("m4", 0, 160), A.mult)
+        for k in range(2):
+            wrap("kc", "kb", 160 * k + 160, 4, 160 * k)
+        for k in range(2):
+            ts(vw("oab", 40 * k, 40 * k + 40), vw("kc", 160 * k + 3, 160 * k + 160, 4), 4.0, A.mult, col("pf", 9), A.add)
+        cuts = list(zip(ZCUT, ZCUT[1:]))
+        for a, b in cuts[1:]:
+            cp("S", vw("ah", 16 * a, 16 * b), ind(vw("Xh"), vw("oab", a, b)))
+        cp("V", vw("ah", 0, 16 * ZCUT[1]), ind(vw("Xh"), vw("oab", 0, ZCUT[1])))
+        for a, b in cuts:
+            tt(vw("Z", 16 * a, 16 * b), ind(vw("Xh"), vw("oab", 40 + a, 40 + b)), vw("ah", 16 * a, 16 * b), A.add)
+        quant("qz", "sz", 0, 160, vw("Z"))
+        if r == 0:
+            cp("S", vw("lp"), ind(vw("p3"), vw("oidx")))
+        cp("S", vw("pn"), ind(vw("t320"), vw("onp", 0, 20)))
+        for b in range(4):
+            mm("p" + "ABCD"[b], ("qw", "sw", 128 * b), ("qz", "sz", 0, 160))
+        tt(vw("kb"), ind(vw("Gp"), vw("oidx")), vw("m16"), A.mult)
+        if r == 0:
+            consts_f()
+        for b in range(4):
+            cp("SV"[b // 2], vw("H", b, 640, 4), vw("p" + "ABCD"[b], 0, 160), 0.03125)
+        quant("qh", "sh", 0, 160, vw("H"))
+        mm("pE", U16R, ("qh", "sh", 0, 160))
+        mm("pF", U16R, ("qh", "sh", 0, 160))
+        cp("S", vw("pc"), ind(vw("t320"), vw("onp", 20, 40)))
+        wrap("kc", "kb", C, 16)
+        ts(vw("olam"), vw("kc", 15, C, 16), 240.0, A.add)
+        ts(vw("win", 0, 160), vw("pE", 0, 160), 0.0, A.is_gt, 320.0, A.mult)
+        ts(vw("win", 160, C), vw("pE", 0, 160), 0.0, A.is_le, 320.0, A.mult)
+        add("S", lambda q: q.activation(ap(vw("win", C, 480)), ap(vw("pF", 0, 160)), ACT.Relu), [vw("pF", 0, 160)], [vw("win", C, 480)])
+        sign(vw("tb", 160, C), ind(vw("win"), vw("olam", 10, 20)), 0.0, 1.0)
+        ts(vw("tb", 0, 160), ind(vw("win"), vw("olam", 0, 10)), 0.0, A.is_gt)
+        scan(vw("tc"), vw("tb"), vw("zero", 0, C), -160.0, A.add)
+        s_rows(vw("tc"), 2, 6, lambda m: col("lx", m))
+
+        def y_piece(a, b):
+            k = 0 if a < 40 else 640
+            tt(vw("Y", 16 * a, 16 * b), ind(vw(xs), vw("oab", a, b)), vw("H", 16 * a - k, 16 * b - k), A.subtract if k else A.add)
+        y_piece(0, 10)
+        for m in range(2):
+            v_row(vw("tc"), m, lambda m: col("lw", m), A.is_le)
+        for m in range(2):
+            v_sum(m)
+        y_piece(10, 40)
+        y_piece(40, 52)
+        counts("osg", 2, 6, 0.5, 160.0)
+        y_piece(52, 62)
+        tt(vw("kb", 0, L), ind(vw("lp"), vw("osg")), vw("m4", 0, L), A.mult)
+        cp("S", vw("ps%d" % r), ind(vw("pn"), vw("osg")))
+        cp("S", vw("lpl"), ind(vw("ic2"), vw("oidx")))
+        y_piece(62, 72)
+        wrap("kc", "kb", L, 4)
+        y_piece(72, 80)
+        ts(vw("ol4"), vw("kc", 3, L, 4), 4.0, A.mult, col("pf", 17), A.add)
+        cp("S", vw("cmp", 192, 384), ind(vw("Y", 0, 4 * C), vw("ol4", 12, 24)))
+        cp("V", vw("cmp", 0, 192), ind(vw("Y", 0, 4 * C), vw("ol4", 0, 12)))
+        quant("qc%d" % r, "sc%d" % r, 0, 128, vw("cmp"))
+        send(vw("pa%d" % r), vw("ps%d" % r), "ap%d" % r)
+        send(vw("lq%d" % r, 0, L), vw("qc%d" % r, 0, L), "aq%d" % r, dt.uint8)
+        send(vw("ls%d" % r, 0, L), vw("sc%d" % r, 0, L), "as%d" % r)
+        cp("S", vw("old"), ind(vw("pc"), vw("osg")))
+        tt(vw("kb", 0, L), ind(vw("lpl"), vw("osg")), vw("m16", 0, L), A.mult)
+        if r == 0:
+            consts_c()
+        wrap("kc", "kb", L, 16)
+        if r == 0:
+            quant("qe", "se", 0, 512, vw("et"))
+        ts(vw("ol16"), vw("kc", 15, L, 16), 160.0, A.add)
+        scat(vw("Gp", 0, C), vw("ol16"), vw("icb", C, C + L))
+        tt(vw("kd"), ind(vw("Gp", 0, C), vw("oplace")), vw("m16"), A.mult)
+        tt(vw("kb"), ind(vw("Gp", 0, C), vw("oplace")), vw("m4"), A.mult)
+        wrap("ke", "kd", C, 16)
+        wrap("kc", "kb", C, 4)
+        ts(vw("os16"), vw("ke", 15, C, 16), 240.0, A.add)
+        ts(vw("os4"), vw("kc", 3, C, 4), 4.0, A.mult, col("pf", 17), A.add)
+        arrive(vw("lq%d" % r, 0, L), "aq%d" % r)
+        arrive(vw("ls%d" % r, 0, L), "as%d" % r)
+        arrive(vw("pa%d" % r), "ap%d" % r)
+        new_points(r)
+        if r == R - 1:
+            ts(vw("po"), vw("kst"), 1.0 / 320, A.mult, 12582912.0, A.add)
+            quant("qv", "sv", 0, 128, vw("vt"))
+            ts(vw("po2"), vw("po"), 12582913.0, A.subtract)
+            dma("Y", lambda: T.pts[:], lambda: T.po2[0:128:16, :], [vw("po2")], [])
+        for b in range(4):
+            mm("p" + "ABCD"[b], ("qe", "se", 128 * b), ("lq%d" % r, "ls%d" % r, 0, 128))
+        for b in range(4):
+            cp("SV"[b % 2], vw("Y", 4 * C + b, 4 * (C + L), 4), vw("p" + "ABCD"[b], 0, L))
+        cp("S", vw("X", 640, 1280), ind(vw("Y"), vw("os4", 40, 80)))
+        cp("V", vw("X", 0, 640), ind(vw("Y"), vw("os4", 0, 40)))
+        if r < R - 1:
+            sign(vw("junk", 0, C), vw("kst"), col("pf", 10), 1.0, col("es", 0))
+
+    quant("qx", "sx", 0, C, vw("X"))
+    mm("pE", ("qv", "sv", 0), QX)
+    dma("Y", lambda: T.oc[:], lambda: ap(vw("qx"), dt.uint8), [vw("qx")], [])
+    cp("V", vw("yo"), vw("pE", 0, C))
+    for k in range(4):
+        dma("YS"[k // 2], lambda k=k: T.osc[4 * k:4 * k + 4, :], lambda k=k: T.sx[32 * k:32 * k + 4, :], [vw("sx")], [])
+    dma("S", lambda: T.y[:], lambda: T.yo[:], [vw("yo")], [])
+
+    hist = {}
+    for i, o in enumerate(ops):
+        deps = set()
+        for v, wr in [(v, False) for v in o["r"]] + [(v, True) for v in o["w"]]:
+            psum = SCRATCH[v[0]][0] == "psum"
+            m = np.zeros(SCRATCH[v[0]][1][1], bool)
+            m[v[1]:v[2]:v[3]] = True
+            if psum:
+                m[:] = True
+            h = hist.setdefault(v[0], [])
+            for j, mj, wj in h:
+                if j == i or not (m & mj).any():
+                    continue
+                same = ops[j]["eng"] == o["eng"]
+                if (wr or wj or (psum and not same)) and not (same and o["acc"]):
+                    deps.add(j)
+            if wr and not o["acc"]:
+                h[:] = [e for e in h if (e[1] & ~m).any()]
+            h.append((i, m, wr))
+        o["deps"] = deps
+    needed = set()
+    for o in ops:
+        needed |= o["deps"]
+    n = {"V": 0, "S": 0, "T": 0, "G": 0}
+    for i, o in enumerate(ops):
+        o["inc"] = False
+        if o["sem"] is None and i in needed:
+            n[o["eng"]] += 1
+            o["sem"], o["val"], o["inc"] = "c" + o["eng"], n[o["eng"]], True
+    known = {e: {} for e in Q}
+    for o in ops:
+        if o["eng"] is None:
+            o["know"] = {}
+            continue
+        k = known[o["eng"]]
+        for j in sorted(o["deps"], reverse=True):
+            d = ops[j]
+            if k.get(d["sem"], 0) < d["val"]:
+                Q[o["eng"]].wait_ge(T.sem[d["sem"]], d["val"])
+                k[d["sem"]] = d["val"]
+                for s, x in d["know"].items():
+                    k[s] = max(k.get(s, 0), x)
+        o["know"] = dict(k)
+        inst = o["fn"](Q[o["eng"]])
+        if o["inc"]:
+            inst.then_inc(T.sem[o["sem"]], 1)
+        elif o["val"] == 16:
+            inst.then_inc(T.sem[o["sem"]], 16)
+    for e in n:
+        if n[e]:
+            g.wait_ge(T.sem["c" + e], n[e])
+    for i in range(ndma[0]):
+        g.wait_ge(T.sem["d%d" % i], 16)
+    g.wait_ge(T.sem.sent, nsent[0])

@@ -2,11 +2,17 @@ import numpy as np
 from concourse.mybir import dt, AluOpType, ActivationFunctionType
 
 C, L, R = 320, 96, 3
-F32, BF, I32, U16, Q4, U8 = "float32", "bfloat16", "int32", "uint16", "float8_e4m3fn_x4", "uint8"
-NV1, NV2 = (4, 6, 6), 8
-PAT1 = "rsrsrssrTsrTrTsTT"
+F32, BF, F16, I32, U16, Q4, U8 = "float32", "bfloat16", "float16", "int32", "uint16", "float8_e4m3fn_x4", "uint8"
+BIG = 1e29
+TILES = ((20, 19, 18, 17), (16, 15, 14, 13), (12, 11, 10, 9), (8, 7, 6, 5), (4, 3, 2, 1))
+TILE0 = (0, 320, 576, 768, 896, 1024)
+NS = (12, 12, 12)
+NVL = 3
 ZCUT = (0, 8, 24, 40)
-XH = 800
+ZV = 1
+KW = 2
+WAKE, LOCAL, REMOTE, SLACK = 220.0, 2500.0, 2600.0, 60.0
+SCHED = True
 
 
 def _sb(n, d):
@@ -16,27 +22,26 @@ def _sb(n, d):
 SCRATCH = {
     "x0": _sb(4 * C, BF), "X": _sb(4 * C, BF), "Xh": _sb(4 * C, BF), "Y": _sb(4 * (C + L), BF),
     "ut": _sb(512, BF), "vt": _sb(512, BF),
-    "qu": _sb(128, Q4), "su": _sb(128, U8), "qur": _sb(384, Q4), "sur": _sb(384, U8), "qv": _sb(128, Q4), "sv": _sb(128, U8),
+    "qu": _sb(128, Q4), "su": _sb(128, U8), "qur": _sb(128, Q4), "sur": _sb(128, U8), "qv": _sb(128, Q4), "sv": _sb(128, U8),
     "qw": _sb(512, Q4), "sw": _sb(512, U8), "qx": _sb(C, Q4), "sx": _sb(C, U8),
     "qz": _sb(160, Q4), "sz": _sb(160, U8), "qh": _sb(160, Q4), "sh": _sb(160, U8),
-    "ones": _sb(512, BF), "zero": _sb(512, BF), "et": _sb(2048, BF), "qe": _sb(512, Q4), "se": _sb(512, U8),
-    "a1i": _sb(512, BF), "a0i": _sb(512, BF), "at": _sb(1024, BF), "qa": _sb(256, Q4), "sa": _sb(256, U8),
-    "q0": _sb(128, Q4), "s0": _sb(128, U8),
-    "bits": _sb(5 * 4 * C, BF), "qb": _sb(5 * C, Q4), "sb": _sb(5 * C, U8), "pb": _sb(4 * C, BF), "qp": _sb(C, Q4), "sp": _sb(C, U8),
-    "tr": _sb(C, F32), "ah": _sb(640, BF), "Z": _sb(640, BF), "H": _sb(640, BF), "cmp": _sb(512, BF),
-    "ic": _sb(C, F32), "icb": _sb(C + L, BF), "ic2": _sb(2 * C, BF), "i16": _sb(C, BF), "i4": _sb(C, BF), "fr0": _sb(C, F32),
-    "m16": _sb(C, BF), "m4": _sb(C, BF), "r16": _sb(C, BF), "r4": _sb(C, BF), "r8": _sb(160, BF),
-    "pi": _sb(8, I32), "pf": _sb(20, F32), "ui": _sb(24, I32), "uo": _sb(24, U16),
-    "kst": _sb(C, F32), "K": _sb(C, F32), "km": _sb(C, F32), "kw": _sb(C, F32),
-    "kb": _sb(C, BF), "kc": _sb(C, BF), "kd": _sb(C, BF), "ke": _sb(C, BF),
-    "cb": _sb(3 * C, BF), "co": _sb(20 * 160, BF), "junk": _sb(2 * C, BF),
-    "O": _sb(C, BF), "Gp": _sb(2 * C, BF), "p3": _sb(2 * C, BF), "pc": _sb(C, BF), "t320": _sb(16, BF), "old": _sb(L, BF),
-    "lp": _sb(C, BF), "lpl": _sb(C, BF), "pn": _sb(C, BF), "tb": _sb(C, BF), "tc": _sb(C, BF),
-    "win": _sb(480, BF), "wi": _sb(80, I32), "ei": _sb(16, I32), "sm": _sb(320, F32),
-    "seg": _sb(160, F32), "sgo": _sb(160, F32), "seh": _sb(C, F32), "sho": _sb(C, F32),
-    "oplace": _sb(20, U16), "opt": _sb(20, U16), "oab": _sb(80, U16), "oidx": _sb(20, U16), "olam": _sb(20, U16), "onp": _sb(40, U16),
-    "osg": _sb(6, U16), "ol4": _sb(24, U16), "ol16": _sb(6, U16), "os4": _sb(80, U16), "os16": _sb(20, U16),
-    "yo": _sb(C, F32), "po": _sb(C, F32), "po2": _sb(C, F32),
+    "zero": _sb(640, BF), "et": _sb(2048, BF), "qe": _sb(512, Q4), "se": _sb(512, U8),
+    "ai": _sb(512, BF), "at": _sb(1024, BF), "qa": _sb(256, Q4), "sa": _sb(256, U8), "q0": _sb(128, Q4), "s0": _sb(128, U8),
+    "bits": _sb(4096, BF), "qb": _sb(1024, Q4), "sb": _sb(1024, U8), "pb": _sb(4 * C, BF), "qp": _sb(C, Q4), "sp": _sb(C, U8),
+    "ah": _sb(640, BF), "Z": _sb(640, BF), "H": _sb(4 * C, BF), "cmp": _sb(512, BF),
+    "ic2": _sb(C, F32), "icb": _sb(C + L, BF), "i16": _sb(C, BF), "i4": _sb(C, BF), "t16": _sb(16, BF), "sg0": _sb(52, F32),
+    "m16": _sb(C, BF), "m4": _sb(C, BF), "r16": _sb(C, BF), "r4": _sb(C, BF), "r8": _sb(C, BF), "r32": _sb(2 * C, BF),
+    "bigm": _sb(C, BF), "rbig": _sb(C, BF), "rmin": _sb(C + 32, BF),
+    "pi": _sb(8, I32), "pf": _sb(24, F32), "ui": _sb(8, I32), "uo": _sb(8, U16), "ic2h": _sb(C, F16),
+    "km": _sb(C, F32), "kw": _sb(C, F32), "sj": _sb(4 * C, BF), "k2": _sb(2 * C, F16), "k3": _sb(2 * C, F16),
+    "kb": _sb(C, F16), "kc": _sb(C, F16), "kd": _sb(C, BF), "ke": _sb(C, F16), "kf": _sb(C, F16), "kg": _sb(C, F16),
+    "kh": _sb(2 * L, F16), "ki": _sb(2 * L, F16),
+    "cb": _sb(6 * C, BF), "co": _sb(12 * 160, F16), "cd": _sb(168, F16), "junk": _sb(7 * C, BF),
+    "cls": _sb(C, BF), "pm": _sb(C, BF), "xq": _sb(C, F16), "Lr": _sb(C, F32), "La": _sb(C, F32), "O": _sb(C, F32),
+    "val": _sb(C + 32, F16), "tv": _sb(2 * C + 32, F16), "tw": _sb(2 * C + 32, BF),
+    "CS": _sb(C, F32), "tab": _sb(10 * C, BF),
+    "seg": _sb(160, BF), "sgo": _sb(160, F16), "seh": _sb(160, F32), "sho": _sb(160, F32), "sgl": _sb(C, F16), "sgm": _sb(C, F16),
+    "yo": _sb(C, F32), "po": _sb(C, F32),
 }
 for _r in range(R):
     SCRATCH["qc%d" % _r] = _sb(128, Q4)
@@ -49,12 +54,23 @@ for _b in "ABCDEFG":
     SCRATCH["p" + _b] = ("psum", [128, 512], F32)
 SMALL = {}
 _at = 0
-for _n, _w in (("mpar", 32), ("em", 32), ("ef", 32), ("acc", 32), ("es", 1), ("e16", 16), ("bk", 8), ("wk", 8), ("su2", 8), ("df", 8),
-               ("dg", 8), ("jw", 10), ("sig", 20), ("s2", 20), ("s1", 20), ("lw", 6), ("lx", 6)):
-    SMALL[_n] = (_at, _w)
+for _n, _w in (("mpar", 32), ("em", 32), ("ef", 32), ("acc", 6), ("es", 1), ("eq", 1), ("e16", 16), ("bi", 8), ("bk", 8), ("wk", 8),
+               ("mu", 8), ("su2", 8), ("nk", 8), ("dg", 8), ("Pb", 40), ("s2", 20), ("cz", 20), ("base", 20),
+               ("tn", 20), ("zz", 20), ("pr", 20), ("e160", 20), ("ix", 20), ("rs", 20), ("lw", 6), ("lx", 6),
+               ("nj", 40), ("ib", 40), ("sl", 40), ("a1", 20), ("a2", 20), ("os0", 2)):
+    SMALL[_n] = ("sm", _at, _w)
     _at += _w
+SCRATCH["sm"] = _sb(_at, F32)
+_at = 0
+for _n, _w in (("orank", 20), ("oplr", 32), ("osel", 2), ("opt", 20), ("oab", 80), ("oidx", 20), ("olam", 20), ("onp", 20),
+               ("ogp", 40), ("osg", 6), ("ol4", 24), ("olc", 6), ("os4", 80)):
+    SMALL[_n] = ("so", _at, _w)
+    _at += _w
+SCRATCH["so"] = _sb(_at, U16)
+for _at, _n in enumerate(("Gp", "SR", "SC", "WP", "WR", "lp", "pn", "tb", "tc", "win")):
+    SMALL[_n] = ("tab", C * _at, C)
 
-NDMA = 20
+NDMA = 24
 SEMAPHORES = ["cV", "cS", "cT", "cG", "sent"] + ["d%d" % i for i in range(NDMA)] + \
     ["a%s%d" % (k, r) for k in "qsp" for r in range(R)]
 
@@ -64,8 +80,8 @@ ACT = ActivationFunctionType
 
 def vw(name, a=0, b=None, s=1):
     if name in SMALL:
-        o, w = SMALL[name]
-        return ("sm", o + a, o + (w if b is None else b), s)
+        n, o, w = SMALL[name]
+        return (n, o + a, o + (w if b is None else b), s)
     return (name, a, SCRATCH[name][1][1] if b is None else b, s)
 
 
@@ -75,6 +91,72 @@ def col(name, j):
 
 def ind(win, off):
     return ("*", win, off)
+
+
+def size(v):
+    return 16 * size(v[2]) if v[0] == "*" else len(range(v[1], v[2], v[3]))
+
+
+def span(out, *ins, both=False):
+    vs = [v for v in (out,) + ins if isinstance(v, tuple)]
+    if out[0] == "*":
+        return 50 + 2.5 * size(out)
+    if any(v[0] == "*" for v in vs):
+        return 55 + 1.2 * size(out)
+    kinds = [SCRATCH[v[0]] for v in vs if size(v) > 1 or v is out]
+    if both:
+        return max(53, size(out) * (0.83 if any(k[0] == "psum" for k in kinds) else 1.66))
+    return max(53, size(out) * (0.42 if all(k[2] in (BF, F16, U16) for k in kinds) else 0.83))
+
+
+def issue_order(ops):
+    n = len(ops)
+    after = [[] for _ in ops]
+    for i, o in enumerate(ops):
+        for j in o["deps"] | o["order"]:
+            after[j].append(i)
+    gap = lambda j, i: 0.0 if j not in ops[i]["deps"] or ops[i]["eng"] is None else WAKE
+    chain = [0.0] * n
+    for i in range(n - 1, -1, -1):
+        chain[i] = ops[i]["cost"] + ops[i]["lat"] + max([gap(i, k) + chain[k] for k in after[i]], default=0.0)
+    left = [len(o["deps"] | o["order"]) for o in ops]
+    ready, done, free, pool, out = [0.0] * n, [0.0] * n, {}, {}, []
+
+    def place(i, t):
+        out.append((t, len(out), i))
+        done[i] = t + ops[i]["cost"] + ops[i]["lat"]
+        for k in after[i]:
+            ready[k] = max(ready[k], done[i] + gap(i, k) if i in ops[k]["deps"] or ops[k]["eng"] is None else t)
+            left[k] -= 1
+            if not left[k]:
+                offer(k)
+
+    def offer(k):
+        if ops[k]["eng"] is None:
+            place(k, ready[k])
+        else:
+            pool.setdefault(ops[k]["eng"], []).append(k)
+    for i in range(n):
+        if not left[i]:
+            offer(i)
+    while any(pool.values()):
+        best = None
+        for e, c in pool.items():
+            if not c:
+                continue
+            c.sort(key=lambda k: -chain[k])
+            pick, limit = c[0], max(free.get(e, 0.0), ready[c[0]])
+            for k in c[1:]:
+                t = max(free.get(e, 0.0), ready[k])
+                if t + ops[k]["cost"] <= limit + SLACK and t < limit:
+                    pick, limit = k, t
+            if best is None or limit < best[0]:
+                best = (limit, e, pick)
+        t, e, k = best
+        pool[e].remove(k)
+        free[e] = t + ops[k]["cost"]
+        place(k, t)
+    return [ops[i] for _, _, i in sorted(out)]
 
 
 def rank_program(g, core, T, topo):
@@ -103,416 +185,365 @@ def rank_program(g, core, T, topo):
                 out += [v[1], v[2]] if v[0] == "*" else [v]
         return out
 
-    def add(eng, fn, reads, writes, sem=None, val=0, acc=False):
-        ops.append({"eng": eng, "fn": fn, "r": parts(reads), "w": parts(writes), "sem": sem, "val": val, "acc": acc})
+    def add(eng, fn, reads, writes, cost, sem=None, val=0, acc=False, lat=0.0, order=()):
+        ops.append({"eng": eng, "fn": fn, "r": parts(reads), "w": parts(writes), "sem": sem, "val": val, "acc": acc,
+                    "cost": cost, "lat": lat, "order": set(order)})
 
     def scat(out, off, in_):
-        add("V", lambda q: q.tensor_copy(ap(ind(out, off)), ap(in_)), [off, in_], [out])
+        add("V", lambda q: q.tensor_copy(ap(ind(out, off)), ap(in_)), [off, in_], [out], span(ind(out, off)))
+
+    def act(out, in_, func, accum=None, bias=0.0, scale=1.0):
+        cost = span(out, in_) if in_[0] == "*" else 60 + 0.83 * size(out)
+        kw = {} if func == ACT.Copy else {"bias": sc(bias)}
+        if isinstance(scale, tuple) or scale != 1.0:
+            kw["scale"] = sc(scale)
+        if accum is not None:
+            kw["accum_out"] = ap(accum)
+        add("S", lambda q: q.activation(ap(out), ap(in_), func, **kw), [in_, bias, scale], [out, accum], cost)
 
     def cp(e, out, in_, scale=None):
-        if e == "V" and scale is None:
-            add(e, lambda q: q.tensor_copy(ap(out), ap(in_)), [in_], [out])
-        elif e == "V":
-            ts(out, in_, scale, A.mult)
+        if e == "S":
+            act(out, in_, ACT.Copy, None, 0.0, 1.0 if scale is None else scale)
         elif scale is None:
-            add(e, lambda q: q.activation(ap(out), ap(in_), ACT.Copy), [in_], [out])
+            add(e, lambda q: q.tensor_copy(ap(out), ap(in_)), [in_], [out], span(out, in_))
         else:
-            add(e, lambda q: q.activation(ap(out), ap(in_), ACT.Copy, scale=scale), [in_], [out])
+            ts(out, in_, scale, A.mult)
 
-    def plus(out, in_, bias):
-        add("S", lambda q: q.activation(ap(out), ap(in_), ACT.Identity, bias=ap(bias)), [in_, bias], [out])
+    def sign(out, in_, bias, scale, accum=None):
+        act(out, in_, ACT.Sign, accum, bias, scale)
 
     def ts(out, in0, s1, o0, s2=None, o1=None):
         if o1 is None:
-            add("V", lambda q: q.tensor_scalar(ap(out), ap(in0), sc(s1), None, o0), [in0, s1], [out])
+            add("V", lambda q: q.tensor_scalar(ap(out), ap(in0), sc(s1), None, o0), [in0, s1], [out], span(out, in0))
         else:
-            add("V", lambda q: q.tensor_scalar(ap(out), ap(in0), sc(s1), sc(s2), o0, o1), [in0, s1, s2], [out])
+            add("V", lambda q: q.tensor_scalar(ap(out), ap(in0), sc(s1), sc(s2), o0, o1), [in0, s1, s2], [out], span(out, in0))
 
     def tt(out, in0, in1, o):
-        add("V", lambda q: q.tensor_tensor(ap(out), ap(in0), ap(in1), o), [in0, in1], [out])
+        add("V", lambda q: q.tensor_tensor(ap(out), ap(in0), ap(in1), o), [in0, in1], [out], span(out, in0, in1, both=True))
 
-    def scan(out, d0, d1, init, o0):
-        add("V", lambda q: q.tensor_tensor_scan(ap(out), ap(d0), ap(d1), init, o0, A.add), [d0, d1], [out])
-
-    def sign(out, in_, bias, scale, accum=None):
-        if accum is None:
-            add("S", lambda q: q.activation(ap(out), ap(in_), ACT.Sign, bias=sc(bias), scale=scale), [in_, bias], [out])
-        else:
-            add("S", lambda q: q.activation(ap(out), ap(in_), ACT.Sign, bias=sc(bias), scale=scale, accum_out=ap(accum)),
-                [in_, bias], [out, accum])
+    def scan(out, d0, d1, init, o0, o1=A.add):
+        add("V", lambda q: q.tensor_tensor_scan(ap(out), ap(d0), ap(d1), sc(init), o0, o1), [d0, d1, init], [out], span(out, d0, d1))
 
     def fill(out, c):
-        add("V", lambda q: q.memset(ap(out), c), [], [out])
+        add("V", lambda q: q.memset(ap(out), c), [], [out], span(out))
 
     def trans(out, in_):
-        add("V", lambda q: q.transpose(ap(out), ap(in_)), [in_], [out])
+        add("V", lambda q: q.transpose(ap(out), ap(in_)), [in_], [out], span(out, in_))
 
     def quant(qn, sn, a, b, in_):
-        add("V", lambda q: q.quantize_mx(ap(vw(qn, a, b)), ap(vw(sn, a, b)), ap(in_)), [in_], [vw(qn, a, b), vw(sn, a, b)])
+        add("V", lambda q: q.quantize_mx(ap(vw(qn, a, b)), ap(vw(sn, a, b)), ap(in_)), [in_], [vw(qn, a, b), vw(sn, a, b)],
+            12 + 0.22 * size(in_))
 
     def mm(bank, w, x, start=True, stop=True):
         lq, ls, rq, rs = vw(w[0], w[2], w[2] + 128), vw(w[1], w[2], w[2] + 128), vw(x[0], x[2], x[3]), vw(x[1], x[2], x[3])
         out = vw(bank, 0, x[3] - x[2])
-        add("T", lambda q: q.matmul_mx(ap(out), ap(lq), ap(ls), ap(rq), ap(rs), start, stop), [lq, ls, rq, rs], [out], acc=not start)
+        add("T", lambda q: q.matmul_mx(ap(out), ap(lq), ap(ls), ap(rq), ap(rs), start, stop), [lq, ls, rq, rs], [out],
+            0.6 * (size(rq) + 16), acc=not start)
 
     def iota(out, pat, base, cm):
         if SCRATCH[out[0]][2] == I32:
-            add("G", lambda q: q.iota(ap(out), pat, base, cm), [], [out])
+            add("G", lambda q: q.iota(ap(out), pat, base, cm), [], [out], 130 + 1.66 * size(out))
         else:
-            add("G", lambda q: q.iota(ap(out), pat, base, cm, allow_small_or_imprecise_dtypes=True), [], [out])
+            add("G", lambda q: q.iota(ap(out), pat, base, cm, allow_small_or_imprecise_dtypes=True), [], [out], 130 + 1.66 * size(out))
 
     def where(out, pat, op, base, cm):
-        ones = vw("ones", 0, out[2] - out[1])
-        add("G", lambda q: q.affine_select(ap(out), ap(ones), pat, op, 0.0, base, cm), [ones], [out])
+        z = vw("zero", 0, out[2] - out[1])
+        add("G", lambda q: q.affine_select(ap(out), ap(z), pat, op, 1.0, base, cm), [z], [out], 170 + 1.66 * size(out))
 
-    def dma(e, fo, fi, reads, writes):
+    def dma(e, fo, fi, reads, writes, adding=False):
         s = "d%d" % ndma[0]
         ndma[0] += 1
-        add(e, lambda q: q.dma_start(fo(), fi()), reads, writes, sem=s, val=16)
+        if adding:
+            add(e, lambda q: q.dma_start(fo(), fi(), accum_op=A.add), reads, writes, 600, sem=s, val=16, lat=LOCAL)
+        else:
+            add(e, lambda q: q.dma_start(fo(), fi()), reads, writes, 60, sem=s, val=16, lat=LOCAL)
 
     rid, pid, _ = topo.addr(nxt)
     nout, nin = len(topo.engines(core, nxt)), len(topo.engines(prv, core))
     nsent = [0]
+    sent_at = {}
 
     def send(dst, src, sem, cast=None):
         nsent[0] += nout
+        sent_at[sem] = len(ops)
         add("G", lambda q: q.remote_dma(ap(dst, cast), ap(src, cast), T.sem[sem], T.sem.sent, pid, rid, topo.mask(core, nxt)),
-            [src], [], sem="-")
+            [src], [], 400, sem="-", lat=REMOTE)
 
     def arrive(dst, sem):
-        add(None, None, [], [dst], sem=sem, val=nin)
+        add(None, None, [], [dst], 0.0, sem=sem, val=nin, order=[sent_at[sem]])
 
     def wrap(out, masked, b, seg, a=0):
         scan(vw(out, a, b), vw("r%d" % seg, a, b), vw(masked, a, b), 0.0, A.mult)
-
-    def pick(a, b):
-        o, s, off = vw("qur", 16 * a, 16 * b), vw("sur", 16 * a, 16 * b), vw("uo", a, b)
-        add("V", lambda q: q.tensor_copy(ap(o, dt.uint32), ap(ind(vw("qu"), off), dt.uint32)), [vw("qu"), off], [o])
-        cp("S", s, ind(vw("su"), off))
 
     dma("S", lambda: T.ut[:], lambda: T.u[:], [], [vw("ut")])
     dma("Y", lambda: T.x0[:], lambda: T.x[:], [], [vw("x0")])
     dma("Y", lambda: ap(vw("qw"), dt.uint8), lambda: T.wc[:], [], [vw("qw")])
     dma("Y", lambda: T.sw[:], lambda: T.ws[:], [], [vw("sw")])
-    dma("Y", lambda: T.vt[:], lambda: T.v[:], [], [vw("vt")])
+    dma("G", lambda: T.vt[:], lambda: T.v[:], [], [vw("vt")])
+    fill(vw("zero"), 0.0)
     iota(col("pi", 0), [[0, 1]], 0, 1)
-    iota(vw("ui", 0, 8), [[16, 8]], 0, 0)
-    iota(vw("ui", 8, 24), [[16, 2], [32, 4], [0, 2]], 0, 0)
-    iota(vw("a0i"), [[1, 8], [0, 16], [50, 4]], 0, 0)
-    iota(vw("ic"), [[1, C]], 0, 0)
-    iota(vw("a1i"), [[1, 8], [0, 32], [-1, 2]], 0, 0)
-    iota(vw("seg"), [[0, 160]], 0, 0)
-    iota(vw("seh"), [[0, C]], 0, 0)
+    iota(vw("ui"), [[16, 8]], 0, 0)
     iota(vw("i16"), [[0, 20], [1, 16]], 0, 0)
-    iota(vw("ones"), [[0, 512]], 1, 0)
-    for n, w, k in (("r8", 160, 8), ("r16", C, 16), ("r4", C, 4)):
-        where(vw(n), [[0, w // k], [1, k]], A.not_equal, 0, 0)
-    iota(vw("icb"), [[1, C + L]], -240, 0)
-    iota(vw("Gp", 0, C), [[0, C]], 0, 0)
-    iota(vw("O"), [[0, C]], 0, 0)
-    iota(vw("ic2"), [[0, 2], [1, C]], -160, 0)
+    iota(vw("ai"), [[1, 8], [0, 64]], 0, 0)
+    iota(vw("sg0", 0, 20), [[16, 20]], 0, 0)
+    iota(vw("sg0", 20, 52), [[1, 2], [0, 16]], 0, 0)
+    iota(vw("ic2"), [[2, C]], 2, 0)
+    where(vw("r8"), [[0, 40], [1, 8]], A.is_equal, 0, 0)
+    where(vw("r32"), [[0, 20], [1, 32]], A.is_equal, 0, 0)
+    for k in range(5):
+        a, b = 4 * (TILE0[k] + 16 * TILES[k][3]), 4 * TILE0[k + 1]
+        iota(vw("bits", a, b), [[0, b - a]], 0, 0)
+    iota(vw("Lr"), [[0, C]], 0, 0)
     iota(vw("i4"), [[0, 80], [1, 4]], 0, 0)
-    iota(vw("t320"), [[320, 16]], 320, 0)
-    iota(vw("zero"), [[0, 512]], 0, 0)
+    iota(vw("icb"), [[1, C + L]], -208, 0)
+    where(vw("r4"), [[0, 80], [1, 4]], A.is_equal, 0, 0)
+    iota(vw("O"), [[0, C]], 0, 0)
+    iota(vw("t16"), [[1, 16]], 0, 0)
     iota(vw("cmp", 4 * L, 512), [[0, 512 - 4 * L]], 0, 0)
     for b in range(4):
-        where(vw("et", 512 * b, 512 * b + 512), [[1, 512]], A.is_equal, -b, -4)
+        where(vw("et", 512 * b, 512 * b + 512), [[1, 512]], A.not_equal, -b, -4)
     fill(vw("pb"), 0.0)
-    for j, m in ((1, 15), (2, 3), (3, 7)):
+    for j, m in ((1, 15), (2, 3), (3, 7), (5, 1)):
         ts(col("pi", j), col("pi", 0), m, A.bitwise_and)
     ts(col("pi", 4), col("pi", 0), 4, A.arith_shift_right)
-    ts(col("pi", 5), col("pi", 0), 5, A.arith_shift_right)
     ts(col("pi", 6), col("pi", 0), 15, A.bitwise_and, 2, A.arith_shift_right)
     ts(col("pi", 7), col("pi", 0), 4, A.arith_shift_right, 1, A.bitwise_and)
     cp("V", vw("uo"), vw("ui"))
+    lin = lambda out, in_, scale, bias: act(out, in_, ACT.Identity, None, bias, scale)
+    sig = vw("Pb", 0, 20)
+    cp("S", vw("seg"), vw("zero", 0, 160))
+    cp("S", vw("seh"), vw("zero", 0, 160))
+    sign(vw("r16"), vw("i16"), 0.0, 1.0)
     cp("V", vw("pf", 0, 8), vw("pi"))
-    fill(col("pf", 16), 160.0)
+    fill(col("rs", 0), 0.0)
     ts(col("pf", 11), col("pf", 1), 2.0, A.subtract)
-    ts(col("pf", 9), col("pf", 2), 640.0, A.add)
+    ts(col("pf", 9), col("pf", 2), -4.0, A.add)
+    ts(col("pf", 10), col("pf", 3), -1.0, A.mult, 0.5, A.add)
     tt(col("pf", 12), col("pf", 11), col("pf", 11), A.mult)
-    ts(col("pf", 8), col("pf", 5), 2.0, A.mult)
+    ts(vw("m16"), vw("i16"), col("pf", 1), A.is_equal)
+    ts(col("pf", 8), col("pf", 1), -1.0, A.add)
+    ts(col("pf", 17), col("pf", 2), 4.0 * 208, A.add)
     ts(col("pf", 13), col("pf", 12), 1.5, A.is_gt, 20.0, A.mult)
-    ts(col("pf", 10), col("pf", 3), -320.0, A.mult, -160.0, A.add)
+    ts(col("pf", 15), col("pf", 5), col("pf", 7), A.not_equal, 21.0, A.mult)
+    ts(col("pf", 16), col("pf", 1), -1.0, A.mult, 15.0, A.add)
     tt(col("pf", 14), col("pf", 13), col("pf", 4), A.add)
-    ts(col("pf", 17), col("pf", 2), 960.0, A.add)
+    lin(vw("bigm"), vw("m16"), BIG, -BIG)
+    lin(vw("rbig"), vw("r16"), 2 * BIG, -BIG)
+    lin(vw("rmin", 0, C), vw("r16"), 1185.0, -161.0)
+    lin(vw("rmin", C, C + 32), vw("r16", 0, 32), 1185.0, -161.0)
+    cp("V", vw("sgl"), vw("zero", 0, C))
+    cp("V", vw("val"), vw("zero", 0, C + 32))
+    cp("V", vw("cd", 0, 8), vw("zero", 0, 8))
+    cp("V", vw("k2", 1, 2 * C, 2), vw("zero", 0, C))
     quant("qu", "su", 0, 128, vw("ut"))
-    quant("qx", "sx", 0, C, vw("x0"))
-    pick(0, 8)
-    pick(16, 24)
-    pick(8, 16)
+    add("V", lambda q: q.tensor_copy(ap(vw("qur"), dt.uint32), ap(ind(vw("qu"), vw("uo")), dt.uint32)), [vw("qu"), vw("uo")], [vw("qur")], 210)
+    cp("S", vw("sur"), ind(vw("su"), vw("uo")))
+    lin(sig, vw("sg0", 0, 20), 1.0, col("pf", 1))
+    lin(vw("base"), vw("sg0", 0, 20), 1.0, col("pf", 16))
+    lin(vw("s2"), sig, -1.0, 640.0)
+    lin(vw("seh", 7, 160, 8), sig, -1.0, 319.0)
+    lin(vw("cz"), sig, -0.5, 319.25)
+    cp("S", vw("seg", 7, 80, 8), vw("Pb", 0, 10))
+    cp("S", vw("seg", 87, 160, 8), vw("Pb", 0, 10))
+    lin(vw("lw"), vw("Pb", 0, 6), 1.0, -160.0)
+    lin(vw("lx"), vw("Pb", 0, 6), 1.0, -159.5)
+    ts(vw("at", 512, 1024), vw("ai"), col("pf", 14), A.is_equal)
+    quant("qa", "sa", 128, 256, vw("at", 512, 1024))
+    ts(vw("at", 0, 512), vw("ai"), col("pf", 4), A.is_equal)
+    quant("qa", "sa", 0, 128, vw("at", 0, 512))
+    ts(vw("mpar"), vw("sg0", 20, 52), col("pf", 7), A.is_equal)
+    ts(vw("sgl", 7, 160, 8), sig, -0.5, A.mult, -0.25, A.add)
+    ts(vw("os0"), vw("Pb", 0, 2), col("pf", 15), A.add, 41.0, A.min)
+    ts(vw("osel"), vw("os0"), 16.0, A.mult, 15.0, A.add)
+    ts(vw("pf", 18, 22), vw("i4", 0, 4), col("pf", 6), A.is_equal)
+    ts(vw("m4"), vw("i4"), col("pf", 6), A.is_equal)
+    cp("V", vw("ic2h"), vw("ic2"))
+    quant("q0", "s0", 0, 128, vw("zero", 0, 512))
+    for r in range(R):
+        dma("Y", lambda r=r: ap(vw("lq%d" % r, L, 128), dt.uint8), lambda: ap(vw("q0", 0, 128 - L), dt.uint8),
+            [vw("q0")], [vw("lq%d" % r, L, 128)])
+        dma("Y", lambda r=r: ap(vw("ls%d" % r, L, 128)), lambda: ap(vw("s0", 0, 128 - L)), [vw("s0")], [vw("ls%d" % r, L, 128)])
+    quant("qe", "se", 0, 512, vw("et"))
+    quant("qv", "sv", 0, 128, vw("vt"))
 
-    def consts_0():
-        ts(vw("at", 512, 1024), vw("a0i"), col("pf", 14), A.is_equal, 320.0, A.mult)
-        quant("qa", "sa", 128, 256, vw("at", 512, 1024))
-
-    def consts_a():
-        ts(vw("at", 0, 512), vw("a1i"), col("pf", 8), A.is_equal, -0.25, A.mult)
-        quant("qa", "sa", 0, 128, vw("at", 0, 512))
-
-    def consts_b():
-        ts(vw("em"), vw("ic", 0, 32), 15.5, A.is_gt)
-        ts(vw("sig"), vw("ic", 0, 20), 16.0, A.mult, col("pf", 1), A.add)
-        ts(vw("m16"), vw("i16"), col("pf", 1), A.is_equal)
-        ts(vw("mpar"), vw("em"), col("pf", 7), A.is_equal)
-        cp("V", vw("jw"), vw("sig", 0, 10))
-        cp("V", vw("seg", 7, 80, 8), vw("sig", 0, 10))
-        cp("V", vw("seg", 87, 160, 8), vw("sig", 0, 10))
-        ts(vw("s2"), vw("sig"), -2.0, A.mult, 640.0, A.add)
-        ts(vw("s1"), vw("sig"), -1.0, A.mult, 320.0, A.add)
-        ts(vw("seh", 15, C, 16), vw("sig"), -2.0, A.mult, 2.0 * 639, A.add)
-
-    def consts_e():
-        ts(vw("m4"), vw("i4"), col("pf", 6), A.is_equal)
-
-    def consts_f():
-        ts(vw("lw"), vw("sig", 0, 6), -160.0, A.add)
-        ts(vw("lx"), vw("sig", 0, 6), -159.5, A.add)
-
-    def consts_c():
-        quant("q0", "s0", 0, 128, vw("zero"))
-        for r in range(R):
-            dma("Y", lambda r=r: ap(vw("lq%d" % r, L, 128), dt.uint8), lambda: ap(vw("q0", 0, 128 - L), dt.uint8),
-                [vw("q0")], [vw("lq%d" % r, L, 128)])
-            dma("Y", lambda r=r: ap(vw("ls%d" % r, L, 128)), lambda: ap(vw("s0", 0, 128 - L)), [vw("s0")], [vw("ls%d" % r, L, 128)])
-
-    def statics(r):
+    def from_points(r):
         top = 3 + r
-        st = []
-        st.append(lambda: ts(vw("em"), vw("mpar"), col("es", 0), A.mult))
-        st.append(lambda: trans(vw("ef"), vw("em")))
-        st.append(lambda: tt(vw("e16"), vw("ef", 0, 16), vw("ef", 16, 32), A.add))
+        e0, e1, b0, b1 = vw("e16", 0, 7), vw("e16", 1, 8), vw("bk", 0, 7), vw("bk", 1, 8)
+        ts(vw("pm"), vw("cls"), col("pf", 8), A.is_equal, 0.5, A.subtract)
+        scan(vw("xq"), vw("ic2h"), vw("pm"), 0.0, A.max, A.mult)
+        sign(vw("junk", 6 * C, 7 * C), vw("cls"), col("pf", 10), 1.0, col("es", 0))
+        ts(vw("eq"), vw("es"), 0.5, A.mult, 160.0, A.add)
+        ts(vw("em"), vw("mpar"), col("eq", 0), A.mult)
+        trans(vw("ef"), vw("em"))
+        tt(vw("e16"), vw("ef", 0, 16), vw("ef", 16, 32), A.add)
+        ts(vw("bi"), vw("e16", 0, 8), -0.5, A.add, 1.5 * 2 ** 24, A.add)
+        tt(vw("nk", 0, 7), e0, e1, A.subtract)
+        tt(vw("su2", 0, 7), e0, e1, A.add)
+        ts(vw("bk"), vw("bi"), 1.5 * 2 ** 24, A.subtract, 0.5, A.mult)
+        ts(vw("dg", 0, 7), vw("nk", 0, 7), 1024.0, A.add)
+        tt(vw("wk", 0, 7), b0, b1, A.subtract)
+        tt(vw("mu", 0, 7), b0, b1, A.add)
+        for k in range(top + 1):
+            ts(vw("seg", 80 + k, 160, 8), vw("Pb", 0, 10), col("bk", k + 1), A.is_ge, col("wk", k), A.mult)
+            if k:
+                ts(vw("seg", k, 80, 8), vw("Pb", 0, 10), col("bk", k), A.is_ge, col("wk", k), A.mult)
+        wrap("sgo", "seg", 160, 8)
+        cp("V", vw("opt"), vw("sgo", 7, 160, 8))
+        for k in range(top):
+            ts(vw("seh", k, 160, 8), vw("s2"), col("su2", k), A.is_le, col("dg", k), A.mult)
+        wrap("sho", "seh", 160, 8)
+        ts(vw("tn"), vw("sho", 7, 160, 8), 1.5 * 2 ** 33, A.add, 1.5 * 2 ** 33, A.subtract)
+        tt(vw("Pb", 20, 40), vw("sho", 7, 160, 8), vw("tn"), A.subtract)
+        ts(vw("onp"), vw("tn"), 1.0 / 1024, A.mult)
+        cp("V", vw("oidx"), vw("Pb", 20, 40))
+        ts(vw("sgl", 167, C, 8), vw("Pb", 20, 40), -0.5, A.mult, -0.25, A.add)
+        for k in range(top + 1):
+            ts(vw("sgl", k, C, 8), vw("Pb"), col("mu", k), A.is_ge, col("wk", k), A.mult)
+        wrap("sgm", "sgl", C, 8)
+        y = vw("sgm", 7, C, 8)
+        tt(vw("zz"), vw("Pb", 20, 40), vw("cz"), A.subtract)
+        tt(vw("nj"), y, vw("sgl", 7, C, 8), A.add)
+        ts(vw("ib"), y, 0.0, A.is_gt, 160.0, A.mult)
+        tt(vw("pr"), vw("zz"), vw("sgm", 167, C, 8), A.mult)
+        tt(vw("sl"), vw("ib"), vw("nj"), A.subtract)
+        ts(vw("e160"), vw("pr"), 0.0, A.is_gt, 160.0, A.mult)
+        ts(vw("ogp"), vw("sl"), -0.5, A.add)
+        tt(vw("ix"), vw("e160"), vw("nj", 20, 40), A.subtract)
+        ts(vw("olam"), vw("ix"), -0.5, A.add)
+        cp("S", vw("Gp"), ind(vw("icb"), vw("ogp", 0, 20)))
+        cp("S", vw("lp"), ind(vw("icb"), vw("ogp", 20, 40)))
+        cp("S", vw("pn"), ind(vw("t16"), vw("onp")))
 
-        def s1():
-            ts(vw("ei", 0, 8), vw("e16", 0, 8), 320.0, A.add)
-            tt(vw("su2", 0, 7), vw("e16", 0, 7), vw("e16", 1, 8), A.add)
-            tt(vw("df", 0, 7), vw("e16", 0, 7), vw("e16", 1, 8), A.subtract)
-            ts(vw("ei", 8, 16), vw("ei", 0, 8), 2, A.arith_shift_right)
+    def lane(m, a, b, s=1):
+        k = [m in x for x in TILES].index(True)
+        o = 4 * TILE0[k] + TILES[k].index(m)
+        return vw("bits", o + 4 * a, o + 4 * (b - 1) + 1, 4 * s)
 
-        def s2():
-            ts(vw("dg", 0, 7), vw("df", 0, 7), 2048.0 - 640.0, A.add)
-            cp("V", vw("bk"), vw("ei", 8, 16))
-            for k in range(top):
-                ts(vw("seh", 8 + k, C, 16), vw("s1"), col("e16", k + 1), A.is_le, 16384.0 + 640.0, A.mult)
-            tt(vw("wk", 0, 7), vw("bk", 0, 7), vw("bk", 1, 8), A.subtract)
-            for k in range(top + 1):
-                ts(vw("seh", k, C, 16), vw("s2"), col("su2", k), A.is_le, col("dg", k), A.mult)
-
-        def s3():
-            for k in range(top + 1):
-                if k:
-                    ts(vw("seg", k, 80, 8), vw("jw"), col("bk", k), A.is_ge, col("wk", k), A.mult)
-                ts(vw("seg", 80 + k, 160, 8), vw("jw"), col("bk", k + 1), A.is_ge, col("wk", k), A.mult)
-
-        def s4():
-            wrap("sgo", "seg", 160, 8)
-            wrap("sho", "seh", C, 16)
-
-        def s5():
-            cp("V", vw("opt"), vw("sgo", 7, 160, 8))
-            cp("V", vw("wi", 0, 20), vw("sho", 15, C, 16))
-
-        def s6():
-            ts(vw("wi", 20, 40), vw("wi", 0, 20), 2047, A.bitwise_and)
-            ts(vw("wi", 40, 60), vw("wi", 0, 20), 11, A.arith_shift_right, 7, A.bitwise_and)
-            ts(vw("wi", 60, 80), vw("wi", 0, 20), 14, A.arith_shift_right)
-
-        def s7():
-            ts(vw("oidx"), vw("wi", 20, 40), 0.5, A.mult)
-            cp("V", vw("onp"), vw("wi", 40, 80))
-        return st + [s1, s2, s3, s4, s5, s6, s7]
-
-    def s_rows(keys, a, b, own):
-        for m in range(a, b):
-            sign(vw("junk", C * (m % 2), C * (m % 2) + C), keys, own(m), -1.0, col("acc", m))
-
-    def v_row(keys, m, own, op):
-        ts(vw("cb", C * (m % 3), C * (m % 3) + C), keys, own(m), op)
-
-    def v_sum(m):
-        k = C * (m % 3)
-        scan(vw("co", 160 * m, 160 * m + 160), vw("cb", k, k + 160), vw("cb", k + 160, k + C), -160.0, A.add)
-
-    def counts(out, nv, rows, s_mul, s_add):
-        ts(vw(out, 0, nv), vw("co", 159, 160 * nv, 160), 160.0, A.add)
-        ts(vw(out, nv, rows), vw("acc", nv, rows), s_mul, A.mult, s_add, A.add)
-
-    def new_points(r):
-        tt(vw("win", C, C + L), vw("pa%d" % r), vw("old"), A.subtract)
-        tt(vw("kst"), ind(vw("win", 0, C + L), vw("os16")), vw("kst"), A.add)
-
-    U16R, U32A, U32B = ("qur", "sur", 0), ("qur", "sur", 128), ("qur", "sur", 256)
+    own = lambda m: col("kw", 16 * m + 15)
+    U16R = ("qur", "sur", 0)
     QX = ("qx", "sx", 0, C)
     for r in range(R):
         xs = "x0" if r == 0 else "X"
+        ns = NS[r]
+        quant("qx", "sx", 0, C, vw(xs))
+        mm("pA", U16R, QX)
+        mm("pB", U16R, QX)
         if r == 0:
             mm("pF", ("qu", "su", 0), QX)
-        else:
-            quant("qx", "sx", 0, C, vw(xs))
-        mm("pA", U16R, QX)
-        mm("pD", U32B, QX)
-        mm("pB", U32A, QX)
-        mm("pC", U32A, QX)
-        side = statics(r)
-        if r == 0:
             ts(vw("pb", 0, 4 * C, 4), vw("pF", 0, C), 0.0, A.is_gt)
-            trans(vw("tr"), vw("pA", 0, C))
             quant("qp", "sp", 0, C, vw("pb"))
-            consts_0()
             mm("pG", ("qa", "sa", 128), ("qp", "sp", 0, C))
-            ts(vw("fr0"), vw("ic"), -1.0 / 2048, A.mult, 320 + 511.0 / 2048, A.add)
-            consts_a()
-            tt(vw("kst"), vw("pG", 0, C), vw("fr0"), A.add)
-            consts_b()
-        else:
-            cp("S", vw("Xh", 0, XH), vw(xs, 0, XH), 0.5)
-            trans(vw("tr"), vw("pA", 0, C))
-        rows_v = [(b // 2, 2 * (b % 2)) for b in range(NV1[r])]
-        order = [4, 3, 2, 1, 0]
-        rows_s = [(tl, t) for tl in order for t in (1, 3, 0, 2) if (tl, t) not in rows_v]
-        rows_v = [(tl, t) for tl in order for t in range(4) if (tl, t) in rows_v]
-        for i, (tl, t) in enumerate(rows_s):
-            if r == 0 and i == 5:
-                sign(vw("junk", 0, C), vw("kst"), col("pf", 10), 1.0, col("es", 0))
-            sign(vw("bits", 4 * C * tl + t, 4 * C * (tl + 1), 4), vw("pD" if t % 2 else "pC", 0, C),
-                 col("tr", 32 * (2 * tl + t // 2) + 16 * (t % 2)), -1.0)
-
-        def row(tl, t):
-            ts(vw("bits", 4 * C * tl + t, 4 * C * (tl + 1), 4), vw("pB", 0, C), col("tr", 32 * (2 * tl + t // 2)), A.is_lt, 2.0, A.mult)
-
-        def tile(k):
-            quant("qb", "sb", C * k, C * k + C, vw("bits", 4 * C * k, 4 * C * k + 4 * C))
-            mm("pE", ("qa", "sa", 0), ("qb", "sb", C * k, C * k + C), k == order[0], k == order[-1])
-        rv = [lambda x=x: row(*x) for x in rows_v]
-        tl_ = [lambda k=k: tile(k) for k in order]
-        for ch in PAT1:
-            lst = {"r": rv, "s": side, "T": tl_}[ch]
-            if lst:
-                lst.pop(0)()
-        xa = 0 if r == 0 else XH
-        cp("S", vw("Xh", xa, min(xa + 640, 4 * C)), vw(xs, xa, min(xa + 640, 4 * C)), 0.5)
-        side.pop(0)()
-        h = 16 * NV2
-        tt(vw("K"), vw("pE", 0, C), vw("kst"), A.add)
-        side.pop(0)()
-        tt(vw("km", h, C), vw("K", h, C), vw("m16", h, C), A.mult)
-        wrap("kw", "km", C, 16, h)
-        tt(vw("km", 0, h), vw("K", 0, h), vw("m16", 0, h), A.mult)
-        wrap("kw", "km", h, 16)
-        own = lambda m: col("kw", 16 * m + 15)
-        s_rows(vw("K"), NV2, 20, own)
-        scat(vw("Gp", 0, C), vw("opt"), vw("icb", 0, C))
-        for m in range(NV2 + 1):
-            if m < NV2:
-                v_row(vw("K"), m, own, A.is_gt)
-            if m:
-                v_sum(m - 1)
-            if side:
-                side.pop(0)()
-        if r == 0:
-            consts_e()
-        counts("oplace", NV2, 20, -0.5, 159.5)
-        scat(vw("O"), vw("oplace"), vw("ic2", 0, C))
-        if r == 0:
-            cp("S", vw("Xh", 640, 4 * C), vw(xs, 640, 4 * C), 0.5)
-        plus(vw("Gp", C, 2 * C), vw("Gp", 0, C), col("pf", 16))
-        cp("S", vw("p3", 0, C), vw("Gp", 0, C))
-        cp("S", vw("p3", C, 2 * C), vw("Gp", 0, C))
-        if r:
-            cp("S", vw("lp"), ind(vw("p3"), vw("oidx")))
+            cp("V", vw("cls"), vw("pG", 0, C))
+        from_points(r)
+        for a in (0, 640):
+            cp("S", vw("Xh", a, a + 640), vw(xs, a, a + 640), 0.5)
+        h = 16 * (ns - KW)
+        for a, b in ((h, C), (0, h)):
+            tt(vw("km", a, b), vw("pA", a, b), vw("bigm", a, b), A.add)
+            scan(vw("kw", a, b), vw("rbig", a, b), vw("km", a, b), 0.0, A.min, A.max)
+        for m in range(ns, 0, -1):
+            j = vw("sj", C * (m % 4), C * (m % 4) + 16 * m)
+            sign(j, vw("pB", 0, 16 * m), own(m), -1.0)
+            act(lane(m, 0, 16 * m), j, ACT.Relu, col("rs", m))
+        tt(lane(20, 0, C), vw("pA", 0, C), vw("kw"), A.is_le)
+        scan(vw("cd", 8, 168), lane(20, 0, C, 2), lane(20, 1, C, 2), 0.0, A.add)
+        for m in range(19, ns, -1):
+            e = 160 * (m - ns)
+            ts(lane(m, 0, 16 * m), vw("pA", 0, 16 * m), own(m), A.is_lt)
+            scan(vw("co", e - 8 * m, e), lane(m, 0, 8 * m), lane(m, 8 * m, 16 * m), 0.0, A.add)
+        cp("V", vw("rs", ns + 1, 20), vw("co", 159, 160 * (19 - ns), 160))
+        tt(vw("a1"), vw("cd", 7, 160, 8), vw("cd", 15, 168, 8), A.subtract)
+        tt(vw("a2"), vw("a1"), vw("base"), A.add)
+        tt(vw("k2", 1, 2 * C, 32), vw("a2"), vw("rs"), A.subtract)
+        for k in range(5):
+            quant("qb", "sb", TILE0[k], TILE0[k + 1], vw("bits", 4 * TILE0[k], 4 * TILE0[k + 1]))
+            mm("pE", ("qa", "sa", 0), ("qb", "sb", TILE0[k], TILE0[k + 1]), k == 0, k == 4)
+        tt(vw("k2", 0, 2 * C, 2), vw("pE", 0, C), vw("m16"), A.mult)
+        wrap("k3", "k2", 2 * C, 32)
+        cp("V", vw("orank"), vw("k3", 31, 2 * C, 32))
+        scat(vw("Lr"), vw("orank"), vw("xq"))
+        act(vw("La"), vw("Lr"), ACT.Abs)
+        ts(vw("kb"), vw("Lr"), 0.0, A.is_gt)
+        scan(vw("kc"), vw("kb"), vw("zero", 0, C), col("eq", 0), A.add)
+        scan(vw("val", 16, 16 + C), vw("kc"), vw("kb"), 0.0, A.max, A.mult)
+        trans(vw("tv", C, 2 * C + 32), vw("val"))
+        trans(vw("tv", 0, C), vw("val", 16, 16 + C))
+        scan(vw("tw", C, 2 * C + 32), vw("rmin"), vw("tv", C, 2 * C + 32), 0.0, A.min)
+        scan(vw("tw", 0, C), vw("rmin", 0, C), vw("tv", 0, C), 0.0, A.min)
+        ts(vw("oplr"), ind(vw("tw"), vw("osel")), 160.0, A.add)
+        scat(vw("O"), vw("oplr", 0, 20), vw("La"))
+        cp("S", vw("SR"), ind(vw("Gp"), vw("oplr", 0, 20)))
+        cp("S", vw("SC"), ind(vw("SR"), vw("orank")))
+        cp("S", vw("CS"), ind(vw("O"), vw("oidx")))
         for k in range(2):
-            tt(vw("kb", 160 * k, 160 * k + 160), ind(vw("O"), vw("opt", 10 * k, 10 * k + 10)), vw("m4", 0, 160), A.mult)
-        for k in range(2):
-            wrap("kc", "kb", 160 * k + 160, 4, 160 * k)
-        for k in range(2):
-            ts(vw("oab", 40 * k, 40 * k + 40), vw("kc", 160 * k + 3, 160 * k + 160, 4), 4.0, A.mult, col("pf", 9), A.add)
-        cuts = list(zip(ZCUT, ZCUT[1:]))
-        for a, b in cuts[1:]:
-            cp("S", vw("ah", 16 * a, 16 * b), ind(vw("Xh"), vw("oab", a, b)))
-        cp("V", vw("ah", 0, 16 * ZCUT[1]), ind(vw("Xh"), vw("oab", 0, ZCUT[1])))
-        for a, b in cuts:
+            tt(vw("ke", 160 * k, 160 * k + 160), ind(vw("O"), vw("opt", 10 * k, 10 * k + 10)), vw("m4", 0, 160), A.mult)
+            wrap("kf", "ke", 160 * k + 160, 4, 160 * k)
+            ts(vw("oab", 40 * k, 40 * k + 40), vw("kf", 160 * k + 3, 160 * k + 160, 4), 4.0, A.mult, col("pf", 9), A.add)
+        for i, (a, b) in enumerate(zip(ZCUT, ZCUT[1:])):
+            cp("V" if i < ZV else "S", vw("ah", 16 * a, 16 * b), ind(vw("Xh"), vw("oab", a, b)))
             tt(vw("Z", 16 * a, 16 * b), ind(vw("Xh"), vw("oab", 40 + a, 40 + b)), vw("ah", 16 * a, 16 * b), A.add)
         quant("qz", "sz", 0, 160, vw("Z"))
-        if r == 0:
-            cp("S", vw("lp"), ind(vw("p3"), vw("oidx")))
-        cp("S", vw("pn"), ind(vw("t320"), vw("onp", 0, 20)))
+        cp("S", vw("Y", 640, 1280), ind(vw(xs), vw("oab", 40, 80)))
+        cp("V", vw("Y", 0, 640), vw("ah"), 2.0)
         for b in range(4):
             mm("p" + "ABCD"[b], ("qw", "sw", 128 * b), ("qz", "sz", 0, 160))
-        tt(vw("kb"), ind(vw("Gp"), vw("oidx")), vw("m16"), A.mult)
-        if r == 0:
-            consts_f()
-        for b in range(4):
-            cp("SV"[b // 2], vw("H", b, 640, 4), vw("p" + "ABCD"[b], 0, 160), 0.03125)
-        quant("qh", "sh", 0, 160, vw("H"))
+            cp("VS"[b % 2], vw("H", b, 640, 4), vw("p" + "ABCD"[b], 0, 160), 0.03125)
+        quant("qh", "sh", 0, 160, vw("H", 0, 640))
         mm("pE", U16R, ("qh", "sh", 0, 160))
-        mm("pF", U16R, ("qh", "sh", 0, 160))
-        cp("S", vw("pc"), ind(vw("t320"), vw("onp", 20, 40)))
-        wrap("kc", "kb", C, 16)
-        ts(vw("olam"), vw("kc", 15, C, 16), 240.0, A.add)
-        ts(vw("win", 0, 160), vw("pE", 0, 160), 0.0, A.is_gt, 320.0, A.mult)
-        ts(vw("win", 160, C), vw("pE", 0, 160), 0.0, A.is_le, 320.0, A.mult)
-        add("S", lambda q: q.activation(ap(vw("win", C, 480)), ap(vw("pF", 0, 160)), ACT.Relu), [vw("pF", 0, 160)], [vw("win", C, 480)])
-        sign(vw("tb", 160, C), ind(vw("win"), vw("olam", 10, 20)), 0.0, 1.0)
-        ts(vw("tb", 0, 160), ind(vw("win"), vw("olam", 0, 10)), 0.0, A.is_gt)
+        cp("S", vw("H", 640, 960), vw("H", 0, 320), -1.0)
+        cp("V", vw("H", 960, 1280), vw("H", 320, 640), -1.0)
+        for a in (0, 640):
+            dma("G", lambda a=a: ap(vw("Y", a, a + 640)), lambda a=a: ap(vw("H", a, a + 640)),
+                [vw("H", a, a + 640), vw("Y", a, a + 640)], [vw("Y", a, a + 640)], True)
+        ts(vw("win", 0, 160), vw("pE", 0, 160), 0.0, A.is_gt)
+        ts(vw("win", 160, C), vw("pE", 0, 160), 0.0, A.is_le)
+        cp("S", vw("tb", 160, C), ind(vw("win"), vw("olam", 10, 20)))
+        cp("V", vw("tb", 0, 160), ind(vw("win"), vw("olam", 0, 10)))
         scan(vw("tc"), vw("tb"), vw("zero", 0, C), -160.0, A.add)
-        s_rows(vw("tc"), 2, 6, lambda m: col("lx", m))
-
-        def y_piece(a, b):
-            k = 0 if a < 40 else 640
-            tt(vw("Y", 16 * a, 16 * b), ind(vw(xs), vw("oab", a, b)), vw("H", 16 * a - k, 16 * b - k), A.subtract if k else A.add)
-        y_piece(0, 10)
-        for m in range(2):
-            v_row(vw("tc"), m, lambda m: col("lw", m), A.is_le)
-        for m in range(2):
-            v_sum(m)
-        y_piece(10, 40)
-        y_piece(40, 52)
-        counts("osg", 2, 6, 0.5, 160.0)
-        y_piece(52, 62)
-        tt(vw("kb", 0, L), ind(vw("lp"), vw("osg")), vw("m4", 0, L), A.mult)
+        lo, hi = 16 * NVL, 186 + 24 * 5
+        for m in range(NVL, 6):
+            sign(vw("junk", C * m, C * m + hi - lo), vw("tc", lo, hi), col("lx", m), -1.0, col("acc", m))
+        for m in range(NVL):
+            k, n2 = C * m, 93 + 4 * m
+            ts(vw("cb", k, k + 2 * n2), vw("tc", 16 * m, 186 + 24 * m), col("lw", m), A.is_le)
+            scan(vw("co", 160 * (m + 1) - n2, 160 * (m + 1)), vw("cb", k, k + n2), vw("cb", k + n2, k + 2 * n2), 16.0 * m, A.add)
+        if NVL:
+            cp("V", vw("osg", 0, NVL), vw("co", 159, 160 * NVL, 160))
+        if NVL < 6:
+            ts(vw("osg", NVL, 6), vw("acc", NVL, 6), 0.5, A.mult, (lo + hi) / 2, A.add)
+        tt(vw("kh", 0, L), ind(vw("lp"), vw("osg")), vw("m4", 0, L), A.mult)
         cp("S", vw("ps%d" % r), ind(vw("pn"), vw("osg")))
-        cp("S", vw("lpl"), ind(vw("ic2"), vw("oidx")))
-        y_piece(62, 72)
-        wrap("kc", "kb", L, 4)
-        y_piece(72, 80)
-        ts(vw("ol4"), vw("kc", 3, L, 4), 4.0, A.mult, col("pf", 17), A.add)
+        wrap("ki", "kh", L, 4)
+        ts(vw("ol4"), vw("ki", 3, L, 4), 4.0, A.mult, col("pf", 17), A.add)
         cp("S", vw("cmp", 192, 384), ind(vw("Y", 0, 4 * C), vw("ol4", 12, 24)))
         cp("V", vw("cmp", 0, 192), ind(vw("Y", 0, 4 * C), vw("ol4", 0, 12)))
         quant("qc%d" % r, "sc%d" % r, 0, 128, vw("cmp"))
         send(vw("pa%d" % r), vw("ps%d" % r), "ap%d" % r)
         send(vw("lq%d" % r, 0, L), vw("qc%d" % r, 0, L), "aq%d" % r, dt.uint8)
         send(vw("ls%d" % r, 0, L), vw("sc%d" % r, 0, L), "as%d" % r)
-        cp("S", vw("old"), ind(vw("pc"), vw("osg")))
-        tt(vw("kb", 0, L), ind(vw("lpl"), vw("osg")), vw("m16", 0, L), A.mult)
-        if r == 0:
-            consts_c()
-        wrap("kc", "kb", L, 16)
-        if r == 0:
-            quant("qe", "se", 0, 512, vw("et"))
-        ts(vw("ol16"), vw("kc", 15, L, 16), 160.0, A.add)
-        scat(vw("Gp", 0, C), vw("ol16"), vw("icb", C, C + L))
-        tt(vw("kd"), ind(vw("Gp", 0, C), vw("oplace")), vw("m16"), A.mult)
-        tt(vw("kb"), ind(vw("Gp", 0, C), vw("oplace")), vw("m4"), A.mult)
-        wrap("ke", "kd", C, 16)
-        wrap("kc", "kb", C, 4)
-        ts(vw("os16"), vw("ke", 15, C, 16), 240.0, A.add)
-        ts(vw("os4"), vw("kc", 3, C, 4), 4.0, A.mult, col("pf", 17), A.add)
+        cp("S", vw("WP"), ind(vw("win"), vw("ogp", 0, 20)))
+        cp("S", vw("WR"), ind(vw("WP"), vw("oplr", 0, 20)))
+        tt(vw("kh", L, 2 * L), ind(vw("CS"), vw("osg")), vw("m16", 0, L), A.mult)
+        wrap("ki", "kh", 2 * L, 16, L)
+        ts(vw("olc"), vw("ki", L + 15, 2 * L, 16), -1.0, A.add)
+        tt(vw("cls"), ind(vw("WR"), vw("orank")), vw("cls"), A.add)
+        scat(vw("SC"), vw("olc"), vw("icb", C, C + L))
+        for i in range(4):
+            cp("S", vw("kd", i, C, 4), vw("SC", i, C, 4), col("pf", 18 + i))
+        wrap("kg", "kd", C, 4)
+        ts(vw("os4"), vw("kg", 3, C, 4), 4.0, A.mult, col("pf", 17), A.add)
+        arrive(vw("pa%d" % r), "ap%d" % r)
+        scat(vw("cls"), vw("olc"), vw("pa%d" % r))
         arrive(vw("lq%d" % r, 0, L), "aq%d" % r)
         arrive(vw("ls%d" % r, 0, L), "as%d" % r)
-        arrive(vw("pa%d" % r), "ap%d" % r)
-        new_points(r)
         if r == R - 1:
-            ts(vw("po"), vw("kst"), 1.0 / 320, A.mult, 12582912.0, A.add)
-            quant("qv", "sv", 0, 128, vw("vt"))
-            ts(vw("po2"), vw("po"), 12582913.0, A.subtract)
-            dma("Y", lambda: T.pts[:], lambda: T.po2[0:128:16, :], [vw("po2")], [])
+            cp("V", vw("po"), vw("cls"))
+            dma("Y", lambda: T.pts[:], lambda: T.po[0:128:16, :], [vw("po")], [])
         for b in range(4):
             mm("p" + "ABCD"[b], ("qe", "se", 128 * b), ("lq%d" % r, "ls%d" % r, 0, 128))
-        for b in range(4):
             cp("SV"[b % 2], vw("Y", 4 * C + b, 4 * (C + L), 4), vw("p" + "ABCD"[b], 0, L))
         cp("S", vw("X", 640, 1280), ind(vw("Y"), vw("os4", 40, 80)))
         cp("V", vw("X", 0, 640), ind(vw("Y"), vw("os4", 0, 40)))
-        if r < R - 1:
-            sign(vw("junk", 0, C), vw("kst"), col("pf", 10), 1.0, col("es", 0))
 
     quant("qx", "sx", 0, C, vw("X"))
     mm("pE", ("qv", "sv", 0), QX)
@@ -536,29 +567,35 @@ def rank_program(g, core, T, topo):
                 if j == i or not (m & mj).any():
                     continue
                 same = ops[j]["eng"] == o["eng"]
-                if (wr or wj or (psum and not same)) and not (same and o["acc"]):
+                if same and o["acc"]:
+                    o["order"].add(j)
+                elif wr or wj or (psum and not same):
                     deps.add(j)
             if wr and not o["acc"]:
                 h[:] = [e for e in h if (e[1] & ~m).any()]
             h.append((i, m, wr))
         o["deps"] = deps
-    needed = set()
     for o in ops:
-        needed |= o["deps"]
+        o["from"] = [ops[j] for j in o["deps"]]
+        o["inc"] = False
+    for o in ops:
+        for d in o["from"]:
+            d["inc"] = d["sem"] is None
+    if SCHED:
+        ops = issue_order(ops)
     n = {"V": 0, "S": 0, "T": 0, "G": 0}
     for i, o in enumerate(ops):
-        o["inc"] = False
-        if o["sem"] is None and i in needed:
+        o["at"] = i
+        if o["inc"]:
             n[o["eng"]] += 1
-            o["sem"], o["val"], o["inc"] = "c" + o["eng"], n[o["eng"]], True
+            o["sem"], o["val"] = "c" + o["eng"], n[o["eng"]]
     known = {e: {} for e in Q}
     for o in ops:
         if o["eng"] is None:
             o["know"] = {}
             continue
         k = known[o["eng"]]
-        for j in sorted(o["deps"], reverse=True):
-            d = ops[j]
+        for d in sorted(o["from"], key=lambda d: -d["at"]):
             if k.get(d["sem"], 0) < d["val"]:
                 Q[o["eng"]].wait_ge(T.sem[d["sem"]], d["val"])
                 k[d["sem"]] = d["val"]

@@ -4,14 +4,22 @@ from concourse.mybir import dt, AluOpType, ActivationFunctionType
 C, L, R = 320, 96, 3
 F32, BF, F16, I32, U16, Q4, U8 = "float32", "bfloat16", "float16", "int32", "uint16", "float8_e4m3fn_x4", "uint8"
 BIG = 1e29
+FL = "SSS"
+FILL = 1.0
+U = 2.0 ** -14
 TILES = ((20, 19, 18, 17), (16, 15, 14, 13), (12, 11, 10, 9), (8, 7, 6, 5), (4, 3, 2, 1))
 TILE0 = (0, 320, 576, 768, 896, 1024)
-NS = (12, 12, 12)
-NVL = 3
+NS = (13, 12, 12)
+NVL = 4
 ZCUT = (0, 8, 24, 40)
+LCUT = ()
+HS = 320
+YCUT = (0, 8, 16, 24, 32, 40)
+XP = 320
+YA = "S"
 ZV = 1
 KW = 2
-WAKE, LOCAL, REMOTE, SLACK = 220.0, 2500.0, 2600.0, 60.0
+WAKE, LOCAL, REMOTE, SLACK = 220.0, 2200.0, 1600.0, 60.0
 SCHED = True
 
 
@@ -29,18 +37,19 @@ SCRATCH = {
     "ai": _sb(512, BF), "at": _sb(1024, BF), "qa": _sb(256, Q4), "sa": _sb(256, U8), "q0": _sb(128, Q4), "s0": _sb(128, U8),
     "bits": _sb(4096, BF), "qb": _sb(1024, Q4), "sb": _sb(1024, U8), "pb": _sb(4 * C, BF), "qp": _sb(C, Q4), "sp": _sb(C, U8),
     "ah": _sb(640, BF), "Z": _sb(640, BF), "H": _sb(4 * C, BF), "cmp": _sb(512, BF),
-    "ic2": _sb(C, F32), "icb": _sb(C + L, BF), "i16": _sb(C, BF), "i4": _sb(C, BF), "t16": _sb(16, BF), "sg0": _sb(52, F32),
+    "ic2": _sb(C, F32), "icb": _sb(C + L, BF), "i16": _sb(C, BF), "i4": _sb(C, BF), "t16": _sb(16, BF), "sg0": _sb(60, F32),
     "m16": _sb(C, BF), "m4": _sb(C, BF), "r16": _sb(C, BF), "r4": _sb(C, BF), "r8": _sb(C, BF), "r32": _sb(2 * C, BF),
     "bigm": _sb(C, BF), "rbig": _sb(C, BF), "rmin": _sb(C + 32, BF),
     "pi": _sb(8, I32), "pf": _sb(24, F32), "ui": _sb(8, I32), "uo": _sb(8, U16), "ic2h": _sb(C, F16),
     "km": _sb(C, F32), "kw": _sb(C, F32), "sj": _sb(4 * C, BF), "k2": _sb(2 * C, F16), "k3": _sb(2 * C, F16),
-    "kb": _sb(C, F16), "kc": _sb(C, F16), "kd": _sb(C, BF), "ke": _sb(C, F16), "kf": _sb(C, F16), "kg": _sb(C, F16),
+    "kc": _sb(C, F16), "kd": _sb(C, BF), "ke": _sb(C, F16), "kf": _sb(C, F16), "kg": _sb(C, F16),
     "kh": _sb(2 * L, F16), "ki": _sb(2 * L, F16),
-    "cb": _sb(6 * C, BF), "co": _sb(12 * 160, F16), "cd": _sb(168, F16), "junk": _sb(7 * C, BF),
-    "cls": _sb(C, BF), "pm": _sb(C, BF), "xq": _sb(C, F16), "Lr": _sb(C, F32), "La": _sb(C, F32), "O": _sb(C, F32),
+    "cb": _sb(6 * C, BF), "co": _sb(12 * 160, F16), "cd": _sb(168, F16), "ce": _sb(192, F16), "junk": _sb(7 * C, BF),
+    "cls": _sb(C, BF), "pm": _sb(C, BF), "Lr": _sb(C, BF), "xq": _sb(C, F16), "Lf": _sb(C, F32), "Lg": _sb(C, F32), "La": _sb(C, BF), "O": _sb(C, BF),
     "val": _sb(C + 32, F16), "tv": _sb(2 * C + 32, F16), "tw": _sb(2 * C + 32, BF),
-    "CS": _sb(C, F32), "tab": _sb(10 * C, BF),
-    "seg": _sb(160, BF), "sgo": _sb(160, F16), "seh": _sb(160, F32), "sho": _sb(160, F32), "sgl": _sb(C, F16), "sgm": _sb(C, F16),
+    "CS": _sb(C, BF), "tab": _sb(11 * C, BF),
+    "f1": _sb(160, BF), "g1": _sb(160, F32), "o1": _sb(160, F32), "f2": _sb(C, BF), "g2": _sb(C, BF), "o2": _sb(C, BF),
+    "f3": _sb(160, BF), "g3": _sb(160, BF), "o3": _sb(160, BF),
     "yo": _sb(C, F32), "po": _sb(C, F32),
 }
 for _r in range(R):
@@ -54,23 +63,23 @@ for _b in "ABCDEFG":
     SCRATCH["p" + _b] = ("psum", [128, 512], F32)
 SMALL = {}
 _at = 0
-for _n, _w in (("mpar", 32), ("em", 32), ("ef", 32), ("acc", 6), ("es", 1), ("eq", 1), ("e16", 16), ("bi", 8), ("bk", 8), ("wk", 8),
-               ("mu", 8), ("su2", 8), ("nk", 8), ("dg", 8), ("Pb", 40), ("s2", 20), ("cz", 20), ("base", 20),
+for _n, _w in (("bk", 8), ("vn", 8), ("mpar", 32), ("em", 32), ("ef", 32), ("acc", 6), ("es", 1), ("eq", 1), ("e16", 16), ("bi", 8),
+               ("mu", 8), ("su2", 8), ("Pb", 40), ("sig", 20), ("s2", 20), ("cz", 20), ("c1", 20), ("jh", 20), ("jc", 20), ("base", 20),
                ("tn", 20), ("zz", 20), ("pr", 20), ("e160", 20), ("ix", 20), ("rs", 20), ("lw", 6), ("lx", 6),
-               ("nj", 40), ("ib", 40), ("sl", 40), ("a1", 20), ("a2", 20), ("os0", 2)):
+               ("nj", 40), ("yy", 40), ("ib", 40), ("sl", 40), ("a1", 20), ("a2", 20), ("a4", 20), ("a5", 20), ("os0", 2), ("a6", 4), ("bas0", 4)):
     SMALL[_n] = ("sm", _at, _w)
     _at += _w
 SCRATCH["sm"] = _sb(_at, F32)
 _at = 0
 for _n, _w in (("orank", 20), ("oplr", 32), ("osel", 2), ("opt", 20), ("oab", 80), ("oidx", 20), ("olam", 20), ("onp", 20),
-               ("ogp", 40), ("osg", 6), ("ol4", 24), ("olc", 6), ("os4", 80)):
+               ("ogp", 40), ("osg", 6), ("ol4", 24), ("olc", 6), ("os4", 80), ("oc1", 10), ("oc2", 20), ("oc3", 10)):
     SMALL[_n] = ("so", _at, _w)
     _at += _w
 SCRATCH["so"] = _sb(_at, U16)
-for _at, _n in enumerate(("Gp", "SR", "SC", "WP", "WR", "lp", "pn", "tb", "tc", "win")):
+for _at, _n in enumerate(("Gp", "SR", "SC", "WP", "WR", "lp", "pn", "tb", "tc", "win", "cu")):
     SMALL[_n] = ("tab", C * _at, C)
 
-NDMA = 24
+NDMA = 26
 SEMAPHORES = ["cV", "cS", "cT", "cG", "sent"] + ["d%d" % i for i in range(NDMA)] + \
     ["a%s%d" % (k, r) for k in "qsp" for r in range(R)]
 
@@ -148,7 +157,7 @@ def issue_order(ops):
             pick, limit = c[0], max(free.get(e, 0.0), ready[c[0]])
             for k in c[1:]:
                 t = max(free.get(e, 0.0), ready[k])
-                if t + ops[k]["cost"] <= limit + SLACK and t < limit:
+                if t + FILL * ops[k]["cost"] <= limit + SLACK and t < limit:
                     pick, limit = k, t
             if best is None or limit < best[0]:
                 best = (limit, e, pick)
@@ -250,13 +259,13 @@ def rank_program(g, core, T, topo):
         z = vw("zero", 0, out[2] - out[1])
         add("G", lambda q: q.affine_select(ap(out), ap(z), pat, op, 1.0, base, cm), [z], [out], 170 + 1.66 * size(out))
 
-    def dma(e, fo, fi, reads, writes, adding=False):
+    def dma(e, fo, fi, reads, writes, adding=False, lat=LOCAL):
         s = "d%d" % ndma[0]
         ndma[0] += 1
         if adding:
-            add(e, lambda q: q.dma_start(fo(), fi(), accum_op=A.add), reads, writes, 600, sem=s, val=16, lat=LOCAL)
+            add(e, lambda q: q.dma_start(fo(), fi(), accum_op=A.add), reads, writes, 600, sem=s, val=16, lat=lat)
         else:
-            add(e, lambda q: q.dma_start(fo(), fi()), reads, writes, 60, sem=s, val=16, lat=LOCAL)
+            add(e, lambda q: q.dma_start(fo(), fi()), reads, writes, 60, sem=s, val=16, lat=lat)
 
     rid, pid, _ = topo.addr(nxt)
     nout, nin = len(topo.engines(core, nxt)), len(topo.engines(prv, core))
@@ -276,7 +285,7 @@ def rank_program(g, core, T, topo):
         scan(vw(out, a, b), vw("r%d" % seg, a, b), vw(masked, a, b), 0.0, A.mult)
 
     dma("S", lambda: T.ut[:], lambda: T.u[:], [], [vw("ut")])
-    dma("Y", lambda: T.x0[:], lambda: T.x[:], [], [vw("x0")])
+    dma("Y", lambda: T.x0[:], lambda: T.x[:], [], [vw("x0")], lat=LOCAL + 800)
     dma("Y", lambda: ap(vw("qw"), dt.uint8), lambda: T.wc[:], [], [vw("qw")])
     dma("Y", lambda: T.sw[:], lambda: T.ws[:], [], [vw("sw")])
     dma("G", lambda: T.vt[:], lambda: T.v[:], [], [vw("vt")])
@@ -287,10 +296,16 @@ def rank_program(g, core, T, topo):
     iota(vw("ai"), [[1, 8], [0, 64]], 0, 0)
     iota(vw("sg0", 0, 20), [[16, 20]], 0, 0)
     iota(vw("sg0", 20, 52), [[1, 2], [0, 16]], 0, 0)
-    iota(vw("ic2"), [[2, C]], 2, 0)
+    iota(vw("sg0", 52, 60), [[1024, 8]], C, 0)
+    if LCUT:
+        iota(vw("La"), [[0, C]], 0, 0)
+    else:
+        iota(vw("ic2"), [[2, C]], 2, 0)
+        iota(vw("Lf"), [[0, C]], 0, 0)
+        cp("V", vw("ic2h"), vw("ic2"))
     where(vw("r8"), [[0, 40], [1, 8]], A.is_equal, 0, 0)
     where(vw("r32"), [[0, 20], [1, 32]], A.is_equal, 0, 0)
-    for k in range(5):
+    for k in range(4):
         a, b = 4 * (TILE0[k] + 16 * TILES[k][3]), 4 * TILE0[k + 1]
         iota(vw("bits", a, b), [[0, b - a]], 0, 0)
     iota(vw("Lr"), [[0, C]], 0, 0)
@@ -310,14 +325,10 @@ def rank_program(g, core, T, topo):
     ts(col("pi", 7), col("pi", 0), 4, A.arith_shift_right, 1, A.bitwise_and)
     cp("V", vw("uo"), vw("ui"))
     lin = lambda out, in_, scale, bias: act(out, in_, ACT.Identity, None, bias, scale)
-    sig = vw("Pb", 0, 20)
-    cp("S", vw("seg"), vw("zero", 0, 160))
-    cp("S", vw("seh"), vw("zero", 0, 160))
+    sig = vw("sig")
     sign(vw("r16"), vw("i16"), 0.0, 1.0)
     cp("V", vw("pf", 0, 8), vw("pi"))
-    fill(col("rs", 0), 0.0)
     ts(col("pf", 11), col("pf", 1), 2.0, A.subtract)
-    ts(col("pf", 9), col("pf", 2), -4.0, A.add)
     ts(col("pf", 10), col("pf", 3), -1.0, A.mult, 0.5, A.add)
     tt(col("pf", 12), col("pf", 11), col("pf", 11), A.mult)
     ts(vw("m16"), vw("i16"), col("pf", 1), A.is_equal)
@@ -331,7 +342,6 @@ def rank_program(g, core, T, topo):
     lin(vw("rbig"), vw("r16"), 2 * BIG, -BIG)
     lin(vw("rmin", 0, C), vw("r16"), 1185.0, -161.0)
     lin(vw("rmin", C, C + 32), vw("r16", 0, 32), 1185.0, -161.0)
-    cp("V", vw("sgl"), vw("zero", 0, C))
     cp("V", vw("val"), vw("zero", 0, C + 32))
     cp("V", vw("cd", 0, 8), vw("zero", 0, 8))
     cp("V", vw("k2", 1, 2 * C, 2), vw("zero", 0, C))
@@ -339,25 +349,34 @@ def rank_program(g, core, T, topo):
     add("V", lambda q: q.tensor_copy(ap(vw("qur"), dt.uint32), ap(ind(vw("qu"), vw("uo")), dt.uint32)), [vw("qu"), vw("uo")], [vw("qur")], 210)
     cp("S", vw("sur"), ind(vw("su"), vw("uo")))
     lin(sig, vw("sg0", 0, 20), 1.0, col("pf", 1))
-    lin(vw("base"), vw("sg0", 0, 20), 1.0, col("pf", 16))
-    lin(vw("s2"), sig, -1.0, 640.0)
-    lin(vw("seh", 7, 160, 8), sig, -1.0, 319.0)
-    lin(vw("cz"), sig, -0.5, 319.25)
-    cp("S", vw("seg", 7, 80, 8), vw("Pb", 0, 10))
-    cp("S", vw("seg", 87, 160, 8), vw("Pb", 0, 10))
-    lin(vw("lw"), vw("Pb", 0, 6), 1.0, -160.0)
-    lin(vw("lx"), vw("Pb", 0, 6), 1.0, -159.5)
+    ts(vw("k2", 1, 2 * C, 32), vw("sg0", 0, 20), col("pf", 16), A.add)
+    cp("S", vw("cu"), vw("zero", 0, C))
+    cp("V", col("ce", 31), vw("zero", 0, 1))
+    lin(vw("s2"), sig, -1.0, 639.5)
+    lin(vw("c1"), sig, -U, 319.25 * U)
+    lin(vw("cz"), sig, -0.5 * U, 319.5 * U)
+    lin(vw("Pb", 0, 20), sig, U, 0.25 * U)
+    for a in (0, 10):
+        cp("S", vw("jh", a, a + 10), vw("Pb", 0, 10))
+    lin(vw("lw"), vw("sig", 0, 6), 1.0, -160.0)
+    lin(vw("lx"), vw("sig", 0, 6), 1.0, -159.5)
+    lin(vw("f2"), vw("r8"), -2.0, 1.0)
+    lin(vw("f3"), vw("r8", 0, 160), -2.0, 1.0)
+    lin(vw("f3", 1, 160, 8), vw("zero", 0, 20), 1.0, 1.0)
+    lin(vw("f1"), vw("r8", 0, 160), 0.0, -1.0)
+    ts(vw("oc2"), vw("zero", 0, 20), col("pf", 3), A.add)
+    ts(vw("oc3", 0, 5), vw("zero", 0, 5), col("pf", 3), A.add)
+    ts(vw("oc3", 5, 10), vw("zero", 0, 5), col("pf", 3), A.add, -1.0, A.add)
+    ts(vw("oc1"), vw("zero", 0, 10), col("pf", 10), A.add, 6.5, A.add)
     ts(vw("at", 512, 1024), vw("ai"), col("pf", 14), A.is_equal)
     quant("qa", "sa", 128, 256, vw("at", 512, 1024))
     ts(vw("at", 0, 512), vw("ai"), col("pf", 4), A.is_equal)
     quant("qa", "sa", 0, 128, vw("at", 0, 512))
     ts(vw("mpar"), vw("sg0", 20, 52), col("pf", 7), A.is_equal)
-    ts(vw("sgl", 7, 160, 8), sig, -0.5, A.mult, -0.25, A.add)
-    ts(vw("os0"), vw("Pb", 0, 2), col("pf", 15), A.add, 41.0, A.min)
+    ts(vw("os0"), vw("sig", 0, 2), col("pf", 15), A.add, 41.0, A.min)
     ts(vw("osel"), vw("os0"), 16.0, A.mult, 15.0, A.add)
     ts(vw("pf", 18, 22), vw("i4", 0, 4), col("pf", 6), A.is_equal)
     ts(vw("m4"), vw("i4"), col("pf", 6), A.is_equal)
-    cp("V", vw("ic2h"), vw("ic2"))
     quant("q0", "s0", 0, 128, vw("zero", 0, 512))
     for r in range(R):
         dma("Y", lambda r=r: ap(vw("lq%d" % r, L, 128), dt.uint8), lambda: ap(vw("q0", 0, 128 - L), dt.uint8),
@@ -369,47 +388,58 @@ def rank_program(g, core, T, topo):
     def from_points(r):
         top = 3 + r
         e0, e1, b0, b1 = vw("e16", 0, 7), vw("e16", 1, 8), vw("bk", 0, 7), vw("bk", 1, 8)
-        ts(vw("pm"), vw("cls"), col("pf", 8), A.is_equal, 0.5, A.subtract)
-        scan(vw("xq"), vw("ic2h"), vw("pm"), 0.0, A.max, A.mult)
+        if LCUT:
+            ts(vw("pm"), vw("cls"), col("pf", 8), A.is_equal)
+        else:
+            ts(vw("pm"), vw("cls"), col("pf", 8), A.is_equal, 0.5, A.subtract)
+            scan(vw("xq"), vw("ic2h"), vw("pm"), 0.0, A.max, A.mult)
         sign(vw("junk", 6 * C, 7 * C), vw("cls"), col("pf", 10), 1.0, col("es", 0))
-        ts(vw("eq"), vw("es"), 0.5, A.mult, 160.0, A.add)
-        ts(vw("em"), vw("mpar"), col("eq", 0), A.mult)
+        lin(vw("eq"), vw("es"), 0.5, 160.0)
+        cp("S", vw("em"), vw("mpar"), col("eq", 0))
         trans(vw("ef"), vw("em"))
         tt(vw("e16"), vw("ef", 0, 16), vw("ef", 16, 32), A.add)
         ts(vw("bi"), vw("e16", 0, 8), -0.5, A.add, 1.5 * 2 ** 24, A.add)
-        tt(vw("nk", 0, 7), e0, e1, A.subtract)
         tt(vw("su2", 0, 7), e0, e1, A.add)
-        ts(vw("bk"), vw("bi"), 1.5 * 2 ** 24, A.subtract, 0.5, A.mult)
-        ts(vw("dg", 0, 7), vw("nk", 0, 7), 1024.0, A.add)
-        tt(vw("wk", 0, 7), b0, b1, A.subtract)
+        tt(vw("vn"), vw("sg0", 52, 60), vw("e16", 0, 8), A.subtract)
+        ts(vw("bk"), vw("bi"), 1.5 * 2 ** 24, A.subtract, 0.5 * U, A.mult)
         tt(vw("mu", 0, 7), b0, b1, A.add)
+
+        def below(e, out, x, limit):
+            if e == "S":
+                sign(out, x, limit, -1.0)
+            else:
+                ts(out, x, limit, A.is_lt, 0.5, A.subtract)
         for k in range(top + 1):
-            ts(vw("seg", 80 + k, 160, 8), vw("Pb", 0, 10), col("bk", k + 1), A.is_ge, col("wk", k), A.mult)
             if k:
-                ts(vw("seg", k, 80, 8), vw("Pb", 0, 10), col("bk", k), A.is_ge, col("wk", k), A.mult)
-        wrap("sgo", "seg", 160, 8)
-        cp("V", vw("opt"), vw("sgo", 7, 160, 8))
-        for k in range(top):
-            ts(vw("seh", k, 160, 8), vw("s2"), col("su2", k), A.is_le, col("dg", k), A.mult)
-        wrap("sho", "seh", 160, 8)
-        ts(vw("tn"), vw("sho", 7, 160, 8), 1.5 * 2 ** 33, A.add, 1.5 * 2 ** 33, A.subtract)
-        tt(vw("Pb", 20, 40), vw("sho", 7, 160, 8), vw("tn"), A.subtract)
-        ts(vw("onp"), vw("tn"), 1.0 / 1024, A.mult)
-        cp("V", vw("oidx"), vw("Pb", 20, 40))
-        ts(vw("sgl", 167, C, 8), vw("Pb", 20, 40), -0.5, A.mult, -0.25, A.add)
+                below(FL[2], vw("f3", k + 1, 160, 8), vw("jh"), col("bk", k))
+        cp("S", vw("g3"), ind(vw("bk"), vw("oc3")), -1.0)
+        scan(vw("o3"), vw("f3"), vw("g3"), 0.0, A.max, A.min)
+        tt(vw("a4"), vw("jh"), vw("o3", 7, 160, 8), A.subtract)
+        ts(vw("opt"), vw("a4"), 1 / U, A.mult)
+        for n in range(1, top + 1):
+            below(FL[0], vw("f1", 8 - n, 160, 8), vw("s2"), col("su2", n - 1))
+        cp("S", vw("g1"), ind(vw("vn"), vw("oc1")), U)
+        scan(vw("o1"), vw("f1"), vw("g1"), 0.0, A.min, A.max)
+        ts(vw("tn"), vw("o1", 7, 160, 8), 1.5 * 2 ** 33 * U, A.add, 1.5 * 2 ** 33 * U, A.subtract)
+        tt(vw("a5"), vw("o1", 7, 160, 8), vw("c1"), A.add)
+        tt(vw("Pb", 20, 40), vw("a5"), vw("tn"), A.subtract)
+        ts(vw("onp"), vw("tn"), 1 / (1024 * U), A.mult)
+        ts(vw("oidx"), vw("Pb", 20, 40), 1 / U, A.mult)
         for k in range(top + 1):
-            ts(vw("sgl", k, C, 8), vw("Pb"), col("mu", k), A.is_ge, col("wk", k), A.mult)
-        wrap("sgm", "sgl", C, 8)
-        y = vw("sgm", 7, C, 8)
+            below(FL[1], vw("f2", k + 1, C, 8), vw("Pb"), col("mu", k))
+        cp("S", vw("g2"), ind(vw("bk"), vw("oc2")), -1.0)
+        scan(vw("o2"), vw("f2"), vw("g2"), 0.0, A.max, A.min)
+        y = vw("o2", 7, C, 8)
         tt(vw("zz"), vw("Pb", 20, 40), vw("cz"), A.subtract)
-        tt(vw("nj"), y, vw("sgl", 7, C, 8), A.add)
-        ts(vw("ib"), y, 0.0, A.is_gt, 160.0, A.mult)
-        tt(vw("pr"), vw("zz"), vw("sgm", 167, C, 8), A.mult)
-        tt(vw("sl"), vw("ib"), vw("nj"), A.subtract)
-        ts(vw("e160"), vw("pr"), 0.0, A.is_gt, 160.0, A.mult)
-        ts(vw("ogp"), vw("sl"), -0.5, A.add)
-        tt(vw("ix"), vw("e160"), vw("nj", 20, 40), A.subtract)
-        ts(vw("olam"), vw("ix"), -0.5, A.add)
+        tt(vw("nj"), vw("Pb"), y, A.add)
+        tt(vw("yy"), vw("nj"), y, A.add)
+        ts(vw("ib"), vw("yy"), 0.0, A.is_lt, 160 * U, A.mult)
+        tt(vw("pr"), vw("zz"), vw("yy", 20, 40), A.mult)
+        tt(vw("sl"), vw("ib"), vw("nj"), A.add)
+        ts(vw("e160"), vw("pr"), 0.0, A.is_lt, 160 * U, A.mult)
+        ts(vw("ogp"), vw("sl"), 1 / U, A.mult)
+        tt(vw("ix"), vw("e160"), vw("nj", 20, 40), A.add)
+        ts(vw("olam"), vw("ix"), 1 / U, A.mult)
         cp("S", vw("Gp"), ind(vw("icb"), vw("ogp", 0, 20)))
         cp("S", vw("lp"), ind(vw("icb"), vw("ogp", 20, 40)))
         cp("S", vw("pn"), ind(vw("t16"), vw("onp")))
@@ -435,12 +465,16 @@ def rank_program(g, core, T, topo):
             mm("pG", ("qa", "sa", 128), ("qp", "sp", 0, C))
             cp("V", vw("cls"), vw("pG", 0, C))
         from_points(r)
-        for a in (0, 640):
-            cp("S", vw("Xh", a, a + 640), vw(xs, a, a + 640), 0.5)
+        for a in range(0, 4 * C, XP):
+            cp("S", vw("Xh", a, a + XP), vw(xs, a, a + XP), 0.5)
         h = 16 * (ns - KW)
         for a, b in ((h, C), (0, h)):
             tt(vw("km", a, b), vw("pA", a, b), vw("bigm", a, b), A.add)
             scan(vw("kw", a, b), vw("rbig", a, b), vw("km", a, b), 0.0, A.min, A.max)
+        for m in range(4):
+            ts(vw("cu", 80 * m, 64 * m + 64), vw("pA", 16 * m + 16, 80), own(m), A.is_gt)
+        scan(vw("ce", 32, 160), vw("cu", 0, 256, 2), vw("cu", 1, 256, 2), 0.0, A.add)
+        tt(vw("k2", 7, 128, 32), vw("ce", 63, 160, 32), vw("ce", 31, 128, 32), A.subtract)
         for m in range(ns, 0, -1):
             j = vw("sj", C * (m % 4), C * (m % 4) + 16 * m)
             sign(j, vw("pB", 0, 16 * m), own(m), -1.0)
@@ -451,21 +485,28 @@ def rank_program(g, core, T, topo):
             e = 160 * (m - ns)
             ts(lane(m, 0, 16 * m), vw("pA", 0, 16 * m), own(m), A.is_lt)
             scan(vw("co", e - 8 * m, e), lane(m, 0, 8 * m), lane(m, 8 * m, 16 * m), 0.0, A.add)
-        cp("V", vw("rs", ns + 1, 20), vw("co", 159, 160 * (19 - ns), 160))
-        tt(vw("a1"), vw("cd", 7, 160, 8), vw("cd", 15, 168, 8), A.subtract)
-        tt(vw("a2"), vw("a1"), vw("base"), A.add)
-        tt(vw("k2", 1, 2 * C, 32), vw("a2"), vw("rs"), A.subtract)
-        for k in range(5):
+        ts(vw("k2", 32 * (ns + 1) + 5, 2 * C, 32), vw("co", 159, 160 * (19 - ns), 160), -1.0, A.mult)
+        for a, b in ((5, ns + 1), (1, 5)):
+            ts(vw("k2", 32 * a + 5, 32 * b, 32), vw("rs", a, b), -1.0, A.mult)
+        tt(vw("k2", 3, 2 * C, 32), vw("cd", 7, 160, 8), vw("cd", 15, 168, 8), A.subtract)
+        for k in range(4):
             quant("qb", "sb", TILE0[k], TILE0[k + 1], vw("bits", 4 * TILE0[k], 4 * TILE0[k + 1]))
-            mm("pE", ("qa", "sa", 0), ("qb", "sb", TILE0[k], TILE0[k + 1]), k == 0, k == 4)
-        tt(vw("k2", 0, 2 * C, 2), vw("pE", 0, C), vw("m16"), A.mult)
-        wrap("k3", "k2", 2 * C, 32)
-        cp("V", vw("orank"), vw("k3", 31, 2 * C, 32))
-        scat(vw("Lr"), vw("orank"), vw("xq"))
-        act(vw("La"), vw("Lr"), ACT.Abs)
-        ts(vw("kb"), vw("Lr"), 0.0, A.is_gt)
-        scan(vw("kc"), vw("kb"), vw("zero", 0, C), col("eq", 0), A.add)
-        scan(vw("val", 16, 16 + C), vw("kc"), vw("kb"), 0.0, A.max, A.mult)
+            mm("pE", ("qa", "sa", 0), ("qb", "sb", TILE0[k], TILE0[k + 1]), k == 0, k == 3)
+        for a in (160, 0):
+            tt(vw("k2", 2 * a, 2 * a + C, 2), vw("pE", a, a + 160), vw("m16", a, a + 160), A.mult)
+            wrap("k3", "k2", 2 * a + C, 32, 2 * a)
+            cp("V", vw("orank", a // 16, a // 16 + 10), vw("k3", 2 * a + 31, 2 * a + C, 32))
+        if LCUT:
+            scat(vw("Lr"), vw("orank"), vw("pm"))
+            for a, b in zip(LCUT, LCUT[1:]):
+                scat(vw("La"), vw("orank", a, b), vw("icb", 16 * a, 16 * b))
+        else:
+            scat(vw("Lf"), vw("orank"), vw("xq"))
+            ts(vw("Lr"), vw("Lf"), 0.0, A.is_gt)
+            act(vw("Lg"), vw("Lf"), ACT.Abs)
+            lin(vw("La"), vw("Lg"), 1.0, -209.0)
+        scan(vw("kc"), vw("Lr"), vw("zero", 0, C), col("eq", 0), A.add)
+        scan(vw("val", 16, 16 + C), vw("kc"), vw("Lr"), 0.0, A.max, A.mult)
         trans(vw("tv", C, 2 * C + 32), vw("val"))
         trans(vw("tv", 0, C), vw("val", 16, 16 + C))
         scan(vw("tw", C, 2 * C + 32), vw("rmin"), vw("tv", C, 2 * C + 32), 0.0, A.min)
@@ -478,21 +519,25 @@ def rank_program(g, core, T, topo):
         for k in range(2):
             tt(vw("ke", 160 * k, 160 * k + 160), ind(vw("O"), vw("opt", 10 * k, 10 * k + 10)), vw("m4", 0, 160), A.mult)
             wrap("kf", "ke", 160 * k + 160, 4, 160 * k)
-            ts(vw("oab", 40 * k, 40 * k + 40), vw("kf", 160 * k + 3, 160 * k + 160, 4), 4.0, A.mult, col("pf", 9), A.add)
+            ts(vw("oab", 40 * k, 40 * k + 40), vw("kf", 160 * k + 3, 160 * k + 160, 4), 4.0, A.mult, col("pf", 17), A.add)
         for i, (a, b) in enumerate(zip(ZCUT, ZCUT[1:])):
             cp("V" if i < ZV else "S", vw("ah", 16 * a, 16 * b), ind(vw("Xh"), vw("oab", a, b)))
             tt(vw("Z", 16 * a, 16 * b), ind(vw("Xh"), vw("oab", 40 + a, 40 + b)), vw("ah", 16 * a, 16 * b), A.add)
         quant("qz", "sz", 0, 160, vw("Z"))
-        cp("S", vw("Y", 640, 1280), ind(vw(xs), vw("oab", 40, 80)))
-        cp("V", vw("Y", 0, 640), vw("ah"), 2.0)
+        if not YCUT:
+            cp("S", vw("Y", 640, 1280), ind(vw(xs), vw("oab", 40, 80)))
+        cp(YA, vw("Y", 0, 640), vw("ah"), 2.0)
         for b in range(4):
             mm("p" + "ABCD"[b], ("qw", "sw", 128 * b), ("qz", "sz", 0, 160))
             cp("VS"[b % 2], vw("H", b, 640, 4), vw("p" + "ABCD"[b], 0, 160), 0.03125)
         quant("qh", "sh", 0, 160, vw("H", 0, 640))
         mm("pE", U16R, ("qh", "sh", 0, 160))
-        cp("S", vw("H", 640, 960), vw("H", 0, 320), -1.0)
-        cp("V", vw("H", 960, 1280), vw("H", 320, 640), -1.0)
-        for a in (0, 640):
+        for a, b in zip(YCUT, YCUT[1:]):
+            tt(vw("Y", 640 + 16 * a, 640 + 16 * b), ind(vw(xs), vw("oab", 40 + a, 40 + b)), vw("H", 16 * a, 16 * b), A.subtract)
+        if not YCUT:
+            cp("S", vw("H", 640, 640 + HS), vw("H", 0, HS), -1.0)
+            cp("V", vw("H", 640 + HS, 1280), vw("H", HS, 640), -1.0)
+        for a in (0,) if YCUT else (0, 640):
             dma("G", lambda a=a: ap(vw("Y", a, a + 640)), lambda a=a: ap(vw("H", a, a + 640)),
                 [vw("H", a, a + 640), vw("Y", a, a + 640)], [vw("Y", a, a + 640)], True)
         ts(vw("win", 0, 160), vw("pE", 0, 160), 0.0, A.is_gt)
@@ -525,7 +570,7 @@ def rank_program(g, core, T, topo):
         cp("S", vw("WR"), ind(vw("WP"), vw("oplr", 0, 20)))
         tt(vw("kh", L, 2 * L), ind(vw("CS"), vw("osg")), vw("m16", 0, L), A.mult)
         wrap("ki", "kh", 2 * L, 16, L)
-        ts(vw("olc"), vw("ki", L + 15, 2 * L, 16), -1.0, A.add)
+        ts(vw("olc"), vw("ki", L + 15, 2 * L, 16), 208.0, A.add)
         tt(vw("cls"), ind(vw("WR"), vw("orank")), vw("cls"), A.add)
         scat(vw("SC"), vw("olc"), vw("icb", C, C + L))
         for i in range(4):
@@ -545,13 +590,14 @@ def rank_program(g, core, T, topo):
         cp("S", vw("X", 640, 1280), ind(vw("Y"), vw("os4", 40, 80)))
         cp("V", vw("X", 0, 640), ind(vw("Y"), vw("os4", 0, 40)))
 
-    quant("qx", "sx", 0, C, vw("X"))
-    mm("pE", ("qv", "sv", 0), QX)
+    for k, a in enumerate((0, 160)):
+        quant("qx", "sx", a, a + 160, vw("X", 4 * a, 4 * a + 640))
+        mm("p" + "EF"[k], ("qv", "sv", 0), ("qx", "sx", a, a + 160))
+        cp("SV"[k], vw("yo", a, a + 160), vw("p" + "EF"[k], 0, 160))
+        dma("SY"[k], lambda a=a: T.y[:, a:a + 160], lambda a=a: T.yo[:, a:a + 160], [vw("yo", a, a + 160)], [])
     dma("Y", lambda: T.oc[:], lambda: ap(vw("qx"), dt.uint8), [vw("qx")], [])
-    cp("V", vw("yo"), vw("pE", 0, C))
     for k in range(4):
-        dma("YS"[k // 2], lambda k=k: T.osc[4 * k:4 * k + 4, :], lambda k=k: T.sx[32 * k:32 * k + 4, :], [vw("sx")], [])
-    dma("S", lambda: T.y[:], lambda: T.yo[:], [vw("yo")], [])
+        dma("Y", lambda k=k: T.osc[4 * k:4 * k + 4, :], lambda k=k: T.sx[32 * k:32 * k + 4, :], [vw("sx")], [])
 
     hist = {}
     for i, o in enumerate(ops):

@@ -6,15 +6,29 @@ F32, BF, F16, I32, U16, Q4, U8 = "float32", "bfloat16", "float16", "int32", "uin
 BIG = 1e29
 FL = "SSS"
 FILL = 1.0
+TRO, ESO = True, (1, 2)
 U = 2.0 ** -14
 TILES = ((20, 19, 18, 17), (16, 15, 14, 13), (12, 11, 10, 9), (8, 7, 6, 5), (4, 3, 2, 1))
 TILE0 = (0, 320, 576, 768, 896, 1024)
-NS = (13, 12, 12)
+NS = (12, 12, 12)
 NVL = 4
 ZCUT = (0, 8, 24, 40)
-LCUT = ()
+WS, DS = "S", False
+XL, TB = 800, (0, 0, 0)
+GL, SL, KO, PBG = False, True, 0, False
+LIFT = 16384.0
+YP = (1, 1, 1, 1, 1, 1, 0)
+ACUT = (40,)
+KC = (320, 112, 0)
+TV, CV, HE, XV = 10, 12, "VSVS", 40
+TCUT, XC = 192, (24, 68)
+NL = 5
+SCA, GAT, FIX, LEAST, SFIX = 2.5, 1.2, 0.0, 53.0, 60.0
+CL, PSO, PMO = "S", True, True
+D = 2.0 ** -17
+TINY = 1e-35
 HS = 320
-YCUT = (0, 8, 16, 24, 32, 40)
+YCUT = (0, 8, 14, 20, 26, 34, 40)
 XP = 320
 YA = "S"
 ZV = 1
@@ -37,17 +51,17 @@ SCRATCH = {
     "ai": _sb(512, BF), "at": _sb(1024, BF), "qa": _sb(256, Q4), "sa": _sb(256, U8), "q0": _sb(128, Q4), "s0": _sb(128, U8),
     "bits": _sb(4096, BF), "qb": _sb(1024, Q4), "sb": _sb(1024, U8), "pb": _sb(4 * C, BF), "qp": _sb(C, Q4), "sp": _sb(C, U8),
     "ah": _sb(640, BF), "Z": _sb(640, BF), "H": _sb(4 * C, BF), "cmp": _sb(512, BF),
-    "ic2": _sb(C, F32), "icb": _sb(C + L, BF), "i16": _sb(C, BF), "i4": _sb(C, BF), "t16": _sb(16, BF), "sg0": _sb(60, F32),
+    "icb": _sb(C + L, BF), "i16": _sb(C, BF), "t16": _sb(16, BF), "sg0": _sb(60, F32),
     "m16": _sb(C, BF), "m4": _sb(C, BF), "r16": _sb(C, BF), "r4": _sb(C, BF), "r8": _sb(C, BF), "r32": _sb(2 * C, BF),
-    "bigm": _sb(C, BF), "rbig": _sb(C, BF), "rmin": _sb(C + 32, BF),
-    "pi": _sb(8, I32), "pf": _sb(24, F32), "ui": _sb(8, I32), "uo": _sb(8, U16), "ic2h": _sb(C, F16),
-    "km": _sb(C, F32), "kw": _sb(C, F32), "sj": _sb(4 * C, BF), "k2": _sb(2 * C, F16), "k3": _sb(2 * C, F16),
-    "kc": _sb(C, F16), "kd": _sb(C, BF), "ke": _sb(C, F16), "kf": _sb(C, F16), "kg": _sb(C, F16),
+    "bigm": _sb(C, BF), "rbig": _sb(C, BF),
+    "pi": _sb(8, I32), "pf": _sb(32, F32), "ui": _sb(8, I32), "uo": _sb(8, U16), "amp": _sb(C, F32),
+    "km": _sb(C, F32), "kw": _sb(C, F32), "sj": _sb(8 * 15 * 16, BF), "k2": _sb(2 * C, F16), "k3": _sb(2 * C, F16),
+    "kd": _sb(C, BF), "ke": _sb(C, F16), "kf": _sb(C, F16), "kg": _sb(C, F16),
     "kh": _sb(2 * L, F16), "ki": _sb(2 * L, F16),
-    "cb": _sb(6 * C, BF), "co": _sb(12 * 160, F16), "cd": _sb(168, F16), "ce": _sb(192, F16), "junk": _sb(7 * C, BF),
-    "cls": _sb(C, BF), "pm": _sb(C, BF), "Lr": _sb(C, BF), "xq": _sb(C, F16), "Lf": _sb(C, F32), "Lg": _sb(C, F32), "La": _sb(C, BF), "O": _sb(C, BF),
-    "val": _sb(C + 32, F16), "tv": _sb(2 * C + 32, F16), "tw": _sb(2 * C + 32, BF),
-    "CS": _sb(C, BF), "tab": _sb(11 * C, BF),
+    "cb": _sb(6 * C, BF), "co": _sb(12 * 160, F16), "cd": _sb(4 * 296, F16), "ce": _sb(192, F16), "junk": _sb(7 * C, BF),
+    "cls": _sb(C, BF), "pm": _sb(C, BF), "xq": _sb(C, F32), "Lf": _sb(C, F32), "Lg": _sb(C, F32), "La": _sb(C, BF), "O": _sb(C, BF),
+    "val": _sb(C + 32, BF), "tv": _sb(2 * C + 32, BF), "tw": _sb(2 * C + 32, BF),
+    "tab": _sb(13 * C, BF),
     "f1": _sb(160, BF), "g1": _sb(160, F32), "o1": _sb(160, F32), "f2": _sb(C, BF), "g2": _sb(C, BF), "o2": _sb(C, BF),
     "f3": _sb(160, BF), "g3": _sb(160, BF), "o3": _sb(160, BF),
     "yo": _sb(C, F32), "po": _sb(C, F32),
@@ -63,7 +77,7 @@ for _b in "ABCDEFG":
     SCRATCH["p" + _b] = ("psum", [128, 512], F32)
 SMALL = {}
 _at = 0
-for _n, _w in (("bk", 8), ("vn", 8), ("mpar", 32), ("em", 32), ("ef", 32), ("acc", 6), ("es", 1), ("eq", 1), ("e16", 16), ("bi", 8),
+for _n, _w in (("bk", 8), ("vn", 8), ("mpar", 32), ("em", 32), ("ef", 32), ("acc", 6), ("es", 1), ("eq", 1), ("e0", 2), ("e16", 16), ("bi", 8),
                ("mu", 8), ("su2", 8), ("Pb", 40), ("sig", 20), ("s2", 20), ("cz", 20), ("c1", 20), ("jh", 20), ("jc", 20), ("base", 20),
                ("tn", 20), ("zz", 20), ("pr", 20), ("e160", 20), ("ix", 20), ("rs", 20), ("lw", 6), ("lx", 6),
                ("nj", 40), ("yy", 40), ("ib", 40), ("sl", 40), ("a1", 20), ("a2", 20), ("a4", 20), ("a5", 20), ("os0", 2), ("a6", 4), ("bas0", 4)):
@@ -76,10 +90,10 @@ for _n, _w in (("orank", 20), ("oplr", 32), ("osel", 2), ("opt", 20), ("oab", 80
     SMALL[_n] = ("so", _at, _w)
     _at += _w
 SCRATCH["so"] = _sb(_at, U16)
-for _at, _n in enumerate(("Gp", "SR", "SC", "WP", "WR", "lp", "pn", "tb", "tc", "win", "cu")):
+for _at, _n in enumerate(("Gp", "SR", "SC", "WP", "WR", "lp", "pn", "tb", "tc", "win", "cu", "one", "CS")):
     SMALL[_n] = ("tab", C * _at, C)
 
-NDMA = 26
+NDMA = 28
 SEMAPHORES = ["cV", "cS", "cT", "cG", "sent"] + ["d%d" % i for i in range(NDMA)] + \
     ["a%s%d" % (k, r) for k in "qsp" for r in range(R)]
 
@@ -109,13 +123,13 @@ def size(v):
 def span(out, *ins, both=False):
     vs = [v for v in (out,) + ins if isinstance(v, tuple)]
     if out[0] == "*":
-        return 50 + 2.5 * size(out)
+        return 50 + SCA * size(out)
     if any(v[0] == "*" for v in vs):
-        return 55 + 1.2 * size(out)
+        return 55 + GAT * size(out)
     kinds = [SCRATCH[v[0]] for v in vs if size(v) > 1 or v is out]
     if both:
-        return max(53, size(out) * (0.83 if any(k[0] == "psum" for k in kinds) else 1.66))
-    return max(53, size(out) * (0.42 if all(k[2] in (BF, F16, U16) for k in kinds) else 0.83))
+        return FIX + max(LEAST, size(out) * (0.83 if any(k[0] == "psum" for k in kinds) else 1.66))
+    return FIX + max(LEAST, size(out) * (0.42 if all(k[2] in (BF, F16, U16) for k in kinds) else 0.83))
 
 
 def issue_order(ops):
@@ -157,7 +171,7 @@ def issue_order(ops):
             pick, limit = c[0], max(free.get(e, 0.0), ready[c[0]])
             for k in c[1:]:
                 t = max(free.get(e, 0.0), ready[k])
-                if t + FILL * ops[k]["cost"] <= limit + SLACK and t < limit:
+                if t + ops[k]["cost"] * (FILL if ops[k]["loose"] else 1.0) <= limit + SLACK and t < limit:
                     pick, limit = k, t
             if best is None or limit < best[0]:
                 best = (limit, e, pick)
@@ -196,13 +210,14 @@ def rank_program(g, core, T, topo):
 
     def add(eng, fn, reads, writes, cost, sem=None, val=0, acc=False, lat=0.0, order=()):
         ops.append({"eng": eng, "fn": fn, "r": parts(reads), "w": parts(writes), "sem": sem, "val": val, "acc": acc,
-                    "cost": cost, "lat": lat, "order": set(order)})
+                    "cost": cost, "lat": lat, "order": set(order),
+                    "loose": any(isinstance(v, tuple) and v[0] == "*" for v in reads)})
 
     def scat(out, off, in_):
         add("V", lambda q: q.tensor_copy(ap(ind(out, off)), ap(in_)), [off, in_], [out], span(ind(out, off)))
 
     def act(out, in_, func, accum=None, bias=0.0, scale=1.0):
-        cost = span(out, in_) if in_[0] == "*" else 60 + 0.83 * size(out)
+        cost = span(out, in_) if in_[0] == "*" else SFIX + 0.83 * size(out)
         kw = {} if func == ACT.Copy else {"bias": sc(bias)}
         if isinstance(scale, tuple) or scale != 1.0:
             kw["scale"] = sc(scale)
@@ -276,7 +291,7 @@ def rank_program(g, core, T, topo):
         nsent[0] += nout
         sent_at[sem] = len(ops)
         add("G", lambda q: q.remote_dma(ap(dst, cast), ap(src, cast), T.sem[sem], T.sem.sent, pid, rid, topo.mask(core, nxt)),
-            [src], [], 400, sem="-", lat=REMOTE)
+            [src], [], 400, sem="-", lat=REMOTE, order=[sent_at["ap" + sem[2]]] if PSO and sem[1] != "p" else [])
 
     def arrive(dst, sem):
         add(None, None, [], [dst], 0.0, sem=sem, val=nin, order=[sent_at[sem]])
@@ -285,39 +300,38 @@ def rank_program(g, core, T, topo):
         scan(vw(out, a, b), vw("r%d" % seg, a, b), vw(masked, a, b), 0.0, A.mult)
 
     dma("S", lambda: T.ut[:], lambda: T.u[:], [], [vw("ut")])
-    dma("Y", lambda: T.x0[:], lambda: T.x[:], [], [vw("x0")], lat=LOCAL + 800)
-    dma("Y", lambda: ap(vw("qw"), dt.uint8), lambda: T.wc[:], [], [vw("qw")])
-    dma("Y", lambda: T.sw[:], lambda: T.ws[:], [], [vw("sw")])
+    dma("Y", lambda: T.x0[:], lambda: T.x[:], [], [vw("x0")], lat=LOCAL + XL)
+    dma("Y", lambda: ap(vw("qw"), dt.uint8), lambda: T.wc[:], [vw("x0")], [vw("qw")])
+    dma("Y", lambda: T.sw[:], lambda: T.ws[:], [vw("x0")], [vw("sw")])
     dma("G", lambda: T.vt[:], lambda: T.v[:], [], [vw("vt")])
     fill(vw("zero"), 0.0)
     iota(col("pi", 0), [[0, 1]], 0, 1)
-    iota(vw("ui"), [[16, 8]], 0, 0)
+    first = len(ops) - 1
     iota(vw("i16"), [[0, 20], [1, 16]], 0, 0)
+    iota(vw("ui"), [[16, 8]], 0, 0)
     iota(vw("ai"), [[1, 8], [0, 64]], 0, 0)
     iota(vw("sg0", 0, 20), [[16, 20]], 0, 0)
     iota(vw("sg0", 20, 52), [[1, 2], [0, 16]], 0, 0)
     iota(vw("sg0", 52, 60), [[1024, 8]], C, 0)
-    if LCUT:
-        iota(vw("La"), [[0, C]], 0, 0)
-    else:
-        iota(vw("ic2"), [[2, C]], 2, 0)
-        iota(vw("Lf"), [[0, C]], 0, 0)
-        cp("V", vw("ic2h"), vw("ic2"))
+    if PBG:
+        iota(vw("pb"), [[0, 4 * C]], 0, 0)
+    iota(vw("icb"), [[1, C + L]], -208, 0)
     where(vw("r8"), [[0, 40], [1, 8]], A.is_equal, 0, 0)
     where(vw("r32"), [[0, 20], [1, 32]], A.is_equal, 0, 0)
-    for k in range(4):
-        a, b = 4 * (TILE0[k] + 16 * TILES[k][3]), 4 * TILE0[k + 1]
-        iota(vw("bits", a, b), [[0, b - a]], 0, 0)
-    iota(vw("Lr"), [[0, C]], 0, 0)
-    iota(vw("i4"), [[0, 80], [1, 4]], 0, 0)
-    iota(vw("icb"), [[1, C + L]], -208, 0)
-    where(vw("r4"), [[0, 80], [1, 4]], A.is_equal, 0, 0)
-    iota(vw("O"), [[0, C]], 0, 0)
+    iota(vw("Lf"), [[0, C]], 0, 0)
     iota(vw("t16"), [[1, 16]], 0, 0)
+    iota(vw("O"), [[0, C]], 0, 0)
+    where(vw("r4"), [[0, 80], [1, 4]], A.is_equal, 0, 0)
     iota(vw("cmp", 4 * L, 512), [[0, 512 - 4 * L]], 0, 0)
     for b in range(4):
         where(vw("et", 512 * b, 512 * b + 512), [[1, 512]], A.not_equal, -b, -4)
-    fill(vw("pb"), 0.0)
+    for i in range(first + 1, len(ops)):
+        ops[i]["order"].add(i - 1)
+    for k in range(4):
+        a, b = 4 * (TILE0[k] + 16 * min(TILES[k])), 4 * TILE0[k + 1]
+        cp("S", vw("bits", a, b), vw("zero", 0, b - a))
+    if not PBG:
+        fill(vw("pb"), 0.0)
     for j, m in ((1, 15), (2, 3), (3, 7), (5, 1)):
         ts(col("pi", j), col("pi", 0), m, A.bitwise_and)
     ts(col("pi", 4), col("pi", 0), 4, A.arith_shift_right)
@@ -332,7 +346,7 @@ def rank_program(g, core, T, topo):
     ts(col("pf", 10), col("pf", 3), -1.0, A.mult, 0.5, A.add)
     tt(col("pf", 12), col("pf", 11), col("pf", 11), A.mult)
     ts(vw("m16"), vw("i16"), col("pf", 1), A.is_equal)
-    ts(col("pf", 8), col("pf", 1), -1.0, A.add)
+    ts(col("pf", 8), col("pf", 3), -1.0, A.add)
     ts(col("pf", 17), col("pf", 2), 4.0 * 208, A.add)
     ts(col("pf", 13), col("pf", 12), 1.5, A.is_gt, 20.0, A.mult)
     ts(col("pf", 15), col("pf", 5), col("pf", 7), A.not_equal, 21.0, A.mult)
@@ -340,9 +354,16 @@ def rank_program(g, core, T, topo):
     tt(col("pf", 14), col("pf", 13), col("pf", 4), A.add)
     lin(vw("bigm"), vw("m16"), BIG, -BIG)
     lin(vw("rbig"), vw("r16"), 2 * BIG, -BIG)
-    lin(vw("rmin", 0, C), vw("r16"), 1185.0, -161.0)
-    lin(vw("rmin", C, C + 32), vw("r16", 0, 32), 1185.0, -161.0)
-    cp("V", vw("val"), vw("zero", 0, C + 32))
+    ts(col("pf", 22), col("pf", 1), 7.5, A.is_lt)
+    for j, lo, hi in ((23, 2.0, -2.0), (25, D, 1.0), (26, 0.5 + 48 * D, 1232.0), (27, -0.5, 0.0),
+                      (28, 1 / D, 1.0), (29, -0.5 / D - 48, -1232.0), (30, 0.5, 0.0)):
+        ts(col("pf", j), col("pf", 22), lo - hi, A.mult, hi, A.add)
+    ts(vw("one"), vw("zero", 0, C), col("pf", 22), A.add)
+    lin(vw("amp"), vw("icb", 0, C), col("pf", 25), col("pf", 26))
+    for a in (0, C + 16):
+        cp("V", vw("val", a, a + 16), vw("zero", 0, 16))
+    for a in (C - 8, 2 * C + 24):
+        cp("V", vw("tw", a, a + 8), vw("zero", 0, 8))
     cp("V", vw("cd", 0, 8), vw("zero", 0, 8))
     cp("V", vw("k2", 1, 2 * C, 2), vw("zero", 0, C))
     quant("qu", "su", 0, 128, vw("ut"))
@@ -374,9 +395,10 @@ def rank_program(g, core, T, topo):
     quant("qa", "sa", 0, 128, vw("at", 0, 512))
     ts(vw("mpar"), vw("sg0", 20, 52), col("pf", 7), A.is_equal)
     ts(vw("os0"), vw("sig", 0, 2), col("pf", 15), A.add, 41.0, A.min)
-    ts(vw("osel"), vw("os0"), 16.0, A.mult, 15.0, A.add)
-    ts(vw("pf", 18, 22), vw("i4", 0, 4), col("pf", 6), A.is_equal)
-    ts(vw("m4"), vw("i4"), col("pf", 6), A.is_equal)
+    ts(vw("osel"), vw("os0"), 16.0, A.mult, 7.0, A.add)
+    ts(vw("pf", 18, 22), vw("i16", 0, 4), col("pf", 6), A.is_equal)
+    for i in range(4):
+        ts(vw("m4", i, 160, 4), vw("zero", 0, 40), col("pf", 18 + i), A.add)
     quant("q0", "s0", 0, 128, vw("zero", 0, 512))
     for r in range(R):
         dma("Y", lambda r=r: ap(vw("lq%d" % r, L, 128), dt.uint8), lambda: ap(vw("q0", 0, 128 - L), dt.uint8),
@@ -385,18 +407,25 @@ def rank_program(g, core, T, topo):
     quant("qe", "se", 0, 512, vw("et"))
     quant("qv", "sv", 0, 128, vw("vt"))
 
+    gathered, tables = [0], []
+
     def from_points(r):
         top = 3 + r
         e0, e1, b0, b1 = vw("e16", 0, 7), vw("e16", 1, 8), vw("bk", 0, 7), vw("bk", 1, 8)
-        if LCUT:
-            ts(vw("pm"), vw("cls"), col("pf", 8), A.is_equal)
-        else:
-            ts(vw("pm"), vw("cls"), col("pf", 8), A.is_equal, 0.5, A.subtract)
-            scan(vw("xq"), vw("ic2h"), vw("pm"), 0.0, A.max, A.mult)
+        ts(vw("pm"), vw("cls"), col("pf", 8), A.is_equal, 0.5, A.subtract)
+        if r and PMO:
+            ops[-1]["order"].add(gathered[0])
+        scan(vw("Lg"), vw("amp"), vw("pm"), 0.0, A.max, A.mult)
+        lin(vw("xq"), vw("Lg"), col("pf", 23), col("pf", 30))
         sign(vw("junk", 6 * C, 7 * C), vw("cls"), col("pf", 10), 1.0, col("es", 0))
+        if r in ESO:
+            ops[-1]["order"].add(gathered[0] - 1)
         lin(vw("eq"), vw("es"), 0.5, 160.0)
+        lin(col("e0", 0), vw("es"), 0.5, -1.0)
         cp("S", vw("em"), vw("mpar"), col("eq", 0))
         trans(vw("ef"), vw("em"))
+        if r and TRO:
+            ops[-1]["order"].add(gathered[0])
         tt(vw("e16"), vw("ef", 0, 16), vw("ef", 16, 32), A.add)
         ts(vw("bi"), vw("e16", 0, 8), -0.5, A.add, 1.5 * 2 ** 24, A.add)
         tt(vw("su2", 0, 7), e0, e1, A.add)
@@ -440,9 +469,11 @@ def rank_program(g, core, T, topo):
         ts(vw("ogp"), vw("sl"), 1 / U, A.mult)
         tt(vw("ix"), vw("e160"), vw("nj", 20, 40), A.add)
         ts(vw("olam"), vw("ix"), 1 / U, A.mult)
-        cp("S", vw("Gp"), ind(vw("icb"), vw("ogp", 0, 20)))
+        if not GL:
+            cp("S", vw("Gp"), ind(vw("icb"), vw("ogp", 0, 20)))
         cp("S", vw("lp"), ind(vw("icb"), vw("ogp", 20, 40)))
         cp("S", vw("pn"), ind(vw("t16"), vw("onp")))
+        tables[:] = [len(ops) - 3, len(ops) - 2, len(ops) - 1]
 
     def lane(m, a, b, s=1):
         k = [m in x for x in TILES].index(True)
@@ -463,7 +494,7 @@ def rank_program(g, core, T, topo):
             ts(vw("pb", 0, 4 * C, 4), vw("pF", 0, C), 0.0, A.is_gt)
             quant("qp", "sp", 0, C, vw("pb"))
             mm("pG", ("qa", "sa", 128), ("qp", "sp", 0, C))
-            cp("V", vw("cls"), vw("pG", 0, C))
+            cp(CL, vw("cls"), vw("pG", 0, C))
         from_points(r)
         for a in range(0, 4 * C, XP):
             cp("S", vw("Xh", a, a + XP), vw(xs, a, a + XP), 0.5)
@@ -479,7 +510,8 @@ def rank_program(g, core, T, topo):
             j = vw("sj", C * (m % 4), C * (m % 4) + 16 * m)
             sign(j, vw("pB", 0, 16 * m), own(m), -1.0)
             act(lane(m, 0, 16 * m), j, ACT.Relu, col("rs", m))
-        tt(lane(20, 0, C), vw("pA", 0, C), vw("kw"), A.is_le)
+        for a, b in ((h, C), (0, h)) if DS else ((0, C),):
+            tt(lane(20, a, b), vw("pA", a, b), vw("kw", a, b), A.is_le)
         scan(vw("cd", 8, 168), lane(20, 0, C, 2), lane(20, 1, C, 2), 0.0, A.add)
         for m in range(19, ns, -1):
             e = 160 * (m - ns)
@@ -492,29 +524,19 @@ def rank_program(g, core, T, topo):
         for k in range(4):
             quant("qb", "sb", TILE0[k], TILE0[k + 1], vw("bits", 4 * TILE0[k], 4 * TILE0[k + 1]))
             mm("pE", ("qa", "sa", 0), ("qb", "sb", TILE0[k], TILE0[k + 1]), k == 0, k == 3)
-        for a in (160, 0):
-            tt(vw("k2", 2 * a, 2 * a + C, 2), vw("pE", a, a + 160), vw("m16", a, a + 160), A.mult)
-            wrap("k3", "k2", 2 * a + C, 32, 2 * a)
-            cp("V", vw("orank", a // 16, a // 16 + 10), vw("k3", 2 * a + 31, 2 * a + C, 32))
-        if LCUT:
-            scat(vw("Lr"), vw("orank"), vw("pm"))
-            for a, b in zip(LCUT, LCUT[1:]):
-                scat(vw("La"), vw("orank", a, b), vw("icb", 16 * a, 16 * b))
-        else:
-            scat(vw("Lf"), vw("orank"), vw("xq"))
-            ts(vw("Lr"), vw("Lf"), 0.0, A.is_gt)
-            act(vw("Lg"), vw("Lf"), ACT.Abs)
-            lin(vw("La"), vw("Lg"), 1.0, -209.0)
-        scan(vw("kc"), vw("Lr"), vw("zero", 0, C), col("eq", 0), A.add)
-        scan(vw("val", 16, 16 + C), vw("kc"), vw("Lr"), 0.0, A.max, A.mult)
-        trans(vw("tv", C, 2 * C + 32), vw("val"))
-        trans(vw("tv", 0, C), vw("val", 16, 16 + C))
-        scan(vw("tw", C, 2 * C + 32), vw("rmin"), vw("tv", C, 2 * C + 32), 0.0, A.min)
-        scan(vw("tw", 0, C), vw("rmin", 0, C), vw("tv", 0, C), 0.0, A.min)
+        for b, a in zip(KC, KC[1:]):
+            tt(vw("k2", 2 * a, 2 * b, 2), vw("pE", a, b), vw("m16", a, b), A.mult)
+            wrap("k3", "k2", 2 * b, 32, 2 * a)
+            cp("V", vw("orank", a // 16, b // 16), vw("k3", 2 * a + 31, 2 * b, 32))
+        scat(vw("Lf"), vw("orank"), vw("xq"))
+        act(vw("Lg"), vw("Lf"), ACT.Abs, None, col("pf", 27))
+        lin(vw("La"), vw("Lg"), col("pf", 28), col("pf", 29))
+        scan(vw("val", 16, 16 + C), vw("one"), vw("Lf"), col("e0", 0), A.mult)
+        for a, b, s0 in ((C, 2 * C + 32, 0), (0, C, 16)):
+            trans(vw("tv", a, b), vw("val", s0, s0 + b - a))
+            scan(vw("tw", a, b - 8), vw("tv", a + 8, b), vw("tv", a, b - 8), 0.0, A.min, A.max)
         ts(vw("oplr"), ind(vw("tw"), vw("osel")), 160.0, A.add)
         scat(vw("O"), vw("oplr", 0, 20), vw("La"))
-        cp("S", vw("SR"), ind(vw("Gp"), vw("oplr", 0, 20)))
-        cp("S", vw("SC"), ind(vw("SR"), vw("orank")))
         cp("S", vw("CS"), ind(vw("O"), vw("oidx")))
         for k in range(2):
             tt(vw("ke", 160 * k, 160 * k + 160), ind(vw("O"), vw("opt", 10 * k, 10 * k + 10)), vw("m4", 0, 160), A.mult)
@@ -522,29 +544,56 @@ def rank_program(g, core, T, topo):
             ts(vw("oab", 40 * k, 40 * k + 40), vw("kf", 160 * k + 3, 160 * k + 160, 4), 4.0, A.mult, col("pf", 17), A.add)
         for i, (a, b) in enumerate(zip(ZCUT, ZCUT[1:])):
             cp("V" if i < ZV else "S", vw("ah", 16 * a, 16 * b), ind(vw("Xh"), vw("oab", a, b)))
+            if i == ZV:
+                ops[-1]["order"].update(tables[:TB[r]])
             tt(vw("Z", 16 * a, 16 * b), ind(vw("Xh"), vw("oab", 40 + a, 40 + b)), vw("ah", 16 * a, 16 * b), A.add)
         quant("qz", "sz", 0, 160, vw("Z"))
-        if not YCUT:
-            cp("S", vw("Y", 640, 1280), ind(vw(xs), vw("oab", 40, 80)))
-        cp(YA, vw("Y", 0, 640), vw("ah"), 2.0)
+        if YCUT[0]:
+            cp("S", vw("Y", 640, 640 + 16 * YCUT[0]), ind(vw(xs), vw("oab", 40, 40 + YCUT[0])))
+        if ACUT[0]:
+            cp(YA, vw("Y", 0, 16 * ACUT[0]), vw("ah", 0, 16 * ACUT[0]), 2.0)
         for b in range(4):
             mm("p" + "ABCD"[b], ("qw", "sw", 128 * b), ("qz", "sz", 0, 160))
-            cp("VS"[b % 2], vw("H", b, 640, 4), vw("p" + "ABCD"[b], 0, 160), 0.03125)
+            cp(HE[b], vw("H", b, 640, 4), vw("p" + "ABCD"[b], 0, 160), 0.03125)
         quant("qh", "sh", 0, 160, vw("H", 0, 640))
+        if WS == "S":
+            mm("pF", U16R, ("qh", "sh", 0, 160))
         mm("pE", U16R, ("qh", "sh", 0, 160))
-        for a, b in zip(YCUT, YCUT[1:]):
-            tt(vw("Y", 640 + 16 * a, 640 + 16 * b), ind(vw(xs), vw("oab", 40 + a, 40 + b)), vw("H", 16 * a, 16 * b), A.subtract)
-        if not YCUT:
-            cp("S", vw("H", 640, 640 + HS), vw("H", 0, HS), -1.0)
-            cp("V", vw("H", 640 + HS, 1280), vw("H", HS, 640), -1.0)
-        for a in (0,) if YCUT else (0, 640):
-            dma("G", lambda a=a: ap(vw("Y", a, a + 640)), lambda a=a: ap(vw("H", a, a + 640)),
-                [vw("H", a, a + 640), vw("Y", a, a + 640)], [vw("Y", a, a + 640)], True)
+        pieces = [(40 + a, 40 + b) for a, b in zip(YCUT, YCUT[1:])] + list(zip(ACUT, ACUT[1:]))
+
+        def b_piece(n=1):
+            last = len(ops) - 1
+            for a, b in [pieces.pop(0) for _ in range(min(n, len(pieces)))]:
+                k = 40 if a >= 40 else 0
+                tt(vw("Y", 16 * a, 16 * b), ind(vw(xs), vw("oab", a, b)), vw("H", 16 * (a - k), 16 * (b - k)), A.subtract if k else A.add)
+                ops[-1]["order"].add(last)
+        b_piece(YP[0])
+        if YCUT[0]:
+            cp("S", vw("H", 640, 640 + 16 * YCUT[0]), vw("H", 0, 16 * YCUT[0]), -1.0)
+        for a, b in ((0, 16 * ACUT[0]), (640, 640 + 16 * YCUT[0])):
+            if a < b:
+                ya, ha = vw("Y", a, b), vw("H", a, b)
+                dma("G", lambda ya=ya: ap(ya), lambda ha=ha: ap(ha), [ha, ya], [ya], True)
         ts(vw("win", 0, 160), vw("pE", 0, 160), 0.0, A.is_gt)
-        ts(vw("win", 160, C), vw("pE", 0, 160), 0.0, A.is_le)
-        cp("S", vw("tb", 160, C), ind(vw("win"), vw("olam", 10, 20)))
-        cp("V", vw("tb", 0, 160), ind(vw("win"), vw("olam", 0, 10)))
+        if WS == "S":
+            sign(vw("win", 160, C), vw("pF", 0, 160), TINY, -1.0)
+        else:
+            ts(vw("win", 160, C), vw("pE", 0, 160), 0.0, A.is_le)
+        b_piece(YP[1])
+        act(vw("tb", 16 * TV, C), ind(vw("win"), vw("olam", TV, 20)), ACT.Relu)
+        late = len(ops) - 1
+        if GL:
+            cp("S", vw("Gp"), ind(vw("icb"), vw("ogp", 0, 20)))
+            ops[-1]["order"].add(late)
+        cp("S", vw("SR"), ind(vw("Gp"), vw("oplr", 0, 20)))
+        if SL:
+            ops[-1]["order"].add(late)
+        cp("S", vw("SC"), ind(vw("SR"), vw("orank")))
+        if TV:
+            ts(vw("tb", 0, 16 * TV), ind(vw("win"), vw("olam", 0, TV)), 0.0, A.max)
+        b_piece(YP[2])
         scan(vw("tc"), vw("tb"), vw("zero", 0, C), -160.0, A.add)
+        b_piece(YP[3])
         lo, hi = 16 * NVL, 186 + 24 * 5
         for m in range(NVL, 6):
             sign(vw("junk", C * m, C * m + hi - lo), vw("tc", lo, hi), col("lx", m), -1.0, col("acc", m))
@@ -553,22 +602,30 @@ def rank_program(g, core, T, topo):
             ts(vw("cb", k, k + 2 * n2), vw("tc", 16 * m, 186 + 24 * m), col("lw", m), A.is_le)
             scan(vw("co", 160 * (m + 1) - n2, 160 * (m + 1)), vw("cb", k, k + n2), vw("cb", k + n2, k + 2 * n2), 16.0 * m, A.add)
         if NVL:
+            b_piece(YP[4])
             cp("V", vw("osg", 0, NVL), vw("co", 159, 160 * NVL, 160))
+            b_piece(YP[5])
         if NVL < 6:
             ts(vw("osg", NVL, 6), vw("acc", NVL, 6), 0.5, A.mult, (lo + hi) / 2, A.add)
         tt(vw("kh", 0, L), ind(vw("lp"), vw("osg")), vw("m4", 0, L), A.mult)
+        b_piece(YP[6])
         cp("S", vw("ps%d" % r), ind(vw("pn"), vw("osg")))
         wrap("ki", "kh", L, 4)
+        b_piece(9)
         ts(vw("ol4"), vw("ki", 3, L, 4), 4.0, A.mult, col("pf", 17), A.add)
-        cp("S", vw("cmp", 192, 384), ind(vw("Y", 0, 4 * C), vw("ol4", 12, 24)))
-        cp("V", vw("cmp", 0, 192), ind(vw("Y", 0, 4 * C), vw("ol4", 0, 12)))
+        cp("S", vw("cmp", 16 * CV, 384), ind(vw("Y", 0, 4 * C), vw("ol4", CV, 24)))
+        if CV:
+            cp("V", vw("cmp", 0, 16 * CV), ind(vw("Y", 0, 4 * C), vw("ol4", 0, CV)))
+        composed = len(ops)
         quant("qc%d" % r, "sc%d" % r, 0, 128, vw("cmp"))
         send(vw("pa%d" % r), vw("ps%d" % r), "ap%d" % r)
         send(vw("lq%d" % r, 0, L), vw("qc%d" % r, 0, L), "aq%d" % r, dt.uint8)
         send(vw("ls%d" % r, 0, L), vw("sc%d" % r, 0, L), "as%d" % r)
-        cp("S", vw("WP"), ind(vw("win"), vw("ogp", 0, 20)))
+        act(vw("WP"), ind(vw("win"), vw("ogp", 0, 20)), ACT.Relu)
         cp("S", vw("WR"), ind(vw("WP"), vw("oplr", 0, 20)))
         tt(vw("kh", L, 2 * L), ind(vw("CS"), vw("osg")), vw("m16", 0, L), A.mult)
+        if KO:
+            ops[-1]["order"].add(composed - KO)
         wrap("ki", "kh", 2 * L, 16, L)
         ts(vw("olc"), vw("ki", L + 15, 2 * L, 16), 208.0, A.add)
         tt(vw("cls"), ind(vw("WR"), vw("orank")), vw("cls"), A.add)
@@ -587,15 +644,20 @@ def rank_program(g, core, T, topo):
         for b in range(4):
             mm("p" + "ABCD"[b], ("qe", "se", 128 * b), ("lq%d" % r, "ls%d" % r, 0, 128))
             cp("SV"[b % 2], vw("Y", 4 * C + b, 4 * (C + L), 4), vw("p" + "ABCD"[b], 0, L))
-        cp("S", vw("X", 640, 1280), ind(vw("Y"), vw("os4", 40, 80)))
-        cp("V", vw("X", 0, 640), ind(vw("Y"), vw("os4", 0, 40)))
+        if r < R - 1:
+            cp("S", vw("X", 16 * XV, 1280), ind(vw("Y"), vw("os4", XV, 80)))
+            gathered[0] = len(ops)
+            cp("V", vw("X", 0, 16 * XV), ind(vw("Y"), vw("os4", 0, XV)))
 
-    for k, a in enumerate((0, 160)):
-        quant("qx", "sx", a, a + 160, vw("X", 4 * a, 4 * a + 640))
-        mm("p" + "EF"[k], ("qv", "sv", 0), ("qx", "sx", a, a + 160))
-        cp("SV"[k], vw("yo", a, a + 160), vw("p" + "EF"[k], 0, 160))
-        dma("SY"[k], lambda a=a: T.y[:, a:a + 160], lambda a=a: T.yo[:, a:a + 160], [vw("yo", a, a + 160)], [])
-    dma("Y", lambda: T.oc[:], lambda: ap(vw("qx"), dt.uint8), [vw("qx")], [])
+    for e, a, b in (("V", 0, XC[0]), ("S", XC[0], TCUT // 4), ("S", TCUT // 4, XC[1]), ("V", XC[1], 80)):
+        if a < b:
+            cp(e, vw("X", 16 * a, 16 * b), ind(vw("Y"), vw("os4", a, b)))
+    for k, (a, b) in enumerate(((0, TCUT), (TCUT, C))):
+        quant("qx", "sx", a, b, vw("X", 4 * a, 4 * b))
+        mm("p" + "EF"[k], ("qv", "sv", 0), ("qx", "sx", a, b))
+        cp("SV"[k], vw("yo", a, b), vw("p" + "EF"[k], 0, b - a))
+        dma("SY"[k], lambda a=a, b=b: T.y[:, a:b], lambda a=a, b=b: T.yo[:, a:b], [vw("yo", a, b)], [])
+        dma("YS"[k], lambda a=a, b=b: T.oc[:, 4 * a:4 * b], lambda a=a, b=b: ap(vw("qx", a, b), dt.uint8), [vw("qx", a, b)], [])
     for k in range(4):
         dma("Y", lambda k=k: T.osc[4 * k:4 * k + 4, :], lambda k=k: T.sx[32 * k:32 * k + 4, :], [vw("sx")], [])
 

import numpy as np
from concourse.mybir import dt, AluOpType, ActivationFunctionType

C, L, R = 320, 96, 3
F32, BF, F16, I32, U16, Q4, U8 = "float32", "bfloat16", "float16", "int32", "uint16", "float8_e4m3fn_x4", "uint8"
BIG = 1e29
FL = "SSS"
FILL = 1.0
TRO, ESO = True, (1, 2)
U = 2.0 ** -14
TILES = ((20, 19, 18, 17), (16, 15, 14, 13), (12, 11, 10, 9), (8, 7, 6, 5), (4, 3, 2, 1))
TILE0 = (0, 320, 576, 768, 896, 1024)
NS = (12, 12, 12)
NVL = 4
ZCUT = (0, 8, 24, 40)
WS, DS = "S", False
XL, TB = 800, (0, 0, 0)
GL, SL, KO, PBG = False, True, 0, False
LIFT = 16384.0
YP = (1, 1, 1, 1, 1, 1, 0)
ACUT = (40,)
KC = (320, 112, 0)
TV, CV, HE, XV = 10, 12, "VSVS", 40
TCUT, XC = 192, (24, 68)
NL = 5
SCA, GAT, FIX, LEAST, SFIX = 2.5, 1.2, 0.0, 53.0, 60.0
CL, PSO, PMO = "S", True, True
D = 2.0 ** -17
TINY = 1e-35
HS = 320
YCUT = (0, 8, 14, 20, 26, 34, 40)
XP = 320
YA = "S"
ZV = 1
KW = 2
WAKE, LOCAL, REMOTE, SLACK = 220.0, 2200.0, 1600.0, 60.0
SCHED = True


def _sb(n, d):
    return ("sbuf", [128, n], d)


SCRATCH = {
    "x0": _sb(4 * C, BF), "X": _sb(4 * C, BF), "Xh": _sb(4 * C, BF), "Y": _sb(4 * (C + L), BF),
    "ut": _sb(512, BF), "vt": _sb(512, BF),
    "qu": _sb(128, Q4), "su": _sb(128, U8), "qur": _sb(128, Q4), "sur": _sb(128, U8), "qv": _sb(128, Q4), "sv": _sb(128, U8),
    "qw": _sb(512, Q4), "sw": _sb(512, U8), "qx": _sb(C, Q4), "sx": _sb(C, U8),
    "qz": _sb(160, Q4), "sz": _sb(160, U8), "qh": _sb(160, Q4), "sh": _sb(160, U8),
    "zero": _sb(640, BF), "et": _sb(2048, BF), "qe": _sb(512, Q4), "se": _sb(512, U8),
    "ai": _sb(512, BF), "at": _sb(1024, BF), "qa": _sb(256, Q4), "sa": _sb(256, U8), "q0": _sb(128, Q4), "s0": _sb(128, U8),
    "bits": _sb(4096, BF), "qb": _sb(1024, Q4), "sb": _sb(1024, U8), "pb": _sb(4 * C, BF), "qp": _sb(C, Q4), "sp": _sb(C, U8),
    "ah": _sb(640, BF), "Z": _sb(640, BF), "H": _sb(4 * C, BF), "cmp": _sb(512, BF),
    "icb": _sb(C + L, BF), "i16": _sb(C, BF), "t16": _sb(16, BF), "sg0": _sb(60, F32),
    "m16": _sb(C, BF), "m4": _sb(C, BF), "r16": _sb(C, BF), "r4": _sb(C, BF), "r8": _sb(C, BF), "r32": _sb(2 * C, BF),
    "bigm": _sb(C, BF), "rbig": _sb(C, BF),
    "pi": _sb(8, I32), "pf": _sb(32, F32), "ui": _sb(8, I32), "uo": _sb(8, U16), "amp": _sb(C, F32),
    "km": _sb(C, F32), "kw": _sb(C, F32), "sj": _sb(8 * 15 * 16, BF), "k2": _sb(2 * C, F16), "k3": _sb(2 * C, F16),
    "kd": _sb(C, BF), "ke": _sb(C, F16), "kf": _sb(C, F16), "kg": _sb(C, F16),
    "kh": _sb(2 * L, F16), "ki": _sb(2 * L, F16),
    "cb": _sb(6 * C, BF), "co": _sb(12 * 160, F16), "cd": _sb(4 * 296, F16), "ce": _sb(192, F16), "junk": _sb(7 * C, BF),
    "cls": _sb(C, BF), "pm": _sb(C, BF), "xq": _sb(C, F32), "Lf": _sb(C, F32), "Lg": _sb(C, F32), "La": _sb(C, BF), "O": _sb(C, BF),
    "val": _sb(C + 32, BF), "tv": _sb(2 * C + 32, BF), "tw": _sb(2 * C + 32, BF),
    "tab": _sb(13 * C, BF),
    "f1": _sb(160, BF), "g1": _sb(160, F32), "o1": _sb(160, F32), "f2": _sb(C, BF), "g2": _sb(C, BF), "o2": _sb(C, BF),
    "f3": _sb(160, BF), "g3": _sb(160, BF), "o3": _sb(160, BF),
    "yo": _sb(C, F32), "po": _sb(C, F32),
}
for _r in range(R):
    SCRATCH["qc%d" % _r] = _sb(128, Q4)
    SCRATCH["sc%d" % _r] = _sb(128, U8)
    SCRATCH["lq%d" % _r] = _sb(128, Q4)
    SCRATCH["ls%d" % _r] = _sb(128, U8)
    SCRATCH["pa%d" % _r] = _sb(L, BF)
    SCRATCH["ps%d" % _r] = _sb(L, BF)
for _b in "ABCDEFG":
    SCRATCH["p" + _b] = ("psum", [128, 512], F32)
SMALL = {}
_at = 0
for _n, _w in (("bk", 8), ("vn", 8), ("mpar", 32), ("em", 32), ("ef", 32), ("acc", 6), ("es", 1), ("eq", 1), ("e0", 2), ("e16", 16), ("bi", 8),
               ("mu", 8), ("su2", 8), ("Pb", 40), ("sig", 20), ("s2", 20), ("cz", 20), ("c1", 20), ("jh", 20), ("jc", 20), ("base", 20),
               ("tn", 20), ("zz", 20), ("pr", 20), ("e160", 20), ("ix", 20), ("rs", 20), ("lw", 6), ("lx", 6),
               ("nj", 40), ("yy", 40), ("ib", 40), ("sl", 40), ("a1", 20), ("a2", 20), ("a4", 20), ("a5", 20), ("os0", 2), ("a6", 4), ("bas0", 4)):
    SMALL[_n] = ("sm", _at, _w)
    _at += _w
SCRATCH["sm"] = _sb(_at, F32)
_at = 0
for _n, _w in (("orank", 20), ("oplr", 32), ("osel", 2), ("opt", 20), ("oab", 80), ("oidx", 20), ("olam", 20), ("onp", 20),
               ("ogp", 40), ("osg", 6), ("ol4", 24), ("olc", 6), ("os4", 80), ("oc1", 10), ("oc2", 20), ("oc3", 10)):
    SMALL[_n] = ("so", _at, _w)
    _at += _w
SCRATCH["so"] = _sb(_at, U16)
for _at, _n in enumerate(("Gp", "SR", "SC", "WP", "WR", "lp", "pn", "tb", "tc", "win", "cu", "one", "CS")):
    SMALL[_n] = ("tab", C * _at, C)

NDMA = 28
SEMAPHORES = ["cV", "cS", "cT", "cG", "sent"] + ["d%d" % i for i in range(NDMA)] + \
    ["a%s%d" % (k, r) for k in "qsp" for r in range(R)]

A = AluOpType
ACT = ActivationFunctionType


def vw(name, a=0, b=None, s=1):
    if name in SMALL:
        n, o, w = SMALL[name]
        return (n, o + a, o + (w if b is None else b), s)
    return (name, a, SCRATCH[name][1][1] if b is None else b, s)


def col(name, j):
    return vw(name, j, j + 1)


def ind(win, off):
    return ("*", win, off)


def size(v):
    return 16 * size(v[2]) if v[0] == "*" else len(range(v[1], v[2], v[3]))


def span(out, *ins, both=False):
    vs = [v for v in (out,) + ins if isinstance(v, tuple)]
    if out[0] == "*":
        return 50 + SCA * size(out)
    if any(v[0] == "*" for v in vs):
        return 55 + GAT * size(out)
    kinds = [SCRATCH[v[0]] for v in vs if size(v) > 1 or v is out]
    if both:
        return FIX + max(LEAST, size(out) * (0.83 if any(k[0] == "psum" for k in kinds) else 1.66))
    return FIX + max(LEAST, size(out) * (0.42 if all(k[2] in (BF, F16, U16) for k in kinds) else 0.83))


def issue_order(ops):
    n = len(ops)
    after = [[] for _ in ops]
    for i, o in enumerate(ops):
        for j in o["deps"] | o["order"]:
            after[j].append(i)
    gap = lambda j, i: 0.0 if j not in ops[i]["deps"] or ops[i]["eng"] is None else WAKE
    chain = [0.0] * n
    for i in range(n - 1, -1, -1):
        chain[i] = ops[i]["cost"] + ops[i]["lat"] + max([gap(i, k) + chain[k] for k in after[i]], default=0.0)
    left = [len(o["deps"] | o["order"]) for o in ops]
    ready, done, free, pool, out = [0.0] * n, [0.0] * n, {}, {}, []

    def place(i, t):
        out.append((t, len(out), i))
        done[i] = t + ops[i]["cost"] + ops[i]["lat"]
        for k in after[i]:
            ready[k] = max(ready[k], done[i] + gap(i, k) if i in ops[k]["deps"] or ops[k]["eng"] is None else t)
            left[k] -= 1
            if not left[k]:
                offer(k)

    def offer(k):
        if ops[k]["eng"] is None:
            place(k, ready[k])
        else:
            pool.setdefault(ops[k]["eng"], []).append(k)
    for i in range(n):
        if not left[i]:
            offer(i)
    while any(pool.values()):
        best = None
        for e, c in pool.items():
            if not c:
                continue
            c.sort(key=lambda k: -chain[k])
            pick, limit = c[0], max(free.get(e, 0.0), ready[c[0]])
            for k in c[1:]:
                t = max(free.get(e, 0.0), ready[k])
                if t + ops[k]["cost"] * (FILL if ops[k]["loose"] else 1.0) <= limit + SLACK and t < limit:
                    pick, limit = k, t
            if best is None or limit < best[0]:
                best = (limit, e, pick)
        t, e, k = best
        pool[e].remove(k)
        free[e] = t + ops[k]["cost"]
        place(k, t)
    return [ops[i] for _, _, i in sorted(out)]


def rank_program(g, core, T, topo):
    rank = T.rank_of(core)
    if rank is None:
        return
    cores = list(T.cores)
    nxt, prv = cores[(rank + 1) % len(cores)], cores[(rank - 1) % len(cores)]
    Q = {"V": g.vector, "S": g.scalar, "T": g.tensor, "G": g, "Y": g.sync}
    ops = []
    ndma = [0]

    def ap(v, cast=None):
        if v[0] == "*":
            return ap(v[1], cast).indirect(ap(v[2]))
        a = T[v[0]][:, v[1]:v[2]:v[3]] if v[3] != 1 else T[v[0]][:, v[1]:v[2]]
        return a.bitcast(cast) if cast is not None else a

    def sc(v):
        return ap(v) if isinstance(v, tuple) else v

    def parts(vs):
        out = []
        for v in vs:
            if isinstance(v, tuple):
                out += [v[1], v[2]] if v[0] == "*" else [v]
        return out

    def add(eng, fn, reads, writes, cost, sem=None, val=0, acc=False, lat=0.0, order=()):
        ops.append({"eng": eng, "fn": fn, "r": parts(reads), "w": parts(writes), "sem": sem, "val": val, "acc": acc,
                    "cost": cost, "lat": lat, "order": set(order),
                    "loose": any(isinstance(v, tuple) and v[0] == "*" for v in reads)})

    def scat(out, off, in_):
        add("V", lambda q: q.tensor_copy(ap(ind(out, off)), ap(in_)), [off, in_], [out], span(ind(out, off)))

    def act(out, in_, func, accum=None, bias=0.0, scale=1.0):
        cost = span(out, in_) if in_[0] == "*" else SFIX + 0.83 * size(out)
        kw = {} if func == ACT.Copy else {"bias": sc(bias)}
        if isinstance(scale, tuple) or scale != 1.0:
            kw["scale"] = sc(scale)
        if accum is not None:
            kw["accum_out"] = ap(accum)
        add("S", lambda q: q.activation(ap(out), ap(in_), func, **kw), [in_, bias, scale], [out, accum], cost)

    def cp(e, out, in_, scale=None):
        if e == "S":
            act(out, in_, ACT.Copy, None, 0.0, 1.0 if scale is None else scale)
        elif scale is None:
            add(e, lambda q: q.tensor_copy(ap(out), ap(in_)), [in_], [out], span(out, in_))
        else:
            ts(out, in_, scale, A.mult)

    def sign(out, in_, bias, scale, accum=None):
        act(out, in_, ACT.Sign, accum, bias, scale)

    def ts(out, in0, s1, o0, s2=None, o1=None):
        if o1 is None:
            add("V", lambda q: q.tensor_scalar(ap(out), ap(in0), sc(s1), None, o0), [in0, s1], [out], span(out, in0))
        else:
            add("V", lambda q: q.tensor_scalar(ap(out), ap(in0), sc(s1), sc(s2), o0, o1), [in0, s1, s2], [out], span(out, in0))

    def tt(out, in0, in1, o):
        add("V", lambda q: q.tensor_tensor(ap(out), ap(in0), ap(in1), o), [in0, in1], [out], span(out, in0, in1, both=True))

    def scan(out, d0, d1, init, o0, o1=A.add):
        add("V", lambda q: q.tensor_tensor_scan(ap(out), ap(d0), ap(d1), sc(init), o0, o1), [d0, d1, init], [out], span(out, d0, d1))

    def fill(out, c):
        add("V", lambda q: q.memset(ap(out), c), [], [out], span(out))

    def trans(out, in_):
        add("V", lambda q: q.transpose(ap(out), ap(in_)), [in_], [out], span(out, in_))

    def quant(qn, sn, a, b, in_):
        add("V", lambda q: q.quantize_mx(ap(vw(qn, a, b)), ap(vw(sn, a, b)), ap(in_)), [in_], [vw(qn, a, b), vw(sn, a, b)],
            12 + 0.22 * size(in_))

    def mm(bank, w, x, start=True, stop=True):
        lq, ls, rq, rs = vw(w[0], w[2], w[2] + 128), vw(w[1], w[2], w[2] + 128), vw(x[0], x[2], x[3]), vw(x[1], x[2], x[3])
        out = vw(bank, 0, x[3] - x[2])
        add("T", lambda q: q.matmul_mx(ap(out), ap(lq), ap(ls), ap(rq), ap(rs), start, stop), [lq, ls, rq, rs], [out],
            0.6 * (size(rq) + 16), acc=not start)

    def iota(out, pat, base, cm):
        if SCRATCH[out[0]][2] == I32:
            add("G", lambda q: q.iota(ap(out), pat, base, cm), [], [out], 130 + 1.66 * size(out))
        else:
            add("G", lambda q: q.iota(ap(out), pat, base, cm, allow_small_or_imprecise_dtypes=True), [], [out], 130 + 1.66 * size(out))

    def where(out, pat, op, base, cm):
        z = vw("zero", 0, out[2] - out[1])
        add("G", lambda q: q.affine_select(ap(out), ap(z), pat, op, 1.0, base, cm), [z], [out], 170 + 1.66 * size(out))

    def dma(e, fo, fi, reads, writes, adding=False, lat=LOCAL):
        s = "d%d" % ndma[0]
        ndma[0] += 1
        if adding:
            add(e, lambda q: q.dma_start(fo(), fi(), accum_op=A.add), reads, writes, 600, sem=s, val=16, lat=lat)
        else:
            add(e, lambda q: q.dma_start(fo(), fi()), reads, writes, 60, sem=s, val=16, lat=lat)

    rid, pid, _ = topo.addr(nxt)
    nout, nin = len(topo.engines(core, nxt)), len(topo.engines(prv, core))
    nsent = [0]
    sent_at = {}

    def send(dst, src, sem, cast=None):
        nsent[0] += nout
        sent_at[sem] = len(ops)
        add("G", lambda q: q.remote_dma(ap(dst, cast), ap(src, cast), T.sem[sem], T.sem.sent, pid, rid, topo.mask(core, nxt)),
            [src], [], 400, sem="-", lat=REMOTE, order=[sent_at["ap" + sem[2]]] if PSO and sem[1] != "p" else [])

    def arrive(dst, sem):
        add(None, None, [], [dst], 0.0, sem=sem, val=nin, order=[sent_at[sem]])

    def wrap(out, masked, b, seg, a=0):
        scan(vw(out, a, b), vw("r%d" % seg, a, b), vw(masked, a, b), 0.0, A.mult)

    dma("S", lambda: T.ut[:], lambda: T.u[:], [], [vw("ut")])
    dma("Y", lambda: T.x0[:], lambda: T.x[:], [], [vw("x0")], lat=LOCAL + XL)
    dma("Y", lambda: ap(vw("qw"), dt.uint8), lambda: T.wc[:], [vw("x0")], [vw("qw")])
    dma("Y", lambda: T.sw[:], lambda: T.ws[:], [vw("x0")], [vw("sw")])
    dma("G", lambda: T.vt[:], lambda: T.v[:], [], [vw("vt")])
    fill(vw("zero"), 0.0)
    iota(col("pi", 0), [[0, 1]], 0, 1)
    first = len(ops) - 1
    iota(vw("i16"), [[0, 20], [1, 16]], 0, 0)
    iota(vw("ui"), [[16, 8]], 0, 0)
    iota(vw("ai"), [[1, 8], [0, 64]], 0, 0)
    iota(vw("sg0", 0, 20), [[16, 20]], 0, 0)
    iota(vw("sg0", 20, 52), [[1, 2], [0, 16]], 0, 0)
    iota(vw("sg0", 52, 60), [[1024, 8]], C, 0)
    if PBG:
        iota(vw("pb"), [[0, 4 * C]], 0, 0)
    iota(vw("icb"), [[1, C + L]], -208, 0)
    where(vw("r8"), [[0, 40], [1, 8]], A.is_equal, 0, 0)
    where(vw("r32"), [[0, 20], [1, 32]], A.is_equal, 0, 0)
    iota(vw("Lf"), [[0, C]], 0, 0)
    iota(vw("t16"), [[1, 16]], 0, 0)
    iota(vw("O"), [[0, C]], 0, 0)
    where(vw("r4"), [[0, 80], [1, 4]], A.is_equal, 0, 0)
    iota(vw("cmp", 4 * L, 512), [[0, 512 - 4 * L]], 0, 0)
    for b in range(4):
        where(vw("et", 512 * b, 512 * b + 512), [[1, 512]], A.not_equal, -b, -4)
    for i in range(first + 1, len(ops)):
        ops[i]["order"].add(i - 1)
    for k in range(4):
        a, b = 4 * (TILE0[k] + 16 * min(TILES[k])), 4 * TILE0[k + 1]
        cp("S", vw("bits", a, b), vw("zero", 0, b - a))
    if not PBG:
        fill(vw("pb"), 0.0)
    for j, m in ((1, 15), (2, 3), (3, 7), (5, 1)):
        ts(col("pi", j), col("pi", 0), m, A.bitwise_and)
    ts(col("pi", 4), col("pi", 0), 4, A.arith_shift_right)
    ts(col("pi", 6), col("pi", 0), 15, A.bitwise_and, 2, A.arith_shift_right)
    ts(col("pi", 7), col("pi", 0), 4, A.arith_shift_right, 1, A.bitwise_and)
    cp("V", vw("uo"), vw("ui"))
    lin = lambda out, in_, scale, bias: act(out, in_, ACT.Identity, None, bias, scale)
    sig = vw("sig")
    sign(vw("r16"), vw("i16"), 0.0, 1.0)
    cp("V", vw("pf", 0, 8), vw("pi"))
    ts(col("pf", 11), col("pf", 1), 2.0, A.subtract)
    ts(col("pf", 10), col("pf", 3), -1.0, A.mult, 0.5, A.add)
    tt(col("pf", 12), col("pf", 11), col("pf", 11), A.mult)
    ts(vw("m16"), vw("i16"), col("pf", 1), A.is_equal)
    ts(col("pf", 8), col("pf", 3), -1.0, A.add)
    ts(col("pf", 17), col("pf", 2), 4.0 * 208, A.add)
    ts(col("pf", 13), col("pf", 12), 1.5, A.is_gt, 20.0, A.mult)
    ts(col("pf", 15), col("pf", 5), col("pf", 7), A.not_equal, 21.0, A.mult)
    ts(col("pf", 16), col("pf", 1), -1.0, A.mult, 15.0, A.add)
    tt(col("pf", 14), col("pf", 13), col("pf", 4), A.add)
    lin(vw("bigm"), vw("m16"), BIG, -BIG)
    lin(vw("rbig"), vw("r16"), 2 * BIG, -BIG)
    ts(col("pf", 22), col("pf", 1), 7.5, A.is_lt)
    for j, lo, hi in ((23, 2.0, -2.0), (25, D, 1.0), (26, 0.5 + 48 * D, 1232.0), (27, -0.5, 0.0),
                      (28, 1 / D, 1.0), (29, -0.5 / D - 48, -1232.0), (30, 0.5, 0.0)):
        ts(col("pf", j), col("pf", 22), lo - hi, A.mult, hi, A.add)
    ts(vw("one"), vw("zero", 0, C), col("pf", 22), A.add)
    lin(vw("amp"), vw("icb", 0, C), col("pf", 25), col("pf", 26))
    for a in (0, C + 16):
        cp("V", vw("val", a, a + 16), vw("zero", 0, 16))
    for a in (C - 8, 2 * C + 24):
        cp("V", vw("tw", a, a + 8), vw("zero", 0, 8))
    cp("V", vw("cd", 0, 8), vw("zero", 0, 8))
    cp("V", vw("k2", 1, 2 * C, 2), vw("zero", 0, C))
    quant("qu", "su", 0, 128, vw("ut"))
    add("V", lambda q: q.tensor_copy(ap(vw("qur"), dt.uint32), ap(ind(vw("qu"), vw("uo")), dt.uint32)), [vw("qu"), vw("uo")], [vw("qur")], 210)
    cp("S", vw("sur"), ind(vw("su"), vw("uo")))
    lin(sig, vw("sg0", 0, 20), 1.0, col("pf", 1))
    ts(vw("k2", 1, 2 * C, 32), vw("sg0", 0, 20), col("pf", 16), A.add)
    cp("S", vw("cu"), vw("zero", 0, C))
    cp("V", col("ce", 31), vw("zero", 0, 1))
    lin(vw("s2"), sig, -1.0, 639.5)
    lin(vw("c1"), sig, -U, 319.25 * U)
    lin(vw("cz"), sig, -0.5 * U, 319.5 * U)
    lin(vw("Pb", 0, 20), sig, U, 0.25 * U)
    for a in (0, 10):
        cp("S", vw("jh", a, a + 10), vw("Pb", 0, 10))
    lin(vw("lw"), vw("sig", 0, 6), 1.0, -160.0)
    lin(vw("lx"), vw("sig", 0, 6), 1.0, -159.5)
    lin(vw("f2"), vw("r8"), -2.0, 1.0)
    lin(vw("f3"), vw("r8", 0, 160), -2.0, 1.0)
    lin(vw("f3", 1, 160, 8), vw("zero", 0, 20), 1.0, 1.0)
    lin(vw("f1"), vw("r8", 0, 160), 0.0, -1.0)
    ts(vw("oc2"), vw("zero", 0, 20), col("pf", 3), A.add)
    ts(vw("oc3", 0, 5), vw("zero", 0, 5), col("pf", 3), A.add)
    ts(vw("oc3", 5, 10), vw("zero", 0, 5), col("pf", 3), A.add, -1.0, A.add)
    ts(vw("oc1"), vw("zero", 0, 10), col("pf", 10), A.add, 6.5, A.add)
    ts(vw("at", 512, 1024), vw("ai"), col("pf", 14), A.is_equal)
    quant("qa", "sa", 128, 256, vw("at", 512, 1024))
    ts(vw("at", 0, 512), vw("ai"), col("pf", 4), A.is_equal)
    quant("qa", "sa", 0, 128, vw("at", 0, 512))
    ts(vw("mpar"), vw("sg0", 20, 52), col("pf", 7), A.is_equal)
    ts(vw("os0"), vw("sig", 0, 2), col("pf", 15), A.add, 41.0, A.min)
    ts(vw("osel"), vw("os0"), 16.0, A.mult, 7.0, A.add)
    ts(vw("pf", 18, 22), vw("i16", 0, 4), col("pf", 6), A.is_equal)
    for i in range(4):
        ts(vw("m4", i, 160, 4), vw("zero", 0, 40), col("pf", 18 + i), A.add)
    quant("q0", "s0", 0, 128, vw("zero", 0, 512))
    for r in range(R):
        dma("Y", lambda r=r: ap(vw("lq%d" % r, L, 128), dt.uint8), lambda: ap(vw("q0", 0, 128 - L), dt.uint8),
            [vw("q0")], [vw("lq%d" % r, L, 128)])
        dma("Y", lambda r=r: ap(vw("ls%d" % r, L, 128)), lambda: ap(vw("s0", 0, 128 - L)), [vw("s0")], [vw("ls%d" % r, L, 128)])
    quant("qe", "se", 0, 512, vw("et"))
    quant("qv", "sv", 0, 128, vw("vt"))

    gathered, tables = [0], []

    def from_points(r):
        top = 3 + r
        e0, e1, b0, b1 = vw("e16", 0, 7), vw("e16", 1, 8), vw("bk", 0, 7), vw("bk", 1, 8)
        ts(vw("pm"), vw("cls"), col("pf", 8), A.is_equal, 0.5, A.subtract)
        if r and PMO:
            ops[-1]["order"].add(gathered[0])
        scan(vw("Lg"), vw("amp"), vw("pm"), 0.0, A.max, A.mult)
        lin(vw("xq"), vw("Lg"), col("pf", 23), col("pf", 30))
        sign(vw("junk", 6 * C, 7 * C), vw("cls"), col("pf", 10), 1.0, col("es", 0))
        if r in ESO:
            ops[-1]["order"].add(gathered[0] - 1)
        lin(vw("eq"), vw("es"), 0.5, 160.0)
        lin(col("e0", 0), vw("es"), 0.5, -1.0)
        cp("S", vw("em"), vw("mpar"), col("eq", 0))
        trans(vw("ef"), vw("em"))
        if r and TRO:
            ops[-1]["order"].add(gathered[0])
        tt(vw("e16"), vw("ef", 0, 16), vw("ef", 16, 32), A.add)
        ts(vw("bi"), vw("e16", 0, 8), -0.5, A.add, 1.5 * 2 ** 24, A.add)
        tt(vw("su2", 0, 7), e0, e1, A.add)
        tt(vw("vn"), vw("sg0", 52, 60), vw("e16", 0, 8), A.subtract)
        ts(vw("bk"), vw("bi"), 1.5 * 2 ** 24, A.subtract, 0.5 * U, A.mult)
        tt(vw("mu", 0, 7), b0, b1, A.add)

        def below(e, out, x, limit):
            if e == "S":
                sign(out, x, limit, -1.0)
            else:
                ts(out, x, limit, A.is_lt, 0.5, A.subtract)
        for k in range(top + 1):
            if k:
                below(FL[2], vw("f3", k + 1, 160, 8), vw("jh"), col("bk", k))
        cp("S", vw("g3"), ind(vw("bk"), vw("oc3")), -1.0)
        scan(vw("o3"), vw("f3"), vw("g3"), 0.0, A.max, A.min)
        tt(vw("a4"), vw("jh"), vw("o3", 7, 160, 8), A.subtract)
        ts(vw("opt"), vw("a4"), 1 / U, A.mult)
        for n in range(1, top + 1):
            below(FL[0], vw("f1", 8 - n, 160, 8), vw("s2"), col("su2", n - 1))
        cp("S", vw("g1"), ind(vw("vn"), vw("oc1")), U)
        scan(vw("o1"), vw("f1"), vw("g1"), 0.0, A.min, A.max)
        ts(vw("tn"), vw("o1", 7, 160, 8), 1.5 * 2 ** 33 * U, A.add, 1.5 * 2 ** 33 * U, A.subtract)
        tt(vw("a5"), vw("o1", 7, 160, 8), vw("c1"), A.add)
        tt(vw("Pb", 20, 40), vw("a5"), vw("tn"), A.subtract)
        ts(vw("onp"), vw("tn"), 1 / (1024 * U), A.mult)
        ts(vw("oidx"), vw("Pb", 20, 40), 1 / U, A.mult)
        for k in range(top + 1):
            below(FL[1], vw("f2", k + 1, C, 8), vw("Pb"), col("mu", k))
        cp("S", vw("g2"), ind(vw("bk"), vw("oc2")), -1.0)
        scan(vw("o2"), vw("f2"), vw("g2"), 0.0, A.max, A.min)
        y = vw("o2", 7, C, 8)
        tt(vw("zz"), vw("Pb", 20, 40), vw("cz"), A.subtract)
        tt(vw("nj"), vw("Pb"), y, A.add)
        tt(vw("yy"), vw("nj"), y, A.add)
        ts(vw("ib"), vw("yy"), 0.0, A.is_lt, 160 * U, A.mult)
        tt(vw("pr"), vw("zz"), vw("yy", 20, 40), A.mult)
        tt(vw("sl"), vw("ib"), vw("nj"), A.add)
        ts(vw("e160"), vw("pr"), 0.0, A.is_lt, 160 * U, A.mult)
        ts(vw("ogp"), vw("sl"), 1 / U, A.mult)
        tt(vw("ix"), vw("e160"), vw("nj", 20, 40), A.add)
        ts(vw("olam"), vw("ix"), 1 / U, A.mult)
        if not GL:
            cp("S", vw("Gp"), ind(vw("icb"), vw("ogp", 0, 20)))
        cp("S", vw("lp"), ind(vw("icb"), vw("ogp", 20, 40)))
        cp("S", vw("pn"), ind(vw("t16"), vw("onp")))
        tables[:] = [len(ops) - 3, len(ops) - 2, len(ops) - 1]

    def lane(m, a, b, s=1):
        k = [m in x for x in TILES].index(True)
        o = 4 * TILE0[k] + TILES[k].index(m)
        return vw("bits", o + 4 * a, o + 4 * (b - 1) + 1, 4 * s)

    own = lambda m: col("kw", 16 * m + 15)
    U16R = ("qur", "sur", 0)
    QX = ("qx", "sx", 0, C)
    for r in range(R):
        xs = "x0" if r == 0 else "X"
        ns = NS[r]
        quant("qx", "sx", 0, C, vw(xs))
        mm("pA", U16R, QX)
        mm("pB", U16R, QX)
        if r == 0:
            mm("pF", ("qu", "su", 0), QX)
            ts(vw("pb", 0, 4 * C, 4), vw("pF", 0, C), 0.0, A.is_gt)
            quant("qp", "sp", 0, C, vw("pb"))
            mm("pG", ("qa", "sa", 128), ("qp", "sp", 0, C))
            cp(CL, vw("cls"), vw("pG", 0, C))
        from_points(r)
        for a in range(0, 4 * C, XP):
            cp("S", vw("Xh", a, a + XP), vw(xs, a, a + XP), 0.5)
        h = 16 * (ns - KW)
        for a, b in ((h, C), (0, h)):
            tt(vw("km", a, b), vw("pA", a, b), vw("bigm", a, b), A.add)
            scan(vw("kw", a, b), vw("rbig", a, b), vw("km", a, b), 0.0, A.min, A.max)
        for m in range(4):
            ts(vw("cu", 80 * m, 64 * m + 64), vw("pA", 16 * m + 16, 80), own(m), A.is_gt)
        scan(vw("ce", 32, 160), vw("cu", 0, 256, 2), vw("cu", 1, 256, 2), 0.0, A.add)
        tt(vw("k2", 7, 128, 32), vw("ce", 63, 160, 32), vw("ce", 31, 128, 32), A.subtract)
        for m in range(ns, 0, -1):
            j = vw("sj", C * (m % 4), C * (m % 4) + 16 * m)
            sign(j, vw("pB", 0, 16 * m), own(m), -1.0)
            act(lane(m, 0, 16 * m), j, ACT.Relu, col("rs", m))
        for a, b in ((h, C), (0, h)) if DS else ((0, C),):
            tt(lane(20, a, b), vw("pA", a, b), vw("kw", a, b), A.is_le)
        scan(vw("cd", 8, 168), lane(20, 0, C, 2), lane(20, 1, C, 2), 0.0, A.add)
        for m in range(19, ns, -1):
            e = 160 * (m - ns)
            ts(lane(m, 0, 16 * m), vw("pA", 0, 16 * m), own(m), A.is_lt)
            scan(vw("co", e - 8 * m, e), lane(m, 0, 8 * m), lane(m, 8 * m, 16 * m), 0.0, A.add)
        ts(vw("k2", 32 * (ns + 1) + 5, 2 * C, 32), vw("co", 159, 160 * (19 - ns), 160), -1.0, A.mult)
        for a, b in ((5, ns + 1), (1, 5)):
            ts(vw("k2", 32 * a + 5, 32 * b, 32), vw("rs", a, b), -1.0, A.mult)
        tt(vw("k2", 3, 2 * C, 32), vw("cd", 7, 160, 8), vw("cd", 15, 168, 8), A.subtract)
        for k in range(4):
            quant("qb", "sb", TILE0[k], TILE0[k + 1], vw("bits", 4 * TILE0[k], 4 * TILE0[k + 1]))
            mm("pE", ("qa", "sa", 0), ("qb", "sb", TILE0[k], TILE0[k + 1]), k == 0, k == 3)
        for b, a in zip(KC, KC[1:]):
            tt(vw("k2", 2 * a, 2 * b, 2), vw("pE", a, b), vw("m16", a, b), A.mult)
            wrap("k3", "k2", 2 * b, 32, 2 * a)
            cp("V", vw("orank", a // 16, b // 16), vw("k3", 2 * a + 31, 2 * b, 32))
        scat(vw("Lf"), vw("orank"), vw("xq"))
        act(vw("Lg"), vw("Lf"), ACT.Abs, None, col("pf", 27))
        lin(vw("La"), vw("Lg"), col("pf", 28), col("pf", 29))
        scan(vw("val", 16, 16 + C), vw("one"), vw("Lf"), col("e0", 0), A.mult)
        for a, b, s0 in ((C, 2 * C + 32, 0), (0, C, 16)):
            trans(vw("tv", a, b), vw("val", s0, s0 + b - a))
            scan(vw("tw", a, b - 8), vw("tv", a + 8, b), vw("tv", a, b - 8), 0.0, A.min, A.max)
        ts(vw("oplr"), ind(vw("tw"), vw("osel")), 160.0, A.add)
        scat(vw("O"), vw("oplr", 0, 20), vw("La"))
        cp("S", vw("CS"), ind(vw("O"), vw("oidx")))
        for k in range(2):
            tt(vw("ke", 160 * k, 160 * k + 160), ind(vw("O"), vw("opt", 10 * k, 10 * k + 10)), vw("m4", 0, 160), A.mult)
            wrap("kf", "ke", 160 * k + 160, 4, 160 * k)
            ts(vw("oab", 40 * k, 40 * k + 40), vw("kf", 160 * k + 3, 160 * k + 160, 4), 4.0, A.mult, col("pf", 17), A.add)
        for i, (a, b) in enumerate(zip(ZCUT, ZCUT[1:])):
            cp("V" if i < ZV else "S", vw("ah", 16 * a, 16 * b), ind(vw("Xh"), vw("oab", a, b)))
            if i == ZV:
                ops[-1]["order"].update(tables[:TB[r]])
            tt(vw("Z", 16 * a, 16 * b), ind(vw("Xh"), vw("oab", 40 + a, 40 + b)), vw("ah", 16 * a, 16 * b), A.add)
        quant("qz", "sz", 0, 160, vw("Z"))
        if YCUT[0]:
            cp("S", vw("Y", 640, 640 + 16 * YCUT[0]), ind(vw(xs), vw("oab", 40, 40 + YCUT[0])))
        if ACUT[0]:
            cp(YA, vw("Y", 0, 16 * ACUT[0]), vw("ah", 0, 16 * ACUT[0]), 2.0)
        for b in range(4):
            mm("p" + "ABCD"[b], ("qw", "sw", 128 * b), ("qz", "sz", 0, 160))
            cp(HE[b], vw("H", b, 640, 4), vw("p" + "ABCD"[b], 0, 160), 0.03125)
        quant("qh", "sh", 0, 160, vw("H", 0, 640))
        if WS == "S":
            mm("pF", U16R, ("qh", "sh", 0, 160))
        mm("pE", U16R, ("qh", "sh", 0, 160))
        pieces = [(40 + a, 40 + b) for a, b in zip(YCUT, YCUT[1:])] + list(zip(ACUT, ACUT[1:]))

        def b_piece(n=1):
            last = len(ops) - 1
            for a, b in [pieces.pop(0) for _ in range(min(n, len(pieces)))]:
                k = 40 if a >= 40 else 0
                tt(vw("Y", 16 * a, 16 * b), ind(vw(xs), vw("oab", a, b)), vw("H", 16 * (a - k), 16 * (b - k)), A.subtract if k else A.add)
                ops[-1]["order"].add(last)
        b_piece(YP[0])
        if YCUT[0]:
            cp("S", vw("H", 640, 640 + 16 * YCUT[0]), vw("H", 0, 16 * YCUT[0]), -1.0)
        for a, b in ((0, 16 * ACUT[0]), (640, 640 + 16 * YCUT[0])):
            if a < b:
                ya, ha = vw("Y", a, b), vw("H", a, b)
                dma("G", lambda ya=ya: ap(ya), lambda ha=ha: ap(ha), [ha, ya], [ya], True)
        ts(vw("win", 0, 160), vw("pE", 0, 160), 0.0, A.is_gt)
        if WS == "S":
            sign(vw("win", 160, C), vw("pF", 0, 160), TINY, -1.0)
        else:
            ts(vw("win", 160, C), vw("pE", 0, 160), 0.0, A.is_le)
        b_piece(YP[1])
        act(vw("tb", 16 * TV, C), ind(vw("win"), vw("olam", TV, 20)), ACT.Relu)
        late = len(ops) - 1
        if GL:
            cp("S", vw("Gp"), ind(vw("icb"), vw("ogp", 0, 20)))
            ops[-1]["order"].add(late)
        cp("S", vw("SR"), ind(vw("Gp"), vw("oplr", 0, 20)))
        if SL:
            ops[-1]["order"].add(late)
        cp("S", vw("SC"), ind(vw("SR"), vw("orank")))
        if TV:
            ts(vw("tb", 0, 16 * TV), ind(vw("win"), vw("olam", 0, TV)), 0.0, A.max)
        b_piece(YP[2])
        scan(vw("tc"), vw("tb"), vw("zero", 0, C), -160.0, A.add)
        b_piece(YP[3])
        lo, hi = 16 * NVL, 186 + 24 * 5
        for m in range(NVL, 6):
            sign(vw("junk", C * m, C * m + hi - lo), vw("tc", lo, hi), col("lx", m), -1.0, col("acc", m))
        for m in range(NVL):
            k, n2 = C * m, 93 + 4 * m
            ts(vw("cb", k, k + 2 * n2), vw("tc", 16 * m, 186 + 24 * m), col("lw", m), A.is_le)
            scan(vw("co", 160 * (m + 1) - n2, 160 * (m + 1)), vw("cb", k, k + n2), vw("cb", k + n2, k + 2 * n2), 16.0 * m, A.add)
        if NVL:
            b_piece(YP[4])
            cp("V", vw("osg", 0, NVL), vw("co", 159, 160 * NVL, 160))
            b_piece(YP[5])
        if NVL < 6:
            ts(vw("osg", NVL, 6), vw("acc", NVL, 6), 0.5, A.mult, (lo + hi) / 2, A.add)
        tt(vw("kh", 0, L), ind(vw("lp"), vw("osg")), vw("m4", 0, L), A.mult)
        b_piece(YP[6])
        cp("S", vw("ps%d" % r), ind(vw("pn"), vw("osg")))
        wrap("ki", "kh", L, 4)
        b_piece(9)
        ts(vw("ol4"), vw("ki", 3, L, 4), 4.0, A.mult, col("pf", 17), A.add)
        cp("S", vw("cmp", 16 * CV, 384), ind(vw("Y", 0, 4 * C), vw("ol4", CV, 24)))
        if CV:
            cp("V", vw("cmp", 0, 16 * CV), ind(vw("Y", 0, 4 * C), vw("ol4", 0, CV)))
        composed = len(ops)
        quant("qc%d" % r, "sc%d" % r, 0, 128, vw("cmp"))
        send(vw("pa%d" % r), vw("ps%d" % r), "ap%d" % r)
        send(vw("lq%d" % r, 0, L), vw("qc%d" % r, 0, L), "aq%d" % r, dt.uint8)
        send(vw("ls%d" % r, 0, L), vw("sc%d" % r, 0, L), "as%d" % r)
        act(vw("WP"), ind(vw("win"), vw("ogp", 0, 20)), ACT.Relu)
        cp("S", vw("WR"), ind(vw("WP"), vw("oplr", 0, 20)))
        tt(vw("kh", L, 2 * L), ind(vw("CS"), vw("osg")), vw("m16", 0, L), A.mult)
        if KO:
            ops[-1]["order"].add(composed - KO)
        wrap("ki", "kh", 2 * L, 16, L)
        ts(vw("olc"), vw("ki", L + 15, 2 * L, 16), 208.0, A.add)
        tt(vw("cls"), ind(vw("WR"), vw("orank")), vw("cls"), A.add)
        scat(vw("SC"), vw("olc"), vw("icb", C, C + L))
        for i in range(4):
            cp("S", vw("kd", i, C, 4), vw("SC", i, C, 4), col("pf", 18 + i))
        wrap("kg", "kd", C, 4)
        ts(vw("os4"), vw("kg", 3, C, 4), 4.0, A.mult, col("pf", 17), A.add)
        arrive(vw("pa%d" % r), "ap%d" % r)
        scat(vw("cls"), vw("olc"), vw("pa%d" % r))
        arrive(vw("lq%d" % r, 0, L), "aq%d" % r)
        arrive(vw("ls%d" % r, 0, L), "as%d" % r)
        if r == R - 1:
            cp("V", vw("po"), vw("cls"))
            dma("Y", lambda: T.pts[:], lambda: T.po[0:128:16, :], [vw("po")], [])
        for b in range(4):
            mm("p" + "ABCD"[b], ("qe", "se", 128 * b), ("lq%d" % r, "ls%d" % r, 0, 128))
            cp("SV"[b % 2], vw("Y", 4 * C + b, 4 * (C + L), 4), vw("p" + "ABCD"[b], 0, L))
        if r < R - 1:
            cp("S", vw("X", 16 * XV, 1280), ind(vw("Y"), vw("os4", XV, 80)))
            gathered[0] = len(ops)
            cp("V", vw("X", 0, 16 * XV), ind(vw("Y"), vw("os4", 0, XV)))

    for e, a, b in (("V", 0, XC[0]), ("S", XC[0], TCUT // 4), ("S", TCUT // 4, XC[1]), ("V", XC[1], 80)):
        if a < b:
            cp(e, vw("X", 16 * a, 16 * b), ind(vw("Y"), vw("os4", a, b)))
    for k, (a, b) in enumerate(((0, TCUT), (TCUT, C))):
        quant("qx", "sx", a, b, vw("X", 4 * a, 4 * b))
        mm("p" + "EF"[k], ("qv", "sv", 0), ("qx", "sx", a, b))
        cp("SV"[k], vw("yo", a, b), vw("p" + "EF"[k], 0, b - a))
        dma("SY"[k], lambda a=a, b=b: T.y[:, a:b], lambda a=a, b=b: T.yo[:, a:b], [vw("yo", a, b)], [])
        dma("YS"[k], lambda a=a, b=b: T.oc[:, 4 * a:4 * b], lambda a=a, b=b: ap(vw("qx", a, b), dt.uint8), [vw("qx", a, b)], [])
    for k in range(4):
        dma("Y", lambda k=k: T.osc[4 * k:4 * k + 4, :], lambda k=k: T.sx[32 * k:32 * k + 4, :], [vw("sx")], [])

    hist = {}
    for i, o in enumerate(ops):
        deps = set()
        for v, wr in [(v, False) for v in o["r"]] + [(v, True) for v in o["w"]]:
            psum = SCRATCH[v[0]][0] == "psum"
            m = np.zeros(SCRATCH[v[0]][1][1], bool)
            m[v[1]:v[2]:v[3]] = True
            if psum:
                m[:] = True
            h = hist.setdefault(v[0], [])
            for j, mj, wj in h:
                if j == i or not (m & mj).any():
                    continue
                same = ops[j]["eng"] == o["eng"]
                if same and o["acc"]:
                    o["order"].add(j)
                elif wr or wj or (psum and not same):
                    deps.add(j)
            if wr and not o["acc"]:
                h[:] = [e for e in h if (e[1] & ~m).any()]
            h.append((i, m, wr))
        o["deps"] = deps
    for o in ops:
        o["from"] = [ops[j] for j in o["deps"]]
        o["inc"] = False
    for o in ops:
        for d in o["from"]:
            d["inc"] = d["sem"] is None
    if SCHED:
        ops = issue_order(ops)
    n = {"V": 0, "S": 0, "T": 0, "G": 0}
    for i, o in enumerate(ops):
        o["at"] = i
        if o["inc"]:
            n[o["eng"]] += 1
            o["sem"], o["val"] = "c" + o["eng"], n[o["eng"]]
    known = {e: {} for e in Q}
    for o in ops:
        if o["eng"] is None:
            o["know"] = {}
            continue
        k = known[o["eng"]]
        for d in sorted(o["from"], key=lambda d: -d["at"]):
            if k.get(d["sem"], 0) < d["val"]:
                Q[o["eng"]].wait_ge(T.sem[d["sem"]], d["val"])
                k[d["sem"]] = d["val"]
                for s, x in d["know"].items():
                    k[s] = max(k.get(s, 0), x)
        o["know"] = dict(k)
        inst = o["fn"](Q[o["eng"]])
        if o["inc"]:
            inst.then_inc(T.sem[o["sem"]], 1)
        elif o["val"] == 16:
            inst.then_inc(T.sem[o["sem"]], 16)
    for e in n:
        if n[e]:
            g.wait_ge(T.sem["c" + e], n[e])
    for i in range(ndma[0]):
        g.wait_ge(T.sem["d%d" % i], 16)
    g.wait_ge(T.sem.sent, nsent[0])
